import numpy as np
import ml_dtypes


def mxq(x, axis, fmt="e4m3"):
    dtype, down = {"e4m3": (ml_dtypes.float8_e4m3fn, 7), "e5m2": (ml_dtypes.float8_e5m2, 14)}[fmt]
    v = np.moveaxis(np.asarray(x, np.float32).astype(ml_dtypes.bfloat16).astype(np.float64), axis, -1)
    blocks = v.reshape(v.shape[:-1] + (-1, 32))
    amax = np.abs(blocks).max(-1, keepdims=True)
    byte = np.maximum(np.where(amax > 0, np.frexp(amax)[1] - 1 + 127, 0) - down, 1)
    scale = np.exp2(byte - 127.0)
    codes = (blocks / scale).astype(np.float32).astype(dtype).astype(np.float64)
    return np.moveaxis((codes * scale).reshape(v.shape), -1, axis)


WIDE = False


def mx_kscale(k):
    if not WIDE:
        return np.ones(k)
    levels = np.array([10, -10, 5, -5, 0])
    if k % 512:
        return np.exp2(np.random.permutation(np.resize(levels, k // 32))).repeat(32)
    a = np.empty((k // 512, 16))
    for p in range(k // 512):
        a[p, :8] = np.random.permutation(np.resize(levels, 8))
        for g in range(8):
            far = levels[np.abs(levels - a[p, g]) >= 10]
            a[p, g + 8] = far[np.random.randint(len(far))]
    return np.exp2(a.ravel()).repeat(32)


def f64(x):
    return np.asarray(x).astype(np.float64)


def striped(idx):
    return np.tile(np.asarray(idx).reshape(-1, 16).T, (8, 1)).astype(np.uint16)


def unstriped(offs):
    return offs[:16].T.reshape(-1).astype(np.int64)


B, N, T, D, DV, NQ = 1, 1024, 2048, 512, 128, 512


def setup_inputs():
    n = np.random.standard_normal
    idx = np.sort(np.random.permutation(T)[:B * N].reshape(B, N), axis=1).reshape(-1)
    s = mx_kscale(D)[:, None]
    u = np.ones(T)
    u[idx] = mx_kscale(B * N)
    r = np.random.uniform(0.5, 2.0, T)
    qidx = np.random.permutation(T)[:B * NQ]
    rk = np.random.uniform(0.5, 2.0, T)
    k = n((D, T)) / s / rk
    v = n((DV, T)) / (u * r)
    return {
        "xq": (n((D, T)) * s * (0.80 / np.sqrt(D))).astype(np.float32),
        "kT": k.astype(np.float32),
        "vT": v.astype(np.float32),
        "ks": np.tile(rk, (128, 1)).astype(np.float32),
        "vs": np.tile(u * r, (128, 1)).astype(np.float32),
        "offs": striped(idx),
        "qoffs": striped(qidx),
    }


def reference(xq, kT, vT, ks, vs, offs, qoffs):
    idx = unstriped(offs)
    k = f64(kT)
    v = f64(vT)
    pick = lambda x: x[:, idx].reshape(x.shape[0], B, N).transpose(1, 0, 2)
    q = f64(xq)[:, unstriped(qoffs)].reshape(D, B, NQ).transpose(1, 0, 2)
    score = mxq(q, 1, "e4m3").transpose(0, 2, 1) @ mxq(pick(k), 1, "e4m3")
    score = score * pick(f64(ks))[:, :1, :]
    m = score.max(-1, keepdims=True)
    p = np.exp(score - m)
    total = p.sum(-1, keepdims=True)
    w = p * pick(f64(vs))[:, :1, :]
    y = mxq(w, 2, "e4m3") @ mxq(pick(v).transpose(0, 2, 1), 1, "e4m3")
    y = y / total
    out = np.zeros((DV, T))
    out[:, unstriped(qoffs)] = y.transpose(2, 0, 1).reshape(-1, B * NQ)
    return out

@@ -1,0 +1,382 @@
+from contextlib import ExitStack
+
+import concourse.mybir as mybir
+from concourse.masks import make_identity
+
+P = 128
+D, T, N, NQ, DV = 512, 2048, 1024, 512, 128
+FLOPS = 2 * NQ * N * (D + DV)
+
+F32 = mybir.dt.float32
+BF16 = mybir.dt.bfloat16
+U32 = mybir.dt.uint32
+U16 = mybir.dt.uint16
+U8 = mybir.dt.uint8
+FP8X4 = mybir.dt.float8_e4m3fn_x4
+COPY = mybir.ActivationFunctionType.Copy
+EXP = mybir.ActivationFunctionType.Exp
+MULT = mybir.AluOpType.mult
+ADD = mybir.AluOpType.add
+MIN = mybir.AluOpType.min
+X = mybir.AxisListType.X
+H = T // 2
+
+
+def tile_attend_x_router_ks_kernel(tc, xq, kT, vT, ks, vs, offs, qoffs, out):
+    nc = tc.nc
+    with ExitStack() as ctx:
+        lists = ctx.enter_context(tc.tile_pool(name="lists", bufs=1))
+        keep = ctx.enter_context(tc.tile_pool(name="keep", bufs=1))
+        banks = ctx.enter_context(tc.psum_pool(name="banks", bufs=1))
+
+        slots = lists.tile([P, N // 16], U16, name="slots")
+        qlist = lists.tile([P, NQ // 16], U16, name="qlist")
+        ksw = keep.tile([P, T], F32, name="ksw")
+        vsw = keep.tile([P, T], F32, name="vsw")
+        warm = keep.tile([P, 1], F32, name="warm")
+        nc.vector.memset(warm[:], 0.0)
+        nc.vector.memset(ksw[:], 0.0)
+        nc.vector.memset(vsw[:], 0.0)
+        nc.scalar.activation(warm[:], warm[:], EXP)
+        ident = keep.tile([P, P], F32, name="ident")
+        make_identity(nc, ident[:])
+        ident_bf16 = keep.tile([P, P], BF16, name="ident_bf16")
+        make_identity(nc, ident_bf16[:])
+
+        kview = kT.rearrange("(p t) w -> p t w", t=4)
+        qview = xq.rearrange("(p t) w -> p t w", t=4)
+        raw = {}
+        for key in ("k0", "k1", "q0"):
+            raw_tile = keep.tile([P, 2, T], F32, name="raw_" + key)
+            raw[key] = raw_tile
+
+        def load_pair(key, view, e, lo, hi):
+            nc.sync.dma_start(raw[key][:, :, lo:hi], view[:, 2 * e : 2 * e + 2, lo:hi])
+
+        load_pair("k0", kview, 0, 0, 512)
+        nc.sync.dma_start(slots[:], offs)
+        nc.sync.dma_start(qlist[:], qoffs)
+        load_pair("k0", kview, 0, 512, 1280)
+        nc.sync.dma_start(ksw[0:1, :], ks[0:1, :])
+        load_pair("k0", kview, 0, 1280, 2048)
+        load_pair("k1", kview, 1, 0, H)
+        nc.sync.dma_start(vsw[0:1, :], vs[0:1, :])
+        load_pair("k1", kview, 1, H, T)
+        for lo, hi in ((0, H), (H, T)):
+            load_pair("q0", qview, 0, lo, hi)
+        qpl = {}
+        for t in (2, 3):
+            q_t = keep.tile([P, T], F32, name="qplane%d" % t)
+            nc.sync.dma_start(q_t[:], qview[:, t, :])
+            qpl[t] = q_t
+        vraw = keep.tile([P, T], F32, name="vraw", tag="vraw")
+        nc.sync.dma_start(vraw[:], vT)
+
+        window = keep.tile([P, T], F32, name="window")
+        for i in range(8):
+            nc.gpsimd.memset(window[:, i * 256 : (i + 1) * 256], 0.0)
+
+        ksg = keep.tile([P, N], F32, name="ksg")
+        nc.vector.tensor_copy(ksg[:], ksw[:].indirect(slots[:]))
+        vsg = keep.tile([P, N], F32, name="vsg")
+        nc.vector.tensor_copy(vsg[:], vsw[:].indirect(slots[:]))
+
+        nks_col = keep.tile([P, 8], F32, name="nks_col")
+        vs_col = keep.tile([P, 8], F32, name="vs_col")
+        for g in range(2):
+            b = banks.tile([P, 4, P], F32, name="ksb%d" % g, tag="b%d" % g, bufs=1)
+            for i in range(4):
+                nc.tensor.transpose(b[:, i, :], ksg[:, (4 * g + i) * P : (4 * g + i + 1) * P], ident[:])
+            nc.vector.tensor_scalar(nks_col[:, 4 * g : 4 * g + 4], b[:, :, 0], -1.0, None, MULT)
+        for g in range(2):
+            b = banks.tile([P, 4, P], F32, name="vsb%d" % g, tag="b%d" % (2 + g), bufs=1)
+            for t in range(4):
+                nc.tensor.transpose(b[:, t, :], vsg[:, g * 512 + t : (g + 1) * 512 : 4], ident[:])
+            nc.vector.tensor_copy(vs_col[:, 4 * g : 4 * g + 4], b[:, :, 0])
+
+        kx = keep.tile([P, 4 * N], BF16, name="kx", align_bytes=64)
+        qx = keep.tile([P, 4 * NQ], BF16, name="qx", align_bytes=64)
+        pair = {}
+
+        def cast(key, lo, hi, engine):
+            if lo == hi:
+                return
+            dst = pair[key][:].rearrange("p (w e) -> p w e", e=2)[:, lo:hi, :]
+            src = raw[key][:, :, lo:hi].rearrange("p e w -> p w e")
+            if engine == "s":
+                nc.scalar.activation(dst, src, COPY)
+            else:
+                nc.vector.tensor_copy(dst, src)
+
+        def gather_pair(key, wide, e, offsets):
+            dst = wide[:].bitcast(U32).rearrange("p (n u) -> p n u", u=2)[:, :, e]
+            nc.vector.tensor_copy(dst, pair[key][:].bitcast(U32).indirect(offsets))
+
+        for key in ("k0", "k1", "q0"):
+            pair_tile = keep.tile([P, 2 * T], BF16, name="pair_" + key, align_bytes=64)
+            pair[key] = pair_tile
+        cast("k0", 0, 512, "s")
+        cast("k0", 512, 1280, "s")
+        cast("k0", 1280, 1536, "s")
+        cast("k0", 1536, 2048, "v")
+        gather_pair("k0", kx, 0, slots[:])
+        cast("k1", 0, H, "s")
+        cast("k1", H, 1536, "s")
+        cast("k1", 1536, T, "v")
+        gather_pair("k1", kx, 1, slots[:])
+        kc = keep.tile([P, N], U32, name="kc", align_bytes=64)
+        ksc = keep.tile([P, N], U8, name="ksc", align_bytes=64)
+        nc.vector.quantize_mx(out=kc[:].bitcast(FP8X4), scales=ksc[:], in_=kx[:])
+        cast("q0", 0, H, "s")
+        cast("q0", H, T, "s")
+        gather_pair("q0", qx, 0, qlist[:])
+
+        nks_row = keep.tile([P, 2, 4, P], F32, name="nks_row")
+        for g in range(2):
+            b = banks.tile([P, 4 * P], F32, name="ksr%d" % g, tag="b%d" % (4 + g), bufs=1)
+            for i in range(4):
+                c = 4 * g + i
+                nc.tensor.transpose(b[:, i * P : (i + 1) * P], nks_col[:, c : c + 1].to_broadcast([P, P]), ident[:])
+            nc.scalar.copy(nks_row[:, g, :, :], b[:].rearrange("p (s t) -> p t s", t=4))
+
+        qc = keep.tile([P, NQ], U32, name="qc", align_bytes=64)
+        qsc = keep.tile([P, NQ], U8, name="qsc", align_bytes=64)
+
+        def gather_q(t, lo, hi):
+            dst = qx[:].rearrange("p (n f) -> p n f", f=4)[:, lo:hi, t]
+            nc.vector.tensor_copy(dst, qpl[t][:].indirect(qlist[:, lo // 16 : hi // 16]))
+
+        gather_q(2, 0, 512)
+        for h in range(2):
+            gather_q(3, h * 224, (h + 1) * 256)
+            nc.vector.quantize_mx(
+                out=qc[:, h * 256 : (h + 1) * 256].bitcast(FP8X4),
+                scales=qsc[:, h * 256 : (h + 1) * 256],
+                in_=qx[:, h * 1024 : (h + 1) * 1024],
+            )
+
+        nm = keep.tile([P, 4], F32, name="nm")
+        total = keep.tile([P, 4], F32, name="total")
+        y_sb = keep.tile([P, NQ], F32, name="y_sb")
+        rl_sb = keep.tile([P, NQ], F32, name="rl_sb")
+        rl = keep.tile([P, 4], F32, name="rl")
+        R = (0, 1)
+        by_slot = {}
+        SB, TB, PB, VB, YB, RB = ({0: (0, 1), 1: (2, 3), 2: (4, 5, 6, 7)}, {2: (0, 1), 3: (2, 3)}, {0: (4, 5), 1: (7, 4), 2: (5, 0), 3: (1, 2)}, 6, (6, 7), (3, 3))
+        found = {}
+        state = {}
+        ybanks = []
+
+        def scores(j):
+            q_cols = slice(j * P, (j + 1) * P)
+            res = []
+            for g in range(2):
+                b = banks.tile([P, 512], F32, name="sc%d_%d" % (j, g), tag="b%d" % SB[j][g], bufs=1)
+                k_cols = slice(g * 512, (g + 1) * 512)
+                nc.tensor.matmul_mx(
+                    out=b[:],
+                    lhsT=qc[:, q_cols].bitcast(FP8X4),
+                    lhsT_scale=qsc[:, q_cols],
+                    rhs=kc[:, k_cols].bitcast(FP8X4),
+                    rhs_scale=ksc[:, k_cols],
+                    start=True,
+                    stop=True,
+                )
+                res.append(b)
+            found[j] = res
+
+        def scores_by_slot(js):
+            width = len(js) * P
+            q_cols = slice(js[0] * P, (js[-1] + 1) * P)
+            per = 512 // width
+            at = keep.tile([P, 8, width], F32, name="at%d" % js[0], tag="vraw")
+            for n in range(8 // per):
+                b = banks.tile([P, 512], F32, name="ss%d_%d" % (js[0], n), tag="b%d" % SB[js[0]][n], bufs=1)
+                for i in range(per):
+                    k_cols = slice((per * n + i) * P, (per * n + i + 1) * P)
+                    nc.tensor.matmul_mx(
+                        out=b[:, i * width : (i + 1) * width],
+                        lhsT=kc[:, k_cols].bitcast(FP8X4),
+                        lhsT_scale=ksc[:, k_cols],
+                        rhs=qc[:, q_cols].bitcast(FP8X4),
+                        rhs_scale=qsc[:, q_cols],
+                        start=True,
+                        stop=True,
+                    )
+                for i in range(per):
+                    c = per * n + i
+                    nc.scalar.activation(
+                        at[:, c, :], b[:, i * width : (i + 1) * width], COPY, scale=nks_col[:, c : c + 1]
+                    )
+            for i, j in enumerate(js):
+                by_slot[j] = (at, i)
+
+        def scale_rows(j):
+            if j not in R:
+                at, col = by_slot[j]
+                res = []
+                for g in range(2):
+                    b = banks.tile([P, 512], F32, name="ts%d_%d" % (j, g), tag="b%d" % TB[j][g], bufs=1)
+                    for i in range(4):
+                        nc.tensor.transpose(
+                            b[:, i * P : (i + 1) * P], at[:, 4 * g + i, col * P : (col + 1) * P], ident[:]
+                        )
+                    res.append(b)
+                found[j] = res
+            else:
+                a = keep.tile([P, 2, 4, P], F32, name="a%d" % j)
+                for g in range(2):
+                    nc.vector.tensor_tensor(
+                        a[:, g, :, :], found[j][g][:].rearrange("p (s t) -> p t s", t=4), nks_row[:, g, :, :], MULT
+                    )
+                found[j] = a
+            p = keep.tile([P, 2, 4, P], F32, name="p%d" % j)
+            wx = keep.tile([P, 2, 4 * P], BF16, name="wx%d" % j, align_bytes=64)
+            wc = keep.tile([P, 2 * P], U32, name="wc%d" % j, align_bytes=64)
+            wsc = keep.tile([P, 2 * P], U8, name="wsc%d" % j, align_bytes=64)
+            state[j] = (p, wx, wc, wsc)
+
+        def stabiliser(j):
+            if j not in R:
+                half = keep.tile([P, 2], F32, name="half%d" % j)
+                for g in range(2):
+                    nc.vector.tensor_reduce(half[:, g : g + 1], found[j][g][:], X, MIN)
+                nc.vector.tensor_tensor(nm[:, j : j + 1], half[:, 0:1], half[:, 1:2], MIN)
+            else:
+                nc.vector.tensor_reduce(nm[:, j : j + 1], found[j][:].rearrange("p g t s -> p (g t s)"), X, MIN)
+
+        def weights(j):
+            p = state[j][0]
+            if j in R:
+                nc.scalar.activation(
+                    p[:].rearrange("p g t s -> p (g t s)"),
+                    found[j][:].rearrange("p g t s -> p (g t s)"),
+                    EXP,
+                    bias=nm[:, j : j + 1],
+                    scale=-1.0,
+                    accum_out=total[:, j : j + 1],
+                )
+                return
+            parts = keep.tile([P, 2], F32, name="parts%d" % j)
+            for g in range(2):
+                src = found[j][g][:].rearrange("p (s t) -> p t s", t=4) if j not in R else found[j][:, g, :, :]
+                nc.scalar.activation(
+                    p[:, g, :, :], src, EXP, bias=nm[:, j : j + 1], scale=-1.0, accum_out=parts[:, g : g + 1]
+                )
+            nc.gpsimd.tensor_tensor(total[:, j : j + 1], parts[:, 0:1], parts[:, 1:2], ADD)
+
+        def turn_and_scale(j):
+            p, wx, wc, wsc = state[j]
+            for g in range(2):
+                b = banks.tile([P, 4, P], F32, name="pt%d_%d" % (j, g), tag="b%d" % PB[j][g], bufs=1)
+                for t in range(4):
+                    nc.tensor.transpose(b[:, t, :], p[:, g, t, :], ident[:])
+                nc.vector.tensor_tensor(
+                    wx[:, g, :].rearrange("p (q t) -> p q t", t=4),
+                    b[:].rearrange("p t q -> p q t"),
+                    vs_col[:, 4 * g : 4 * g + 4].unsqueeze(1).to_broadcast([P, P, 4]),
+                    MULT,
+                )
+
+        def quantise_weights(j):
+            p, wx, wc, wsc = state[j]
+            cuts = 2 if j == 3 else 1
+            gs = 2 // cuts
+            for i in range(cuts):
+                cols = slice(i * gs * P, (i + 1) * gs * P)
+                nc.vector.quantize_mx(
+                    out=wc[:, cols].bitcast(FP8X4),
+                    scales=wsc[:, cols],
+                    in_=wx[:, i * gs : (i + 1) * gs, :].rearrange("p g n -> p (g n)"),
+                )
+
+        def values(j):
+            p, wx, wc, wsc = state[j]
+            if j % 2 == 0:
+                y_bank = banks.tile([P, 2 * P], F32, name="y%d" % j, tag="b%d" % YB[j // 2], bufs=1)
+                ybanks.append(y_bank)
+            for g in range(2):
+                cols = slice(g * P, (g + 1) * P)
+                nc.tensor.matmul_mx(
+                    out=ybanks[j // 2][:, j % 2 * P : (j % 2 + 1) * P],
+                    lhsT=vc[:, cols].bitcast(FP8X4),
+                    lhsT_scale=vsc[:, cols],
+                    rhs=wc[:, cols].bitcast(FP8X4),
+                    rhs_scale=wsc[:, cols],
+                    start=(g == 0),
+                    stop=(g == 1),
+                )
+
+        def normaliser(h):
+            js = slice(2 * h, 2 * h + 2)
+            nc.vector.reciprocal(rl[:, js], total[:, js])
+            b = banks.tile([P, 256], F32, name="rlb%d" % h, tag="b%d" % RB[h], bufs=1)
+            for i in range(2):
+                c = 2 * h + i
+                nc.tensor.transpose(b[:, i * P : (i + 1) * P], rl[:, c : c + 1].to_broadcast([P, P]), ident[:])
+            nc.scalar.copy(rl_sb[:, h * 256 : (h + 1) * 256], b[:])
+
+        def scatter(h):
+            cols = slice(h * 256, (h + 1) * 256)
+            nc.scalar.copy(y_sb[:, cols], ybanks[h][:])
+            nc.vector.tensor_tensor(
+                window[:].indirect(qlist[:, h * 16 : (h + 1) * 16]), y_sb[:, cols], rl_sb[:, cols], MULT
+            )
+
+        vb = keep.tile([P, T], BF16, name="vb")
+        vg = keep.tile([P, N, 2], BF16, name="vg")
+        vx = keep.tile([P, 2, DV, 4], BF16, name="vx", align_bytes=64)
+        vc = keep.tile([P, 2 * DV], U32, name="vc", align_bytes=64)
+        vsc = keep.tile([P, 2 * DV], U8, name="vsc", align_bytes=64)
+
+        def load_values():
+            for i in range(2):
+                cols = slice(i * H, (i + 1) * H)
+                nc.scalar.activation(vb[:, cols], vraw[:, cols], COPY)
+
+        def gather_values():
+            for g in range(2):
+                nc.scalar.activation(
+                    vg[:, g * 512 : (g + 1) * 512, 0], vb[:].indirect(slots[:, g * 32 : (g + 1) * 32]), COPY
+                )
+            b = banks.tile([P, 2, 4, DV], BF16, name="vt", tag="b%d" % VB, bufs=1)
+            for g in range(2):
+                for t in range(4):
+                    nc.tensor.transpose(b[:, g, t, :], vg[:, g * 512 + t : (g + 1) * 512 : 4, 0], ident_bf16[:])
+            nc.scalar.copy(vx[:], b[:].rearrange("p g t e -> p g e t"))
+
+        scores(0)
+        scores(1)
+        load_values()
+        scores_by_slot((2, 3,))
+        scale_rows(0)
+        stabiliser(0)
+        weights(0)
+        scale_rows(1)
+        stabiliser(1)
+        weights(1)
+        gather_values()
+        scale_rows(2)
+        stabiliser(2)
+        weights(2)
+        scale_rows(3)
+        stabiliser(3)
+        weights(3)
+        turn_and_scale(0)
+        quantise_weights(0)
+        nc.vector.quantize_mx(out=vc[:].bitcast(FP8X4), scales=vsc[:], in_=vx[:].rearrange("p g e t -> p (g e t)"))
+        values(0)
+        turn_and_scale(1)
+        quantise_weights(1)
+        values(1)
+        turn_and_scale(2)
+        quantise_weights(2)
+        values(2)
+        normaliser(0)
+        turn_and_scale(3)
+        normaliser(1)
+        scatter(0)
+        quantise_weights(3)
+        values(3)
+        scatter(1)
+        nc.sync.dma_start(out, window[:])

@@ -20,6 +20,7 @@ ADD = mybir.AluOpType.add
 MIN = mybir.AluOpType.min
 X = mybir.AxisListType.X
 H = T // 2
+BANK = 512
 
 
 def tile_attend_x_router_ks_kernel(tc, xq, kT, vT, ks, vs, offs, qoffs, out):
@@ -28,27 +29,32 @@ def tile_attend_x_router_ks_kernel(tc, xq, kT, vT, ks, vs, offs, qoffs, out):
         lists = ctx.enter_context(tc.tile_pool(name="lists", bufs=1))
         keep = ctx.enter_context(tc.tile_pool(name="keep", bufs=1))
         banks = ctx.enter_context(tc.psum_pool(name="banks", bufs=1))
+        ps = banks.tile([P, 8 * BANK], F32, name="ps")
+
+        def bank(b, n=1):
+            return ps[:, b * BANK : (b + n) * BANK]
 
         slots = lists.tile([P, N // 16], U16, name="slots")
         qlist = lists.tile([P, NQ // 16], U16, name="qlist")
         ksw = keep.tile([P, T], F32, name="ksw")
         vsw = keep.tile([P, T], F32, name="vsw")
+        window = keep.tile([P, T], F32, name="window")
         warm = keep.tile([P, 1], F32, name="warm")
         nc.vector.memset(warm[:], 0.0)
         nc.vector.memset(ksw[:], 0.0)
         nc.vector.memset(vsw[:], 0.0)
+        nc.vector.memset(window[:], 0.0)
         nc.scalar.activation(warm[:], warm[:], EXP)
         ident = keep.tile([P, P], F32, name="ident")
         make_identity(nc, ident[:])
-        ident_bf16 = keep.tile([P, P], BF16, name="ident_bf16")
-        make_identity(nc, ident_bf16[:])
 
         kview = kT.rearrange("(p t) w -> p t w", t=4)
         qview = xq.rearrange("(p t) w -> p t w", t=4)
         raw = {}
-        for key in ("k0", "k1", "q0"):
-            raw_tile = keep.tile([P, 2, T], F32, name="raw_" + key)
-            raw[key] = raw_tile
+        pair = {}
+        for key in ("k0", "k1"):
+            raw[key] = keep.tile([P, 2, T], F32, name="raw_" + key)
+            pair[key] = keep.tile([P, 2 * T], BF16, name="pair_" + key, align_bytes=64)
 
         def load_pair(key, view, e, lo, hi):
             nc.sync.dma_start(raw[key][:, :, lo:hi], view[:, 2 * e : 2 * e + 2, lo:hi])
@@ -62,19 +68,12 @@ def tile_attend_x_router_ks_kernel(tc, xq, kT, vT, ks, vs, offs, qoffs, out):
         load_pair("k1", kview, 1, 0, H)
         nc.sync.dma_start(vsw[0:1, :], vs[0:1, :])
         load_pair("k1", kview, 1, H, T)
-        for lo, hi in ((0, H), (H, T)):
-            load_pair("q0", qview, 0, lo, hi)
         qpl = {}
-        for t in (2, 3):
-            q_t = keep.tile([P, T], F32, name="qplane%d" % t)
-            nc.sync.dma_start(q_t[:], qview[:, t, :])
-            qpl[t] = q_t
-        vraw = keep.tile([P, T], F32, name="vraw", tag="vraw")
+        for t in range(4):
+            qpl[t] = keep.tile([P, T], F32, name="qplane%d" % t)
+            nc.sync.dma_start(qpl[t][:], qview[:, t, :])
+        vraw = keep.tile([P, T], F32, name="vraw")
         nc.sync.dma_start(vraw[:], vT)
-
-        window = keep.tile([P, T], F32, name="window")
-        for i in range(8):
-            nc.gpsimd.memset(window[:, i * 256 : (i + 1) * 256], 0.0)
 
         ksg = keep.tile([P, N], F32, name="ksg")
         nc.vector.tensor_copy(ksg[:], ksw[:].indirect(slots[:]))
@@ -84,23 +83,19 @@ def tile_attend_x_router_ks_kernel(tc, xq, kT, vT, ks, vs, offs, qoffs, out):
         nks_col = keep.tile([P, 8], F32, name="nks_col")
         vs_col = keep.tile([P, 8], F32, name="vs_col")
         for g in range(2):
-            b = banks.tile([P, 4, P], F32, name="ksb%d" % g, tag="b%d" % g, bufs=1)
             for i in range(4):
-                nc.tensor.transpose(b[:, i, :], ksg[:, (4 * g + i) * P : (4 * g + i + 1) * P], ident[:])
-            nc.vector.tensor_scalar(nks_col[:, 4 * g : 4 * g + 4], b[:, :, 0], -1.0, None, MULT)
+                c = 4 * g + i
+                nc.tensor.transpose(bank(g)[:, i * P : (i + 1) * P], ksg[:, c * P : (c + 1) * P], ident[:])
+            nc.vector.tensor_scalar(nks_col[:, 4 * g : 4 * g + 4], bank(g)[:, 0:BANK:P], -1.0, None, MULT)
         for g in range(2):
-            b = banks.tile([P, 4, P], F32, name="vsb%d" % g, tag="b%d" % (2 + g), bufs=1)
             for t in range(4):
-                nc.tensor.transpose(b[:, t, :], vsg[:, g * 512 + t : (g + 1) * 512 : 4], ident[:])
-            nc.vector.tensor_copy(vs_col[:, 4 * g : 4 * g + 4], b[:, :, 0])
+                nc.tensor.transpose(bank(2 + g)[:, t * P : (t + 1) * P], vsg[:, g * 512 + t : (g + 1) * 512 : 4], ident[:])
+            nc.vector.tensor_copy(vs_col[:, 4 * g : 4 * g + 4], bank(2 + g)[:, 0:BANK:P])
 
         kx = keep.tile([P, 4 * N], BF16, name="kx", align_bytes=64)
         qx = keep.tile([P, 4 * NQ], BF16, name="qx", align_bytes=64)
-        pair = {}
 
         def cast(key, lo, hi, engine):
-            if lo == hi:
-                return
             dst = pair[key][:].rearrange("p (w e) -> p w e", e=2)[:, lo:hi, :]
             src = raw[key][:, :, lo:hi].rearrange("p e w -> p w e")
             if engine == "s":
@@ -108,36 +103,38 @@ def tile_attend_x_router_ks_kernel(tc, xq, kT, vT, ks, vs, offs, qoffs, out):
             else:
                 nc.vector.tensor_copy(dst, src)
 
-        def gather_pair(key, wide, e, offsets):
-            dst = wide[:].bitcast(U32).rearrange("p (n u) -> p n u", u=2)[:, :, e]
-            nc.vector.tensor_copy(dst, pair[key][:].bitcast(U32).indirect(offsets))
+        kg = keep.tile([P, 2, N], U32, name="kg")
 
-        for key in ("k0", "k1", "q0"):
-            pair_tile = keep.tile([P, 2 * T], BF16, name="pair_" + key, align_bytes=64)
-            pair[key] = pair_tile
+        def gather_pair(key, u):
+            nc.vector.tensor_copy(kg[:, u, :], pair[key][:].bitcast(U32).indirect(slots[:]))
+
         cast("k0", 0, 512, "s")
         cast("k0", 512, 1280, "s")
         cast("k0", 1280, 1536, "s")
         cast("k0", 1536, 2048, "v")
-        gather_pair("k0", kx, 0, slots[:])
+        gather_pair("k0", 0)
         cast("k1", 0, H, "s")
         cast("k1", H, 1536, "s")
         cast("k1", 1536, T, "v")
-        gather_pair("k1", kx, 1, slots[:])
+        gather_pair("k1", 1)
         kc = keep.tile([P, N], U32, name="kc", align_bytes=64)
         ksc = keep.tile([P, N], U8, name="ksc", align_bytes=64)
-        nc.vector.quantize_mx(out=kc[:].bitcast(FP8X4), scales=ksc[:], in_=kx[:])
-        cast("q0", 0, H, "s")
-        cast("q0", H, T, "s")
-        gather_pair("q0", qx, 0, qlist[:])
+        qg = keep.tile([P, 2, NQ], BF16, name="qg")
+        for t in range(2):
+            nc.vector.tensor_copy(qg[:, t, :], qpl[t][:].indirect(qlist[:]))
+        for g in range(2):
+            cols = slice(g * 512, (g + 1) * 512)
+            words = kx[:].bitcast(U32).rearrange("p (n u) -> p n u", u=2)
+            nc.scalar.copy(words[:, cols, :], kg[:, :, cols].rearrange("p u n -> p n u"))
+            nc.vector.quantize_mx(out=kc[:, cols].bitcast(FP8X4), scales=ksc[:, cols], in_=kx[:, g * 2048 : (g + 1) * 2048])
+        nc.scalar.copy(qx[:].rearrange("p (n f) -> p n f", f=4)[:, :, 0:2], qg[:].rearrange("p t n -> p n t"))
 
         nks_row = keep.tile([P, 2, 4, P], F32, name="nks_row")
         for g in range(2):
-            b = banks.tile([P, 4 * P], F32, name="ksr%d" % g, tag="b%d" % (4 + g), bufs=1)
             for i in range(4):
                 c = 4 * g + i
-                nc.tensor.transpose(b[:, i * P : (i + 1) * P], nks_col[:, c : c + 1].to_broadcast([P, P]), ident[:])
-            nc.scalar.copy(nks_row[:, g, :, :], b[:].rearrange("p (s t) -> p t s", t=4))
+                nc.tensor.transpose(bank(4 + g)[:, i * P : (i + 1) * P], nks_col[:, c : c + 1].to_broadcast([P, P]), ident[:])
+            nc.scalar.copy(nks_row[:, g, :, :], bank(4 + g).rearrange("p (s t) -> p t s", t=4))
 
         qc = keep.tile([P, NQ], U32, name="qc", align_bytes=64)
         qsc = keep.tile([P, NQ], U8, name="qsc", align_bytes=64)
@@ -146,237 +143,159 @@ def tile_attend_x_router_ks_kernel(tc, xq, kT, vT, ks, vs, offs, qoffs, out):
             dst = qx[:].rearrange("p (n f) -> p n f", f=4)[:, lo:hi, t]
             nc.vector.tensor_copy(dst, qpl[t][:].indirect(qlist[:, lo // 16 : hi // 16]))
 
-        gather_q(2, 0, 512)
-        for h in range(2):
-            gather_q(3, h * 224, (h + 1) * 256)
+        def quantise_q(h):
             nc.vector.quantize_mx(
                 out=qc[:, h * 256 : (h + 1) * 256].bitcast(FP8X4),
                 scales=qsc[:, h * 256 : (h + 1) * 256],
                 in_=qx[:, h * 1024 : (h + 1) * 1024],
             )
 
+        gather_q(2, 0, 512)
+        for h in range(2):
+            gather_q(3, h * 256, (h + 1) * 256)
+            quantise_q(h)
+
         nm = keep.tile([P, 4], F32, name="nm")
         total = keep.tile([P, 4], F32, name="total")
         y_sb = keep.tile([P, NQ], F32, name="y_sb")
         rl_sb = keep.tile([P, NQ], F32, name="rl_sb")
         rl = keep.tile([P, 4], F32, name="rl")
-        R = (0, 1)
-        by_slot = {}
-        SB, TB, PB, VB, YB, RB = ({0: (0, 1), 1: (2, 3), 2: (4, 5, 6, 7)}, {2: (0, 1), 3: (2, 3)}, {0: (4, 5), 1: (7, 4), 2: (5, 0), 3: (1, 2)}, 6, (6, 7), (3, 3))
-        found = {}
-        state = {}
-        ybanks = []
+        a_all = keep.tile([P, 4, N], F32, name="a_all")
+        half = keep.tile([P, 4], F32, name="half")
+        at = keep.tile([P, 8, NQ], F32, name="at")
+        p_all = keep.tile([P, 4, N], F32, name="p_all")
+        wx = keep.tile([P, 4, N], BF16, name="wx", align_bytes=64)
+        wc = keep.tile([P, 4, 2 * P], U32, name="wc", align_bytes=64)
+        wsc = keep.tile([P, 4, 2 * P], U8, name="wsc", align_bytes=64)
+        A_BANK = {1: 0, 2: 2, 3: 4}
+        P_BANK = {0: 6, 1: 0, 2: 2, 3: 4}
 
-        def scores(j):
-            q_cols = slice(j * P, (j + 1) * P)
-            res = []
+        def mx(dst, lhs, lhs_scale, rhs, rhs_scale, start=True, stop=True):
+            nc.tensor.matmul_mx(out=dst, lhsT=lhs.bitcast(FP8X4), lhsT_scale=lhs_scale, rhs=rhs.bitcast(FP8X4), rhs_scale=rhs_scale, start=start, stop=stop)
+
+        def scores_by_query():
             for g in range(2):
-                b = banks.tile([P, 512], F32, name="sc%d_%d" % (j, g), tag="b%d" % SB[j][g], bufs=1)
                 k_cols = slice(g * 512, (g + 1) * 512)
-                nc.tensor.matmul_mx(
-                    out=b[:],
-                    lhsT=qc[:, q_cols].bitcast(FP8X4),
-                    lhsT_scale=qsc[:, q_cols],
-                    rhs=kc[:, k_cols].bitcast(FP8X4),
-                    rhs_scale=ksc[:, k_cols],
-                    start=True,
-                    stop=True,
-                )
-                res.append(b)
-            found[j] = res
+                mx(bank(g), qc[:, 0:P], qsc[:, 0:P], kc[:, k_cols], ksc[:, k_cols])
 
-        def scores_by_slot(js):
-            width = len(js) * P
-            q_cols = slice(js[0] * P, (js[-1] + 1) * P)
-            per = 512 // width
-            at = keep.tile([P, 8, width], F32, name="at%d" % js[0], tag="vraw")
+        def scale_by_query():
+            for g in range(2):
+                dst = a_all[:, 0, g * BANK : (g + 1) * BANK].rearrange("p (t s) -> p t s", t=4)
+                nc.vector.tensor_tensor(dst, bank(g).rearrange("p (s t) -> p t s", t=4), nks_row[:, g, :, :], MULT)
+
+        def scores_by_slot(j0, groups, b0):
+            width = groups * P
+            q_cols = slice(j0 * P, j0 * P + width)
+            per = BANK // width
             for n in range(8 // per):
-                b = banks.tile([P, 512], F32, name="ss%d_%d" % (js[0], n), tag="b%d" % SB[js[0]][n], bufs=1)
                 for i in range(per):
                     k_cols = slice((per * n + i) * P, (per * n + i + 1) * P)
-                    nc.tensor.matmul_mx(
-                        out=b[:, i * width : (i + 1) * width],
-                        lhsT=kc[:, k_cols].bitcast(FP8X4),
-                        lhsT_scale=ksc[:, k_cols],
-                        rhs=qc[:, q_cols].bitcast(FP8X4),
-                        rhs_scale=qsc[:, q_cols],
-                        start=True,
-                        stop=True,
-                    )
+                    mx(bank(b0 + n)[:, i * width : (i + 1) * width], kc[:, k_cols], ksc[:, k_cols], qc[:, q_cols], qsc[:, q_cols])
                 for i in range(per):
                     c = per * n + i
-                    nc.scalar.activation(
-                        at[:, c, :], b[:, i * width : (i + 1) * width], COPY, scale=nks_col[:, c : c + 1]
-                    )
-            for i, j in enumerate(js):
-                by_slot[j] = (at, i)
+                    nc.scalar.activation(at[:, c, q_cols], bank(b0 + n)[:, i * width : (i + 1) * width], COPY, scale=nks_col[:, c : c + 1])
 
-        def scale_rows(j):
-            if j not in R:
-                at, col = by_slot[j]
-                res = []
-                for g in range(2):
-                    b = banks.tile([P, 512], F32, name="ts%d_%d" % (j, g), tag="b%d" % TB[j][g], bufs=1)
-                    for i in range(4):
-                        nc.tensor.transpose(
-                            b[:, i * P : (i + 1) * P], at[:, 4 * g + i, col * P : (col + 1) * P], ident[:]
-                        )
-                    res.append(b)
-                found[j] = res
-            else:
-                a = keep.tile([P, 2, 4, P], F32, name="a%d" % j)
-                for g in range(2):
-                    nc.vector.tensor_tensor(
-                        a[:, g, :, :], found[j][g][:].rearrange("p (s t) -> p t s", t=4), nks_row[:, g, :, :], MULT
-                    )
-                found[j] = a
-            p = keep.tile([P, 2, 4, P], F32, name="p%d" % j)
-            wx = keep.tile([P, 2, 4 * P], BF16, name="wx%d" % j, align_bytes=64)
-            wc = keep.tile([P, 2 * P], U32, name="wc%d" % j, align_bytes=64)
-            wsc = keep.tile([P, 2 * P], U8, name="wsc%d" % j, align_bytes=64)
-            state[j] = (p, wx, wc, wsc)
+        def turn_scores(j):
+            for c in range(8):
+                nc.tensor.transpose(bank(A_BANK[j], 2)[:, c * P : (c + 1) * P], at[:, c, j * P : (j + 1) * P], ident[:])
 
         def stabiliser(j):
-            if j not in R:
-                half = keep.tile([P, 2], F32, name="half%d" % j)
-                for g in range(2):
-                    nc.vector.tensor_reduce(half[:, g : g + 1], found[j][g][:], X, MIN)
-                nc.vector.tensor_tensor(nm[:, j : j + 1], half[:, 0:1], half[:, 1:2], MIN)
-            else:
-                nc.vector.tensor_reduce(nm[:, j : j + 1], found[j][:].rearrange("p g t s -> p (g t s)"), X, MIN)
+            if j == 0:
+                nc.vector.tensor_reduce(nm[:, 0:1], a_all[:, 0, :], X, MIN)
+                return
+            for g in range(2):
+                dst = a_all[:, j, g * BANK : (g + 1) * BANK].rearrange("p (t s) -> p t s", t=4)
+                src = bank(A_BANK[j] + g).rearrange("p (s t) -> p t s", t=4)
+                first = None if g == 0 else half[:, j : j + 1]
+                least = half[:, j : j + 1] if g == 0 else nm[:, j : j + 1]
+                nc.vector.tensor_scalar(dst, src, 1.0, first, MULT, MIN, accum_out=least)
 
         def weights(j):
-            p = state[j][0]
-            if j in R:
-                nc.scalar.activation(
-                    p[:].rearrange("p g t s -> p (g t s)"),
-                    found[j][:].rearrange("p g t s -> p (g t s)"),
-                    EXP,
-                    bias=nm[:, j : j + 1],
-                    scale=-1.0,
-                    accum_out=total[:, j : j + 1],
-                )
-                return
-            parts = keep.tile([P, 2], F32, name="parts%d" % j)
-            for g in range(2):
-                src = found[j][g][:].rearrange("p (s t) -> p t s", t=4) if j not in R else found[j][:, g, :, :]
-                nc.scalar.activation(
-                    p[:, g, :, :], src, EXP, bias=nm[:, j : j + 1], scale=-1.0, accum_out=parts[:, g : g + 1]
-                )
-            nc.gpsimd.tensor_tensor(total[:, j : j + 1], parts[:, 0:1], parts[:, 1:2], ADD)
+            nc.scalar.activation(p_all[:, j, :], a_all[:, j, :], EXP, bias=nm[:, j : j + 1], scale=-1.0, accum_out=total[:, j : j + 1])
 
         def turn_and_scale(j):
-            p, wx, wc, wsc = state[j]
             for g in range(2):
-                b = banks.tile([P, 4, P], F32, name="pt%d_%d" % (j, g), tag="b%d" % PB[j][g], bufs=1)
+                b = bank(P_BANK[j] + g)
                 for t in range(4):
-                    nc.tensor.transpose(b[:, t, :], p[:, g, t, :], ident[:])
+                    c = 4 * g + t
+                    nc.tensor.transpose(b[:, t * P : (t + 1) * P], p_all[:, j, c * P : (c + 1) * P], ident[:])
                 nc.vector.tensor_tensor(
-                    wx[:, g, :].rearrange("p (q t) -> p q t", t=4),
-                    b[:].rearrange("p t q -> p q t"),
+                    wx[:, j, g * BANK : (g + 1) * BANK].rearrange("p (q t) -> p q t", t=4),
+                    b.rearrange("p (t q) -> p q t", t=4),
                     vs_col[:, 4 * g : 4 * g + 4].unsqueeze(1).to_broadcast([P, P, 4]),
                     MULT,
                 )
 
         def quantise_weights(j):
-            p, wx, wc, wsc = state[j]
-            cuts = 2 if j == 3 else 1
-            gs = 2 // cuts
-            for i in range(cuts):
-                cols = slice(i * gs * P, (i + 1) * gs * P)
-                nc.vector.quantize_mx(
-                    out=wc[:, cols].bitcast(FP8X4),
-                    scales=wsc[:, cols],
-                    in_=wx[:, i * gs : (i + 1) * gs, :].rearrange("p g n -> p (g n)"),
-                )
+            nc.vector.quantize_mx(out=wc[:, j, :].bitcast(FP8X4), scales=wsc[:, j, :], in_=wx[:, j, :])
 
         def values(j):
-            p, wx, wc, wsc = state[j]
-            if j % 2 == 0:
-                y_bank = banks.tile([P, 2 * P], F32, name="y%d" % j, tag="b%d" % YB[j // 2], bufs=1)
-                ybanks.append(y_bank)
             for g in range(2):
                 cols = slice(g * P, (g + 1) * P)
-                nc.tensor.matmul_mx(
-                    out=ybanks[j // 2][:, j % 2 * P : (j % 2 + 1) * P],
-                    lhsT=vc[:, cols].bitcast(FP8X4),
-                    lhsT_scale=vsc[:, cols],
-                    rhs=wc[:, cols].bitcast(FP8X4),
-                    rhs_scale=wsc[:, cols],
-                    start=(g == 0),
-                    stop=(g == 1),
-                )
+                mx(bank(j // 2)[:, j % 2 * P : (j % 2 + 1) * P], vc[:, cols], vsc[:, cols], wc[:, j, cols], wsc[:, j, cols], g == 0, g == 1)
 
         def normaliser(h):
             js = slice(2 * h, 2 * h + 2)
             nc.vector.reciprocal(rl[:, js], total[:, js])
-            b = banks.tile([P, 256], F32, name="rlb%d" % h, tag="b%d" % RB[h], bufs=1)
+            dst = bank(7)[:, h * 256 : (h + 1) * 256]
             for i in range(2):
                 c = 2 * h + i
-                nc.tensor.transpose(b[:, i * P : (i + 1) * P], rl[:, c : c + 1].to_broadcast([P, P]), ident[:])
-            nc.scalar.copy(rl_sb[:, h * 256 : (h + 1) * 256], b[:])
+                nc.tensor.transpose(dst[:, i * P : (i + 1) * P], rl[:, c : c + 1].to_broadcast([P, P]), ident[:])
+            nc.scalar.copy(rl_sb[:, h * 256 : (h + 1) * 256], dst)
 
         def scatter(h):
             cols = slice(h * 256, (h + 1) * 256)
-            nc.scalar.copy(y_sb[:, cols], ybanks[h][:])
-            nc.vector.tensor_tensor(
-                window[:].indirect(qlist[:, h * 16 : (h + 1) * 16]), y_sb[:, cols], rl_sb[:, cols], MULT
-            )
+            nc.scalar.copy(y_sb[:, cols], bank(h)[:, 0:256])
+            nc.vector.tensor_tensor(window[:].indirect(qlist[:, h * 16 : (h + 1) * 16]), y_sb[:, cols], rl_sb[:, cols], MULT)
 
         vb = keep.tile([P, T], BF16, name="vb")
-        vg = keep.tile([P, N, 2], BF16, name="vg")
-        vx = keep.tile([P, 2, DV, 4], BF16, name="vx", align_bytes=64)
+        vg = keep.tile([P, N], BF16, name="vg")
+        vx = keep.tile([P, N], BF16, name="vx", align_bytes=64)
         vc = keep.tile([P, 2 * DV], U32, name="vc", align_bytes=64)
         vsc = keep.tile([P, 2 * DV], U8, name="vsc", align_bytes=64)
 
-        def load_values():
+        def gather_values():
             for i in range(2):
                 cols = slice(i * H, (i + 1) * H)
-                nc.scalar.activation(vb[:, cols], vraw[:, cols], COPY)
-
-        def gather_values():
+                nc.vector.tensor_copy(vb[:, cols], vraw[:, cols])
             for g in range(2):
-                nc.scalar.activation(
-                    vg[:, g * 512 : (g + 1) * 512, 0], vb[:].indirect(slots[:, g * 32 : (g + 1) * 32]), COPY
-                )
-            b = banks.tile([P, 2, 4, DV], BF16, name="vt", tag="b%d" % VB, bufs=1)
-            for g in range(2):
-                for t in range(4):
-                    nc.tensor.transpose(b[:, g, t, :], vg[:, g * 512 + t : (g + 1) * 512 : 4, 0], ident_bf16[:])
-            nc.scalar.copy(vx[:], b[:].rearrange("p g t e -> p g e t"))
+                nc.scalar.activation(vg[:, g * 512 : (g + 1) * 512], vb[:].indirect(slots[:, g * 32 : (g + 1) * 32]), COPY)
 
-        scores(0)
-        scores(1)
-        load_values()
-        scores_by_slot((2, 3,))
-        scale_rows(0)
+        def turn_values():
+            words = vg[:].bitcast(F32)
+            for g in range(2):
+                for u in range(2):
+                    c = 2 * g + u
+                    nc.tensor.transpose(bank(6)[:, c * P : (c + 1) * P], words[:, g * 256 + u : (g + 1) * 256 : 2], ident[:])
+            nc.scalar.copy(vx[:].bitcast(F32).rearrange("p (g e u) -> p g e u", g=2, u=2), bank(6).rearrange("p (g u e) -> p g e u", g=2, u=2))
+            nc.vector.quantize_mx(out=vc[:].bitcast(FP8X4), scales=vsc[:], in_=vx[:])
+
+        scores_by_query()
+        scores_by_slot(1, 1, 2)
+        scores_by_slot(2, 2, 4)
+        scale_by_query()
         stabiliser(0)
         weights(0)
-        scale_rows(1)
-        stabiliser(1)
-        weights(1)
+        for j in (1, 2, 3):
+            turn_scores(j)
+            stabiliser(j)
+            weights(j)
         gather_values()
-        scale_rows(2)
-        stabiliser(2)
-        weights(2)
-        scale_rows(3)
-        stabiliser(3)
-        weights(3)
         turn_and_scale(0)
         quantise_weights(0)
-        nc.vector.quantize_mx(out=vc[:].bitcast(FP8X4), scales=vsc[:], in_=vx[:].rearrange("p g e t -> p (g e t)"))
-        values(0)
         turn_and_scale(1)
         quantise_weights(1)
+        turn_values()
+        values(0)
         values(1)
+        normaliser(0)
         turn_and_scale(2)
         quantise_weights(2)
-        values(2)
-        normaliser(0)
         turn_and_scale(3)
-        normaliser(1)
-        scatter(0)
         quantise_weights(3)
+        normaliser(1)
+        values(2)
         values(3)
+        scatter(0)
         scatter(1)
         nc.sync.dma_start(out, window[:])

@@ -53,7 +53,7 @@ def tile_attend_x_router_ks_kernel(tc, xq, kT, vT, ks, vs, offs, qoffs, out):
         raw = {}
         pair = {}
         for key in ("k0", "k1"):
-            raw[key] = keep.tile([P, 2, T], F32, name="raw_" + key)
+            raw[key] = keep.tile([P, 2, T], F32, name="raw_" + key, tag="raw_" + key)
             pair[key] = keep.tile([P, 2 * T], BF16, name="pair_" + key, align_bytes=64)
 
         def load_pair(key, view, e, lo, hi):
@@ -88,8 +88,9 @@ def tile_attend_x_router_ks_kernel(tc, xq, kT, vT, ks, vs, offs, qoffs, out):
                 nc.tensor.transpose(bank(g)[:, i * P : (i + 1) * P], ksg[:, c * P : (c + 1) * P], ident[:])
             nc.vector.tensor_scalar(nks_col[:, 4 * g : 4 * g + 4], bank(g)[:, 0:BANK:P], -1.0, None, MULT)
         for g in range(2):
-            for t in range(4):
-                nc.tensor.transpose(bank(2 + g)[:, t * P : (t + 1) * P], vsg[:, g * 512 + t : (g + 1) * 512 : 4], ident[:])
+            for i in range(4):
+                c = 4 * g + i
+                nc.tensor.transpose(bank(2 + g)[:, i * P : (i + 1) * P], vsg[:, c * P : (c + 1) * P], ident[:])
             nc.vector.tensor_copy(vs_col[:, 4 * g : 4 * g + 4], bank(2 + g)[:, 0:BANK:P])
 
         kx = keep.tile([P, 4 * N], BF16, name="kx", align_bytes=64)
@@ -129,12 +130,18 @@ def tile_attend_x_router_ks_kernel(tc, xq, kT, vT, ks, vs, offs, qoffs, out):
             nc.vector.quantize_mx(out=kc[:, cols].bitcast(FP8X4), scales=ksc[:, cols], in_=kx[:, g * 2048 : (g + 1) * 2048])
         nc.scalar.copy(qx[:].rearrange("p (n f) -> p n f", f=4)[:, :, 0:2], qg[:].rearrange("p t n -> p n t"))
 
-        nks_row = keep.tile([P, 2, 4, P], F32, name="nks_row")
+        nks_row = keep.tile([P, 2, BANK], F32, name="nks_row")
         for g in range(2):
             for i in range(4):
                 c = 4 * g + i
                 nc.tensor.transpose(bank(4 + g)[:, i * P : (i + 1) * P], nks_col[:, c : c + 1].to_broadcast([P, P]), ident[:])
-            nc.scalar.copy(nks_row[:, g, :, :], bank(4 + g).rearrange("p (s t) -> p t s", t=4))
+            nc.scalar.copy(nks_row[:, g, :].rearrange("p (u s e) -> p u s e", u=2, e=2), bank(4 + g).rearrange("p (s u e) -> p u s e", u=2, e=2))
+        vs_row = keep.tile([P, 2, BANK], F32, name="vs_row")
+        for g in range(2):
+            for t in range(4):
+                c = 4 * g + t
+                nc.tensor.transpose(bank(6 + g)[:, t * P : (t + 1) * P], vs_col[:, c : c + 1].to_broadcast([P, P]), ident[:])
+            nc.scalar.copy(vs_row[:, g, :].rearrange("p (u s e) -> p u s e", u=2, e=2), bank(6 + g).rearrange("p (s u e) -> p u s e", u=2, e=2))
 
         qc = keep.tile([P, NQ], U32, name="qc", align_bytes=64)
         qsc = keep.tile([P, NQ], U8, name="qsc", align_bytes=64)
@@ -160,18 +167,32 @@ def tile_attend_x_router_ks_kernel(tc, xq, kT, vT, ks, vs, offs, qoffs, out):
         y_sb = keep.tile([P, NQ], F32, name="y_sb")
         rl_sb = keep.tile([P, NQ], F32, name="rl_sb")
         rl = keep.tile([P, 4], F32, name="rl")
-        a_all = keep.tile([P, 4, N], F32, name="a_all")
+        a_all = keep.tile([P, 4, N], F32, name="a_all", tag="raw_k0")
         half = keep.tile([P, 4], F32, name="half")
-        at = keep.tile([P, 8, NQ], F32, name="at")
+        at = keep.tile([P, 8, NQ], F32, name="at", tag="raw_k1")
         p_all = keep.tile([P, 4, N], F32, name="p_all")
         wx = keep.tile([P, 4, N], BF16, name="wx", align_bytes=64)
         wc = keep.tile([P, 4, 2 * P], U32, name="wc", align_bytes=64)
         wsc = keep.tile([P, 4, 2 * P], U8, name="wsc", align_bytes=64)
+        wq = keep.tile([P, 4, N], BF16, name="wq")
         A_BANK = {1: 0, 2: 2, 3: 4}
-        P_BANK = {0: 6, 1: 0, 2: 2, 3: 4}
+        P_BANK = {0: 6, 1: 0, 2: 1, 3: 2}
+        Y_BANK = (3, 4)
 
         def mx(dst, lhs, lhs_scale, rhs, rhs_scale, start=True, stop=True):
             nc.tensor.matmul_mx(out=dst, lhsT=lhs.bitcast(FP8X4), lhsT_scale=lhs_scale, rhs=rhs.bitcast(FP8X4), rhs_scale=rhs_scale, start=start, stop=stop)
+
+        def dealt(j, g, b):
+            dst = a_all[:, j, g * BANK : (g + 1) * BANK]
+            return dst.rearrange("p (u s e) -> p u s e", u=2, e=2), b.rearrange("p (s u e) -> p u s e", u=2, e=2)
+
+        def scale_and_turn(j):
+            nc.vector.tensor_tensor(wq[:, j, :], p_all[:, j, :], vs_row[:].rearrange("p g n -> p (g n)"), MULT)
+            b = bank(P_BANK[j])
+            words = wq[:, j, :].bitcast(F32)
+            for c in range(4):
+                nc.tensor.transpose(b[:, c * P : (c + 1) * P], words[:, c * P : (c + 1) * P], ident[:])
+            nc.scalar.copy(wx[:, j, :].bitcast(F32).rearrange("p (g q u) -> p g q u", g=2, u=2), b.rearrange("p (g u q) -> p g q u", g=2, u=2))
 
         def scores_by_query():
             for g in range(2):
@@ -180,8 +201,8 @@ def tile_attend_x_router_ks_kernel(tc, xq, kT, vT, ks, vs, offs, qoffs, out):
 
         def scale_by_query():
             for g in range(2):
-                dst = a_all[:, 0, g * BANK : (g + 1) * BANK].rearrange("p (t s) -> p t s", t=4)
-                nc.vector.tensor_tensor(dst, bank(g).rearrange("p (s t) -> p t s", t=4), nks_row[:, g, :, :], MULT)
+                dst, src = dealt(0, g, bank(g))
+                nc.vector.tensor_tensor(dst, src, nks_row[:, g, :].rearrange("p (u s e) -> p u s e", u=2, e=2), MULT)
 
         def scores_by_slot(j0, groups, b0):
             width = groups * P
@@ -204,8 +225,7 @@ def tile_attend_x_router_ks_kernel(tc, xq, kT, vT, ks, vs, offs, qoffs, out):
                 nc.vector.tensor_reduce(nm[:, 0:1], a_all[:, 0, :], X, MIN)
                 return
             for g in range(2):
-                dst = a_all[:, j, g * BANK : (g + 1) * BANK].rearrange("p (t s) -> p t s", t=4)
-                src = bank(A_BANK[j] + g).rearrange("p (s t) -> p t s", t=4)
+                dst, src = dealt(j, g, bank(A_BANK[j] + g))
                 first = None if g == 0 else half[:, j : j + 1]
                 least = half[:, j : j + 1] if g == 0 else nm[:, j : j + 1]
                 nc.vector.tensor_scalar(dst, src, 1.0, first, MULT, MIN, accum_out=least)
@@ -213,31 +233,18 @@ def tile_attend_x_router_ks_kernel(tc, xq, kT, vT, ks, vs, offs, qoffs, out):
         def weights(j):
             nc.scalar.activation(p_all[:, j, :], a_all[:, j, :], EXP, bias=nm[:, j : j + 1], scale=-1.0, accum_out=total[:, j : j + 1])
 
-        def turn_and_scale(j):
-            for g in range(2):
-                b = bank(P_BANK[j] + g)
-                for t in range(4):
-                    c = 4 * g + t
-                    nc.tensor.transpose(b[:, t * P : (t + 1) * P], p_all[:, j, c * P : (c + 1) * P], ident[:])
-                nc.vector.tensor_tensor(
-                    wx[:, j, g * BANK : (g + 1) * BANK].rearrange("p (q t) -> p q t", t=4),
-                    b.rearrange("p (t q) -> p q t", t=4),
-                    vs_col[:, 4 * g : 4 * g + 4].unsqueeze(1).to_broadcast([P, P, 4]),
-                    MULT,
-                )
-
         def quantise_weights(j):
             nc.vector.quantize_mx(out=wc[:, j, :].bitcast(FP8X4), scales=wsc[:, j, :], in_=wx[:, j, :])
 
         def values(j):
             for g in range(2):
                 cols = slice(g * P, (g + 1) * P)
-                mx(bank(j // 2)[:, j % 2 * P : (j % 2 + 1) * P], vc[:, cols], vsc[:, cols], wc[:, j, cols], wsc[:, j, cols], g == 0, g == 1)
+                mx(bank(Y_BANK[j // 2])[:, j % 2 * P : (j % 2 + 1) * P], vc[:, cols], vsc[:, cols], wc[:, j, cols], wsc[:, j, cols], g == 0, g == 1)
 
         def normaliser(h):
             js = slice(2 * h, 2 * h + 2)
             nc.vector.reciprocal(rl[:, js], total[:, js])
-            dst = bank(7)[:, h * 256 : (h + 1) * 256]
+            dst = bank(5 + h)[:, 0:256]
             for i in range(2):
                 c = 2 * h + i
                 nc.tensor.transpose(dst[:, i * P : (i + 1) * P], rl[:, c : c + 1].to_broadcast([P, P]), ident[:])
@@ -245,7 +252,7 @@ def tile_attend_x_router_ks_kernel(tc, xq, kT, vT, ks, vs, offs, qoffs, out):
 
         def scatter(h):
             cols = slice(h * 256, (h + 1) * 256)
-            nc.scalar.copy(y_sb[:, cols], bank(h)[:, 0:256])
+            nc.scalar.copy(y_sb[:, cols], bank(Y_BANK[h])[:, 0:256])
             nc.vector.tensor_tensor(window[:].indirect(qlist[:, h * 16 : (h + 1) * 16]), y_sb[:, cols], rl_sb[:, cols], MULT)
 
         vb = keep.tile([P, T], BF16, name="vb")
@@ -266,8 +273,8 @@ def tile_attend_x_router_ks_kernel(tc, xq, kT, vT, ks, vs, offs, qoffs, out):
             for g in range(2):
                 for u in range(2):
                     c = 2 * g + u
-                    nc.tensor.transpose(bank(6)[:, c * P : (c + 1) * P], words[:, g * 256 + u : (g + 1) * 256 : 2], ident[:])
-            nc.scalar.copy(vx[:].bitcast(F32).rearrange("p (g e u) -> p g e u", g=2, u=2), bank(6).rearrange("p (g u e) -> p g e u", g=2, u=2))
+                    nc.tensor.transpose(bank(7)[:, c * P : (c + 1) * P], words[:, g * 256 + u : (g + 1) * 256 : 2], ident[:])
+            nc.scalar.copy(vx[:].bitcast(F32).rearrange("p (g e u) -> p g e u", g=2, u=2), bank(7).rearrange("p (g u e) -> p g e u", g=2, u=2))
             nc.vector.quantize_mx(out=vc[:].bitcast(FP8X4), scales=vsc[:], in_=vx[:])
 
         scores_by_query()
@@ -281,21 +288,14 @@ def tile_attend_x_router_ks_kernel(tc, xq, kT, vT, ks, vs, offs, qoffs, out):
             stabiliser(j)
             weights(j)
         gather_values()
-        turn_and_scale(0)
-        quantise_weights(0)
-        turn_and_scale(1)
-        quantise_weights(1)
+        for j in range(4):
+            scale_and_turn(j)
         turn_values()
-        values(0)
-        values(1)
-        normaliser(0)
-        turn_and_scale(2)
-        quantise_weights(2)
-        turn_and_scale(3)
-        quantise_weights(3)
-        normaliser(1)
-        values(2)
-        values(3)
+        for j in range(4):
+            quantise_weights(j)
+            values(j)
+            if j % 2 == 1:
+                normaliser(j // 2)
         scatter(0)
         scatter(1)
         nc.sync.dma_start(out, window[:])

@@ -54,7 +54,7 @@ def tile_attend_x_router_ks_kernel(tc, xq, kT, vT, ks, vs, offs, qoffs, out):
         pair = {}
         for key in ("k0", "k1"):
             raw[key] = keep.tile([P, 2, T], F32, name="raw_" + key, tag="raw_" + key)
-            pair[key] = keep.tile([P, 2 * T], BF16, name="pair_" + key, align_bytes=64)
+            pair[key] = keep.tile([P, 2 * T], BF16, name="pair_" + key, tag="pair_" + key, align_bytes=64)
 
         def load_pair(key, view, e, lo, hi):
             nc.sync.dma_start(raw[key][:, :, lo:hi], view[:, 2 * e : 2 * e + 2, lo:hi])
@@ -65,8 +65,8 @@ def tile_attend_x_router_ks_kernel(tc, xq, kT, vT, ks, vs, offs, qoffs, out):
         load_pair("k0", kview, 0, 512, 1280)
         nc.sync.dma_start(ksw[0:1, :], ks[0:1, :])
         load_pair("k0", kview, 0, 1280, 2048)
-        load_pair("k1", kview, 1, 0, H)
         nc.sync.dma_start(vsw[0:1, :], vs[0:1, :])
+        load_pair("k1", kview, 1, 0, H)
         load_pair("k1", kview, 1, H, T)
         qpl = {}
         for t in range(4):
@@ -80,18 +80,14 @@ def tile_attend_x_router_ks_kernel(tc, xq, kT, vT, ks, vs, offs, qoffs, out):
         vsg = keep.tile([P, N], F32, name="vsg")
         nc.vector.tensor_copy(vsg[:], vsw[:].indirect(slots[:]))
 
-        nks_col = keep.tile([P, 8], F32, name="nks_col")
-        vs_col = keep.tile([P, 8], F32, name="vs_col")
         for g in range(2):
             for i in range(4):
                 c = 4 * g + i
                 nc.tensor.transpose(bank(g)[:, i * P : (i + 1) * P], ksg[:, c * P : (c + 1) * P], ident[:])
-            nc.vector.tensor_scalar(nks_col[:, 4 * g : 4 * g + 4], bank(g)[:, 0:BANK:P], -1.0, None, MULT)
         for g in range(2):
             for i in range(4):
                 c = 4 * g + i
                 nc.tensor.transpose(bank(2 + g)[:, i * P : (i + 1) * P], vsg[:, c * P : (c + 1) * P], ident[:])
-            nc.vector.tensor_copy(vs_col[:, 4 * g : 4 * g + 4], bank(2 + g)[:, 0:BANK:P])
 
         kx = keep.tile([P, 4 * N], BF16, name="kx", align_bytes=64)
         qx = keep.tile([P, 4 * NQ], BF16, name="qx", align_bytes=64)
@@ -130,13 +126,19 @@ def tile_attend_x_router_ks_kernel(tc, xq, kT, vT, ks, vs, offs, qoffs, out):
             nc.vector.quantize_mx(out=kc[:, cols].bitcast(FP8X4), scales=ksc[:, cols], in_=kx[:, g * 2048 : (g + 1) * 2048])
         nc.scalar.copy(qx[:].rearrange("p (n f) -> p n f", f=4)[:, :, 0:2], qg[:].rearrange("p t n -> p n t"))
 
-        nks_row = keep.tile([P, 2, BANK], F32, name="nks_row")
+        scales = keep.tile([P, 2 * N + 16], F32, name="scales", tag="pair_k1", align_bytes=64)
+        nks_row = scales[:, 0:N].rearrange("p (g n) -> p g n", g=2)
+        vs_row = scales[:, N : 2 * N].rearrange("p (g n) -> p g n", g=2)
+        nks_col = scales[:, 2 * N : 2 * N + 8]
+        vs_col = scales[:, 2 * N + 8 : 2 * N + 16]
+        for g in range(2):
+            nc.vector.tensor_scalar(nks_col[:, 4 * g : 4 * g + 4], bank(g)[:, 0:BANK:P], -1.0, None, MULT)
+            nc.vector.tensor_copy(vs_col[:, 4 * g : 4 * g + 4], bank(2 + g)[:, 0:BANK:P])
         for g in range(2):
             for i in range(4):
                 c = 4 * g + i
                 nc.tensor.transpose(bank(4 + g)[:, i * P : (i + 1) * P], nks_col[:, c : c + 1].to_broadcast([P, P]), ident[:])
             nc.scalar.copy(nks_row[:, g, :].rearrange("p (u s e) -> p u s e", u=2, e=2), bank(4 + g).rearrange("p (s u e) -> p u s e", u=2, e=2))
-        vs_row = keep.tile([P, 2, BANK], F32, name="vs_row")
         for g in range(2):
             for t in range(4):
                 c = 4 * g + t
@@ -187,7 +189,7 @@ def tile_attend_x_router_ks_kernel(tc, xq, kT, vT, ks, vs, offs, qoffs, out):
             return dst.rearrange("p (u s e) -> p u s e", u=2, e=2), b.rearrange("p (s u e) -> p u s e", u=2, e=2)
 
         def scale_and_turn(j):
-            nc.vector.tensor_tensor(wq[:, j, :], p_all[:, j, :], vs_row[:].rearrange("p g n -> p (g n)"), MULT)
+            nc.vector.tensor_tensor(wq[:, j, :], p_all[:, j, :], vs_row.rearrange("p g n -> p (g n)"), MULT)
             b = bank(P_BANK[j])
             words = wq[:, j, :].bitcast(F32)
             for c in range(4):

@@ -36,14 +36,12 @@ def tile_attend_x_router_ks_kernel(tc, xq, kT, vT, ks, vs, offs, qoffs, out):
 
         slots = lists.tile([P, N // 16], U16, name="slots")
         qlist = lists.tile([P, NQ // 16], U16, name="qlist")
-        ksw = keep.tile([P, T], F32, name="ksw")
+        ksw = keep.tile([P, T], F32, name="ksw", tag="ksw")
         vsw = keep.tile([P, T], F32, name="vsw")
-        window = keep.tile([P, T], F32, name="window")
         warm = keep.tile([P, 1], F32, name="warm")
         nc.vector.memset(warm[:], 0.0)
         nc.vector.memset(ksw[:], 0.0)
         nc.vector.memset(vsw[:], 0.0)
-        nc.vector.memset(window[:], 0.0)
         nc.scalar.activation(warm[:], warm[:], EXP)
         ident = keep.tile([P, P], F32, name="ident")
         make_identity(nc, ident[:])
@@ -59,13 +57,13 @@ def tile_attend_x_router_ks_kernel(tc, xq, kT, vT, ks, vs, offs, qoffs, out):
         def load_pair(key, view, e, lo, hi):
             nc.sync.dma_start(raw[key][:, :, lo:hi], view[:, 2 * e : 2 * e + 2, lo:hi])
 
-        load_pair("k0", kview, 0, 0, 512)
+        load_pair("k0", kview, 0, 0, 768)
         nc.sync.dma_start(slots[:], offs)
-        nc.sync.dma_start(qlist[:], qoffs)
-        load_pair("k0", kview, 0, 512, 1280)
         nc.sync.dma_start(ksw[0:1, :], ks[0:1, :])
-        load_pair("k0", kview, 0, 1280, 2048)
+        load_pair("k0", kview, 0, 768, 1792)
         nc.sync.dma_start(vsw[0:1, :], vs[0:1, :])
+        load_pair("k0", kview, 0, 1792, 2048)
+        nc.sync.dma_start(qlist[:], qoffs)
         load_pair("k1", kview, 1, 0, H)
         load_pair("k1", kview, 1, H, T)
         qpl = {}
@@ -77,6 +75,9 @@ def tile_attend_x_router_ks_kernel(tc, xq, kT, vT, ks, vs, offs, qoffs, out):
 
         ksg = keep.tile([P, N], F32, name="ksg")
         nc.vector.tensor_copy(ksg[:], ksw[:].indirect(slots[:]))
+        window = keep.tile([P, T], F32, name="window", tag="ksw")
+        for i in range(8):
+            nc.gpsimd.memset(window[:, i * 256 : (i + 1) * 256], 0.0)
         vsg = keep.tile([P, N], F32, name="vsg")
         nc.vector.tensor_copy(vsg[:], vsw[:].indirect(slots[:]))
 
@@ -85,9 +86,8 @@ def tile_attend_x_router_ks_kernel(tc, xq, kT, vT, ks, vs, offs, qoffs, out):
                 c = 4 * g + i
                 nc.tensor.transpose(bank(g)[:, i * P : (i + 1) * P], ksg[:, c * P : (c + 1) * P], ident[:])
         for g in range(2):
-            for i in range(4):
-                c = 4 * g + i
-                nc.tensor.transpose(bank(2 + g)[:, i * P : (i + 1) * P], vsg[:, c * P : (c + 1) * P], ident[:])
+            for t in range(4):
+                nc.tensor.transpose(bank(2 + g)[:, t * P : (t + 1) * P], vsg[:, g * 512 + t : (g + 1) * 512 : 4], ident[:])
 
         kx = keep.tile([P, 4 * N], BF16, name="kx", align_bytes=64)
         qx = keep.tile([P, 4 * NQ], BF16, name="qx", align_bytes=64)
@@ -105,10 +105,9 @@ def tile_attend_x_router_ks_kernel(tc, xq, kT, vT, ks, vs, offs, qoffs, out):
         def gather_pair(key, u):
             nc.vector.tensor_copy(kg[:, u, :], pair[key][:].bitcast(U32).indirect(slots[:]))
 
-        cast("k0", 0, 512, "s")
-        cast("k0", 512, 1280, "s")
-        cast("k0", 1280, 1536, "s")
-        cast("k0", 1536, 2048, "v")
+        cast("k0", 0, 768, "s")
+        cast("k0", 768, 1792, "s")
+        cast("k0", 1792, 2048, "v")
         gather_pair("k0", 0)
         cast("k1", 0, H, "s")
         cast("k1", H, 1536, "s")
@@ -143,7 +142,7 @@ def tile_attend_x_router_ks_kernel(tc, xq, kT, vT, ks, vs, offs, qoffs, out):
             for t in range(4):
                 c = 4 * g + t
                 nc.tensor.transpose(bank(6 + g)[:, t * P : (t + 1) * P], vs_col[:, c : c + 1].to_broadcast([P, P]), ident[:])
-            nc.scalar.copy(vs_row[:, g, :].rearrange("p (u s e) -> p u s e", u=2, e=2), bank(6 + g).rearrange("p (s u e) -> p u s e", u=2, e=2))
+            nc.scalar.copy(vs_row[:, g, :].rearrange("p (u s e) -> p u s e", u=2, e=2), bank(6 + g).rearrange("p (u e s) -> p u s e", u=2, e=2))
 
         qc = keep.tile([P, NQ], U32, name="qc", align_bytes=64)
         qsc = keep.tile([P, NQ], U8, name="qsc", align_bytes=64)
@@ -176,22 +175,38 @@ def tile_attend_x_router_ks_kernel(tc, xq, kT, vT, ks, vs, offs, qoffs, out):
         wx = keep.tile([P, 4, N], BF16, name="wx", align_bytes=64)
         wc = keep.tile([P, 4, 2 * P], U32, name="wc", align_bytes=64)
         wsc = keep.tile([P, 4, 2 * P], U8, name="wsc", align_bytes=64)
-        wq = keep.tile([P, 4, N], BF16, name="wq")
+        wq = keep.tile([P, 2, N], BF16, name="wq")
         A_BANK = {1: 0, 2: 2, 3: 4}
-        P_BANK = {0: 6, 1: 0, 2: 1, 3: 2}
-        Y_BANK = (3, 4)
+        BY_WORDS = (0, 2)
+        P_BANK = {0: 6, 1: 0, 2: 6, 3: 2}
+        Y_BANK = (4, 0)
 
         def mx(dst, lhs, lhs_scale, rhs, rhs_scale, start=True, stop=True):
             nc.tensor.matmul_mx(out=dst, lhsT=lhs.bitcast(FP8X4), lhsT_scale=lhs_scale, rhs=rhs.bitcast(FP8X4), rhs_scale=rhs_scale, start=start, stop=stop)
 
         def dealt(j, g, b):
             dst = a_all[:, j, g * BANK : (g + 1) * BANK]
+            if j not in BY_WORDS:
+                return dst.rearrange("p (t s) -> p t s", t=4), b.rearrange("p (s t) -> p t s", t=4)
             return dst.rearrange("p (u s e) -> p u s e", u=2, e=2), b.rearrange("p (s u e) -> p u s e", u=2, e=2)
 
+        def turn_and_scale(j):
+            for g in range(2):
+                b = bank(P_BANK[j] + g)
+                for t in range(4):
+                    c = 4 * g + t
+                    nc.tensor.transpose(b[:, t * P : (t + 1) * P], p_all[:, j, c * P : (c + 1) * P], ident[:])
+                nc.vector.tensor_tensor(
+                    wx[:, j, g * BANK : (g + 1) * BANK].rearrange("p (q t) -> p q t", t=4),
+                    b.rearrange("p (t q) -> p q t", t=4),
+                    vs_col[:, 4 * g : 4 * g + 4].unsqueeze(1).to_broadcast([P, P, 4]),
+                    MULT,
+                )
+
         def scale_and_turn(j):
-            nc.vector.tensor_tensor(wq[:, j, :], p_all[:, j, :], vs_row.rearrange("p g n -> p (g n)"), MULT)
+            nc.gpsimd.tensor_tensor(wq[:, j // 2, :], p_all[:, j, :], vs_row.rearrange("p g n -> p (g n)"), MULT)
             b = bank(P_BANK[j])
-            words = wq[:, j, :].bitcast(F32)
+            words = wq[:, j // 2, :].bitcast(F32)
             for c in range(4):
                 nc.tensor.transpose(b[:, c * P : (c + 1) * P], words[:, c * P : (c + 1) * P], ident[:])
             nc.scalar.copy(wx[:, j, :].bitcast(F32).rearrange("p (g q u) -> p g q u", g=2, u=2), b.rearrange("p (g u q) -> p g q u", g=2, u=2))
@@ -235,8 +250,10 @@ def tile_attend_x_router_ks_kernel(tc, xq, kT, vT, ks, vs, offs, qoffs, out):
         def weights(j):
             nc.scalar.activation(p_all[:, j, :], a_all[:, j, :], EXP, bias=nm[:, j : j + 1], scale=-1.0, accum_out=total[:, j : j + 1])
 
-        def quantise_weights(j):
-            nc.vector.quantize_mx(out=wc[:, j, :].bitcast(FP8X4), scales=wsc[:, j, :], in_=wx[:, j, :])
+        def quantise_weights(j, n):
+            flat = "p j n -> p (j n)"
+            js = slice(j, j + n)
+            nc.vector.quantize_mx(out=wc[:, js, :].rearrange(flat).bitcast(FP8X4), scales=wsc[:, js, :].rearrange(flat), in_=wx[:, js, :].rearrange(flat))
 
         def values(j):
             for g in range(2):
@@ -246,7 +263,7 @@ def tile_attend_x_router_ks_kernel(tc, xq, kT, vT, ks, vs, offs, qoffs, out):
         def normaliser(h):
             js = slice(2 * h, 2 * h + 2)
             nc.vector.reciprocal(rl[:, js], total[:, js])
-            dst = bank(5 + h)[:, 0:256]
+            dst = bank(5 + 2 * h)[:, 0:256]
             for i in range(2):
                 c = 2 * h + i
                 nc.tensor.transpose(dst[:, i * P : (i + 1) * P], rl[:, c : c + 1].to_broadcast([P, P]), ident[:])
@@ -257,18 +274,14 @@ def tile_attend_x_router_ks_kernel(tc, xq, kT, vT, ks, vs, offs, qoffs, out):
             nc.scalar.copy(y_sb[:, cols], bank(Y_BANK[h])[:, 0:256])
             nc.vector.tensor_tensor(window[:].indirect(qlist[:, h * 16 : (h + 1) * 16]), y_sb[:, cols], rl_sb[:, cols], MULT)
 
-        vb = keep.tile([P, T], BF16, name="vb")
         vg = keep.tile([P, N], BF16, name="vg")
         vx = keep.tile([P, N], BF16, name="vx", align_bytes=64)
         vc = keep.tile([P, 2 * DV], U32, name="vc", align_bytes=64)
         vsc = keep.tile([P, 2 * DV], U8, name="vsc", align_bytes=64)
 
         def gather_values():
-            for i in range(2):
-                cols = slice(i * H, (i + 1) * H)
-                nc.vector.tensor_copy(vb[:, cols], vraw[:, cols])
             for g in range(2):
-                nc.scalar.activation(vg[:, g * 512 : (g + 1) * 512], vb[:].indirect(slots[:, g * 32 : (g + 1) * 32]), COPY)
+                nc.vector.tensor_copy(vg[:, g * 512 : (g + 1) * 512], vraw[:].indirect(slots[:, g * 32 : (g + 1) * 32]))
 
         def turn_values():
             words = vg[:].bitcast(F32)
@@ -290,14 +303,15 @@ def tile_attend_x_router_ks_kernel(tc, xq, kT, vT, ks, vs, offs, qoffs, out):
             stabiliser(j)
             weights(j)
         gather_values()
-        for j in range(4):
-            scale_and_turn(j)
         turn_values()
-        for j in range(4):
-            quantise_weights(j)
-            values(j)
-            if j % 2 == 1:
-                normaliser(j // 2)
+        for h in range(2):
+            scale_and_turn(2 * h)
+            turn_and_scale(2 * h + 1)
+        for h in range(2):
+            quantise_weights(2 * h, 2)
+            values(2 * h)
+            values(2 * h + 1)
+            normaliser(h)
         scatter(0)
         scatter(1)
         nc.sync.dma_start(out, window[:])

@@ -18,9 +18,10 @@ EXP = mybir.ActivationFunctionType.Exp
 MULT = mybir.AluOpType.mult
 ADD = mybir.AluOpType.add
 MIN = mybir.AluOpType.min
+MAX = mybir.AluOpType.max
 X = mybir.AxisListType.X
-H = T // 2
 BANK = 512
+LAST = P - 1
 
 
 def tile_attend_x_router_ks_kernel(tc, xq, kT, vT, ks, vs, offs, qoffs, out):
@@ -28,154 +29,130 @@ def tile_attend_x_router_ks_kernel(tc, xq, kT, vT, ks, vs, offs, qoffs, out):
     with ExitStack() as ctx:
         lists = ctx.enter_context(tc.tile_pool(name="lists", bufs=1))
         keep = ctx.enter_context(tc.tile_pool(name="keep", bufs=1))
+        slots = lists.tile([P, N // 16], U16, name="slots")
+        qlist = lists.tile([P, NQ // 16], U16, name="qlist")
+        ident = keep.tile([P, P], F32, name="ident")
+        make_identity(nc, ident[:])
+        ksw = keep.tile([P, T], F32, name="ksw", tag="ksw")
+        vsw = keep.tile([P, T], F32, name="vsw", tag="vsw")
+        nc.vector.memset(vsw[0:LAST, :], 0.0)
+        nc.vector.memset(ksw[0:LAST, :], 0.0)
+
+        kview = kT.rearrange("(p t) w -> p t w", t=4)
+        qview = xq.rearrange("(p t) w -> p t w", t=4)
+        nc.sync.dma_start(slots[:], offs)
+        nc.sync.dma_start(vsw[LAST:P, :], vs[0:1, :])
+        nc.sync.dma_start(ksw[LAST:P, :], ks[0:1, :])
+        kpl = [keep.tile([P, T], F32, name="kplane%d" % t, tag="kplane%d" % t) for t in range(4)]
+        qpl = [keep.tile([P, T], F32, name="qplane%d" % t, tag="qplane%d" % t) for t in range(4)]
+        vraw = keep.tile([P, T], F32, name="vraw")
+        nc.sync.dma_start(kpl[0][:], kview[:, 0, :])
+        nc.sync.dma_start(kpl[1][:], kview[:, 1, :])
+        nc.sync.dma_start(qlist[:], qoffs)
+        for t in (2, 3):
+            nc.sync.dma_start(kpl[t][:], kview[:, t, :])
+        for t in range(4):
+            nc.sync.dma_start(qpl[t][:], qview[:, t, :])
+        nc.sync.dma_start(vraw[:], vT)
+
+        def gather(engine, dst, src):
+            if engine == "s":
+                nc.scalar.activation(dst, src, COPY)
+            else:
+                nc.vector.tensor_copy(dst, src)
+
         banks = ctx.enter_context(tc.psum_pool(name="banks", bufs=1))
         ps = banks.tile([P, 8 * BANK], F32, name="ps")
 
         def bank(b, n=1):
             return ps[:, b * BANK : (b + n) * BANK]
 
-        slots = lists.tile([P, N // 16], U16, name="slots")
-        qlist = lists.tile([P, NQ // 16], U16, name="qlist")
-        ksw = keep.tile([P, T], F32, name="ksw", tag="ksw")
-        vsw = keep.tile([P, T], F32, name="vsw")
-        warm = keep.tile([P, 1], F32, name="warm")
-        nc.vector.memset(warm[:], 0.0)
-        nc.vector.memset(ksw[:], 0.0)
-        nc.vector.memset(vsw[:], 0.0)
-        nc.scalar.activation(warm[:], warm[:], EXP)
-        ident = keep.tile([P, P], F32, name="ident")
-        make_identity(nc, ident[:])
-
-        kview = kT.rearrange("(p t) w -> p t w", t=4)
-        qview = xq.rearrange("(p t) w -> p t w", t=4)
-        raw = {}
-        pair = {}
-        for key in ("k0", "k1"):
-            raw[key] = keep.tile([P, 2, T], F32, name="raw_" + key, tag="raw_" + key)
-            pair[key] = keep.tile([P, 2 * T], BF16, name="pair_" + key, tag="pair_" + key, align_bytes=64)
-
-        def load_pair(key, view, e, lo, hi):
-            nc.sync.dma_start(raw[key][:, :, lo:hi], view[:, 2 * e : 2 * e + 2, lo:hi])
-
-        load_pair("k0", kview, 0, 0, 768)
-        nc.sync.dma_start(slots[:], offs)
-        nc.sync.dma_start(ksw[0:1, :], ks[0:1, :])
-        load_pair("k0", kview, 0, 768, 1792)
-        nc.sync.dma_start(vsw[0:1, :], vs[0:1, :])
-        load_pair("k0", kview, 0, 1792, 2048)
-        nc.sync.dma_start(qlist[:], qoffs)
-        load_pair("k1", kview, 1, 0, H)
-        load_pair("k1", kview, 1, H, T)
-        qpl = {}
-        for t in range(4):
-            qpl[t] = keep.tile([P, T], F32, name="qplane%d" % t)
-            nc.sync.dma_start(qpl[t][:], qview[:, t, :])
-        vraw = keep.tile([P, T], F32, name="vraw")
-        nc.sync.dma_start(vraw[:], vT)
-
         ksg = keep.tile([P, N], F32, name="ksg")
-        nc.vector.tensor_copy(ksg[:], ksw[:].indirect(slots[:]))
-        window = keep.tile([P, T], F32, name="window", tag="ksw")
-        for i in range(8):
-            nc.gpsimd.memset(window[:, i * 256 : (i + 1) * 256], 0.0)
-        vsg = keep.tile([P, N], F32, name="vsg")
-        nc.vector.tensor_copy(vsg[:], vsw[:].indirect(slots[:]))
 
+        def gather_keys(t):
+            for g, eng in enumerate("vs"):
+                gather(eng, kg[g][:, t, :], kpl[t][:].indirect(slots[:, g * 32 : (g + 1) * 32]))
+
+        vsg = keep.tile([P, N], F32, name="vsg")
+        gather("v", ksg[:], ksw[:].indirect(slots[:]))
+        gather("s", vsg[:], vsw[:].indirect(slots[:]))
+        kg = [keep.tile([P, 4, 512], BF16, name="kg0", tag="ksw"), keep.tile([P, 4, 512], BF16, name="kg1")]
+        window = keep.tile([P, T], F32, name="window", tag="vsw")
+        nc.gpsimd.memset(window[:], 0.0)
+        for t in range(4):
+            gather_keys(t)
+
+        kx = keep.tile([P, 4 * N], BF16, name="kx", align_bytes=64)
+        qx = keep.tile([P, 4 * NQ], BF16, name="qx", align_bytes=64)
+        kc = keep.tile([P, N], U32, name="kc", align_bytes=64)
+        ksc = keep.tile([P, N], U8, name="ksc", align_bytes=64)
+        for g in range(2):
+            nc.vector.tensor_copy(kx[:, g * 2048 : (g + 1) * 2048].rearrange("p (n t) -> p n t", t=4), kg[g][:].rearrange("p t n -> p n t"))
+        for g in range(2):
+            cols = slice(g * 512, (g + 1) * 512)
+            nc.vector.quantize_mx(out=kc[:, cols].bitcast(FP8X4), scales=ksc[:, cols], in_=kx[:, g * 2048 : (g + 1) * 2048])
+
+        ks_col = keep.tile([P, 8], F32, name="ks_col", tag="kplane1")
+        vs_col = keep.tile([P, 8], F32, name="vs_col", tag="kplane0")
+        ks_row = keep.tile([P, N], F32, name="ks_row", tag="kplane2")
+        vs_row = keep.tile([P, N], F32, name="vs_row", tag="kplane3")
         for g in range(2):
             for i in range(4):
                 c = 4 * g + i
                 nc.tensor.transpose(bank(g)[:, i * P : (i + 1) * P], ksg[:, c * P : (c + 1) * P], ident[:])
+            nc.vector.tensor_copy(ks_col[:, 4 * g : 4 * g + 4], bank(g)[:, LAST:BANK:P])
         for g in range(2):
             for t in range(4):
                 nc.tensor.transpose(bank(2 + g)[:, t * P : (t + 1) * P], vsg[:, g * 512 + t : (g + 1) * 512 : 4], ident[:])
-
-        kx = keep.tile([P, 4 * N], BF16, name="kx", align_bytes=64)
-        qx = keep.tile([P, 4 * NQ], BF16, name="qx", align_bytes=64)
-
-        def cast(key, lo, hi, engine):
-            dst = pair[key][:].rearrange("p (w e) -> p w e", e=2)[:, lo:hi, :]
-            src = raw[key][:, :, lo:hi].rearrange("p e w -> p w e")
-            if engine == "s":
-                nc.scalar.activation(dst, src, COPY)
-            else:
-                nc.vector.tensor_copy(dst, src)
-
-        kg = keep.tile([P, 2, N], U32, name="kg")
-
-        def gather_pair(key, u):
-            nc.vector.tensor_copy(kg[:, u, :], pair[key][:].bitcast(U32).indirect(slots[:]))
-
-        cast("k0", 0, 768, "s")
-        cast("k0", 768, 1792, "s")
-        cast("k0", 1792, 2048, "v")
-        gather_pair("k0", 0)
-        cast("k1", 0, H, "s")
-        cast("k1", H, 1536, "s")
-        cast("k1", 1536, T, "v")
-        gather_pair("k1", 1)
-        kc = keep.tile([P, N], U32, name="kc", align_bytes=64)
-        ksc = keep.tile([P, N], U8, name="ksc", align_bytes=64)
-        qg = keep.tile([P, 2, NQ], BF16, name="qg")
-        for t in range(2):
-            nc.vector.tensor_copy(qg[:, t, :], qpl[t][:].indirect(qlist[:]))
-        for g in range(2):
-            cols = slice(g * 512, (g + 1) * 512)
-            words = kx[:].bitcast(U32).rearrange("p (n u) -> p n u", u=2)
-            nc.scalar.copy(words[:, cols, :], kg[:, :, cols].rearrange("p u n -> p n u"))
-            nc.vector.quantize_mx(out=kc[:, cols].bitcast(FP8X4), scales=ksc[:, cols], in_=kx[:, g * 2048 : (g + 1) * 2048])
-        nc.scalar.copy(qx[:].rearrange("p (n f) -> p n f", f=4)[:, :, 0:2], qg[:].rearrange("p t n -> p n t"))
-
-        scales = keep.tile([P, 2 * N + 16], F32, name="scales", tag="pair_k1", align_bytes=64)
-        nks_row = scales[:, 0:N].rearrange("p (g n) -> p g n", g=2)
-        vs_row = scales[:, N : 2 * N].rearrange("p (g n) -> p g n", g=2)
-        nks_col = scales[:, 2 * N : 2 * N + 8]
-        vs_col = scales[:, 2 * N + 8 : 2 * N + 16]
-        for g in range(2):
-            nc.vector.tensor_scalar(nks_col[:, 4 * g : 4 * g + 4], bank(g)[:, 0:BANK:P], -1.0, None, MULT)
-            nc.vector.tensor_copy(vs_col[:, 4 * g : 4 * g + 4], bank(2 + g)[:, 0:BANK:P])
+            nc.vector.tensor_copy(vs_col[:, 4 * g : 4 * g + 4], bank(2 + g)[:, LAST:BANK:P])
         for g in range(2):
             for i in range(4):
                 c = 4 * g + i
-                nc.tensor.transpose(bank(4 + g)[:, i * P : (i + 1) * P], nks_col[:, c : c + 1].to_broadcast([P, P]), ident[:])
-            nc.scalar.copy(nks_row[:, g, :].rearrange("p (u s e) -> p u s e", u=2, e=2), bank(4 + g).rearrange("p (s u e) -> p u s e", u=2, e=2))
+                nc.tensor.transpose(bank(4 + g)[:, i * P : (i + 1) * P], ks_col[:, c : c + 1].to_broadcast([P, P]), ident[:])
+            nc.scalar.copy(ks_row[:, g * BANK : (g + 1) * BANK], bank(4 + g))
         for g in range(2):
             for t in range(4):
                 c = 4 * g + t
                 nc.tensor.transpose(bank(6 + g)[:, t * P : (t + 1) * P], vs_col[:, c : c + 1].to_broadcast([P, P]), ident[:])
-            nc.scalar.copy(vs_row[:, g, :].rearrange("p (u s e) -> p u s e", u=2, e=2), bank(6 + g).rearrange("p (u e s) -> p u s e", u=2, e=2))
+            nc.scalar.copy(vs_row[:, g * BANK : (g + 1) * BANK].rearrange("p (u s e) -> p u s e", u=2, e=2), bank(6 + g).rearrange("p (u e s) -> p u s e", u=2, e=2))
 
+        qg = keep.tile([P, 4, NQ], BF16, name="qg")
         qc = keep.tile([P, NQ], U32, name="qc", align_bytes=64)
         qsc = keep.tile([P, NQ], U8, name="qsc", align_bytes=64)
+        for t in range(2):
+            gather("s", qg[:, t, :], qpl[t][:].indirect(qlist[:]))
+        qwords = qx[:].rearrange("p (n t) -> p n t", t=4)
+        nc.vector.tensor_copy(qwords[:, :, 0:2], qg[:, 0:2, :].rearrange("p t n -> p n t"))
+        gather("v", qwords[:, :, 2], qpl[2][:].indirect(qlist[:]))
+        for j in range(4):
+            gather("s", qg[:, 3, j * P : (j + 1) * P], qpl[3][:].indirect(qlist[:, j * 8 : (j + 1) * 8]))
 
-        def gather_q(t, lo, hi):
-            dst = qx[:].rearrange("p (n f) -> p n f", f=4)[:, lo:hi, t]
-            nc.vector.tensor_copy(dst, qpl[t][:].indirect(qlist[:, lo // 16 : hi // 16]))
+        def weave_q(j):
+            nc.vector.tensor_copy(qwords[:, j * P : (j + 1) * P, 3], qg[:, 3, j * P : (j + 1) * P])
 
-        def quantise_q(h):
-            nc.vector.quantize_mx(
-                out=qc[:, h * 256 : (h + 1) * 256].bitcast(FP8X4),
-                scales=qsc[:, h * 256 : (h + 1) * 256],
-                in_=qx[:, h * 1024 : (h + 1) * 1024],
-            )
+        def quantise_q(j):
+            cols = slice(j * P, (j + 1) * P)
+            nc.vector.quantize_mx(out=qc[:, cols].bitcast(FP8X4), scales=qsc[:, cols], in_=qx[:, j * 512 : (j + 1) * 512])
 
-        gather_q(2, 0, 512)
-        for h in range(2):
-            gather_q(3, h * 256, (h + 1) * 256)
-            quantise_q(h)
+        weave_q(0)
+        for j in range(4):
+            if j < 3:
+                weave_q(j + 1)
+            quantise_q(j)
 
         nm = keep.tile([P, 4], F32, name="nm")
         total = keep.tile([P, 4], F32, name="total")
         y_sb = keep.tile([P, NQ], F32, name="y_sb")
         rl_sb = keep.tile([P, NQ], F32, name="rl_sb")
         rl = keep.tile([P, 4], F32, name="rl")
-        a_all = keep.tile([P, 4, N], F32, name="a_all", tag="raw_k0")
+        a_all = keep.tile([P, 4, N], F32, name="a_all")
         half = keep.tile([P, 4], F32, name="half")
-        at = keep.tile([P, 8, NQ], F32, name="at", tag="raw_k1")
+        at = keep.tile([P, 8, NQ], F32, name="at")
         p_all = keep.tile([P, 4, N], F32, name="p_all")
         wx = keep.tile([P, 4, N], BF16, name="wx", align_bytes=64)
         wc = keep.tile([P, 4, 2 * P], U32, name="wc", align_bytes=64)
         wsc = keep.tile([P, 4, 2 * P], U8, name="wsc", align_bytes=64)
-        wq = keep.tile([P, 2, N], BF16, name="wq")
+        wq = keep.tile([P, 4, N], BF16, name="wq")
         A_BANK = {1: 0, 2: 2, 3: 4}
         BY_WORDS = (0, 2)
         P_BANK = {0: 6, 1: 0, 2: 6, 3: 2}
@@ -184,11 +161,14 @@ def tile_attend_x_router_ks_kernel(tc, xq, kT, vT, ks, vs, offs, qoffs, out):
         def mx(dst, lhs, lhs_scale, rhs, rhs_scale, start=True, stop=True):
             nc.tensor.matmul_mx(out=dst, lhsT=lhs.bitcast(FP8X4), lhsT_scale=lhs_scale, rhs=rhs.bitcast(FP8X4), rhs_scale=rhs_scale, start=start, stop=stop)
 
+        def dealt_views(j):
+            if j in BY_WORDS:
+                return "p (u s e) -> p u s e", "p (s u e) -> p u s e", dict(u=2, e=2)
+            return "p (t s) -> p t s", "p (s t) -> p t s", dict(t=4)
+
         def dealt(j, g, b):
-            dst = a_all[:, j, g * BANK : (g + 1) * BANK]
-            if j not in BY_WORDS:
-                return dst.rearrange("p (t s) -> p t s", t=4), b.rearrange("p (s t) -> p t s", t=4)
-            return dst.rearrange("p (u s e) -> p u s e", u=2, e=2), b.rearrange("p (s u e) -> p u s e", u=2, e=2)
+            to, frm, sizes = dealt_views(j)
+            return a_all[:, j, g * BANK : (g + 1) * BANK].rearrange(to, **sizes), b.rearrange(frm, **sizes)
 
         def turn_and_scale(j):
             for g in range(2):
@@ -204,22 +184,25 @@ def tile_attend_x_router_ks_kernel(tc, xq, kT, vT, ks, vs, offs, qoffs, out):
                 )
 
         def scale_and_turn(j):
-            nc.gpsimd.tensor_tensor(wq[:, j // 2, :], p_all[:, j, :], vs_row.rearrange("p g n -> p (g n)"), MULT)
+            nc.gpsimd.tensor_tensor(wq[:, j, :], p_all[:, j, :], vs_row[:], MULT)
             b = bank(P_BANK[j])
-            words = wq[:, j // 2, :].bitcast(F32)
+            words = wq[:, j, :].bitcast(F32)
             for c in range(4):
                 nc.tensor.transpose(b[:, c * P : (c + 1) * P], words[:, c * P : (c + 1) * P], ident[:])
             nc.scalar.copy(wx[:, j, :].bitcast(F32).rearrange("p (g q u) -> p g q u", g=2, u=2), b.rearrange("p (g u q) -> p g q u", g=2, u=2))
 
-        def scores_by_query():
+        def scores_by_query(j, b0):
+            q_cols = slice(j * P, (j + 1) * P)
             for g in range(2):
                 k_cols = slice(g * 512, (g + 1) * 512)
-                mx(bank(g), qc[:, 0:P], qsc[:, 0:P], kc[:, k_cols], ksc[:, k_cols])
+                mx(bank(b0 + g), qc[:, q_cols], qsc[:, q_cols], kc[:, k_cols], ksc[:, k_cols])
 
-        def scale_by_query():
+        def scale_by_query(j, b0):
+            to, frm, sizes = dealt_views(j)
             for g in range(2):
-                dst, src = dealt(0, g, bank(g))
-                nc.vector.tensor_tensor(dst, src, nks_row[:, g, :].rearrange("p (u s e) -> p u s e", u=2, e=2), MULT)
+                dst, src = dealt(j, g, bank(b0 + g))
+                nc.vector.tensor_tensor(dst, src, ks_row[:, g * BANK : (g + 1) * BANK].rearrange(frm, **sizes), MULT)
+            nc.vector.tensor_reduce(nm[:, j : j + 1], a_all[:, j, :], X, MAX, negate=True)
 
         def scores_by_slot(j0, groups, b0):
             width = groups * P
@@ -231,24 +214,21 @@ def tile_attend_x_router_ks_kernel(tc, xq, kT, vT, ks, vs, offs, qoffs, out):
                     mx(bank(b0 + n)[:, i * width : (i + 1) * width], kc[:, k_cols], ksc[:, k_cols], qc[:, q_cols], qsc[:, q_cols])
                 for i in range(per):
                     c = per * n + i
-                    nc.scalar.activation(at[:, c, q_cols], bank(b0 + n)[:, i * width : (i + 1) * width], COPY, scale=nks_col[:, c : c + 1])
+                    nc.scalar.activation(at[:, c, q_cols], bank(b0 + n)[:, i * width : (i + 1) * width], COPY, scale=ks_col[:, c : c + 1])
 
         def turn_scores(j):
             for c in range(8):
                 nc.tensor.transpose(bank(A_BANK[j], 2)[:, c * P : (c + 1) * P], at[:, c, j * P : (j + 1) * P], ident[:])
 
         def stabiliser(j):
-            if j == 0:
-                nc.vector.tensor_reduce(nm[:, 0:1], a_all[:, 0, :], X, MIN)
-                return
             for g in range(2):
                 dst, src = dealt(j, g, bank(A_BANK[j] + g))
                 first = None if g == 0 else half[:, j : j + 1]
                 least = half[:, j : j + 1] if g == 0 else nm[:, j : j + 1]
-                nc.vector.tensor_scalar(dst, src, 1.0, first, MULT, MIN, accum_out=least)
+                nc.vector.tensor_scalar(dst, src, -1.0, first, MULT, MIN, accum_out=least)
 
-        def weights(j):
-            nc.scalar.activation(p_all[:, j, :], a_all[:, j, :], EXP, bias=nm[:, j : j + 1], scale=-1.0, accum_out=total[:, j : j + 1])
+        def weights(j, sign):
+            nc.scalar.activation(p_all[:, j, :], a_all[:, j, :], EXP, bias=nm[:, j : j + 1], scale=sign, accum_out=total[:, j : j + 1])
 
         def quantise_weights(j, n):
             flat = "p j n -> p (j n)"
@@ -269,19 +249,23 @@ def tile_attend_x_router_ks_kernel(tc, xq, kT, vT, ks, vs, offs, qoffs, out):
                 nc.tensor.transpose(dst[:, i * P : (i + 1) * P], rl[:, c : c + 1].to_broadcast([P, P]), ident[:])
             nc.scalar.copy(rl_sb[:, h * 256 : (h + 1) * 256], dst)
 
-        def scatter(h):
+        def scatter_vector(h):
             cols = slice(h * 256, (h + 1) * 256)
             nc.scalar.copy(y_sb[:, cols], bank(Y_BANK[h])[:, 0:256])
             nc.vector.tensor_tensor(window[:].indirect(qlist[:, h * 16 : (h + 1) * 16]), y_sb[:, cols], rl_sb[:, cols], MULT)
+
+        def scatter_scalar(h):
+            cols = slice(h * 256, (h + 1) * 256)
+            nc.vector.tensor_tensor(y_sb[:, cols], bank(Y_BANK[h])[:, 0:256], rl_sb[:, cols], MULT)
+            nc.scalar.activation(window[:].indirect(qlist[:, h * 16 : (h + 1) * 16]), y_sb[:, cols], COPY)
 
         vg = keep.tile([P, N], BF16, name="vg")
         vx = keep.tile([P, N], BF16, name="vx", align_bytes=64)
         vc = keep.tile([P, 2 * DV], U32, name="vc", align_bytes=64)
         vsc = keep.tile([P, 2 * DV], U8, name="vsc", align_bytes=64)
 
-        def gather_values():
-            for g in range(2):
-                nc.vector.tensor_copy(vg[:, g * 512 : (g + 1) * 512], vraw[:].indirect(slots[:, g * 32 : (g + 1) * 32]))
+        def gather_values(g, eng):
+            gather(eng, vg[:, g * 512 : (g + 1) * 512], vraw[:].indirect(slots[:, g * 32 : (g + 1) * 32]))
 
         def turn_values():
             words = vg[:].bitcast(F32)
@@ -289,29 +273,29 @@ def tile_attend_x_router_ks_kernel(tc, xq, kT, vT, ks, vs, offs, qoffs, out):
                 for u in range(2):
                     c = 2 * g + u
                     nc.tensor.transpose(bank(7)[:, c * P : (c + 1) * P], words[:, g * 256 + u : (g + 1) * 256 : 2], ident[:])
-            nc.scalar.copy(vx[:].bitcast(F32).rearrange("p (g e u) -> p g e u", g=2, u=2), bank(7).rearrange("p (g u e) -> p g e u", g=2, u=2))
+            nc.vector.tensor_copy(vx[:].bitcast(F32).rearrange("p (g e u) -> p g e u", g=2, u=2), bank(7).rearrange("p (g u e) -> p g e u", g=2, u=2))
             nc.vector.quantize_mx(out=vc[:].bitcast(FP8X4), scales=vsc[:], in_=vx[:])
 
-        scores_by_query()
+        scores_by_query(0, 0)
         scores_by_slot(1, 1, 2)
         scores_by_slot(2, 2, 4)
-        scale_by_query()
-        stabiliser(0)
-        weights(0)
+        scale_by_query(0, 0)
+        weights(0, 1.0)
         for j in (1, 2, 3):
             turn_scores(j)
             stabiliser(j)
-            weights(j)
-        gather_values()
+            weights(j, -1.0)
+        gather_values(0, "v")
+        gather_values(1, "v")
         turn_values()
         for h in range(2):
             scale_and_turn(2 * h)
             turn_and_scale(2 * h + 1)
-        for h in range(2):
+            normaliser(h)
             quantise_weights(2 * h, 2)
             values(2 * h)
             values(2 * h + 1)
-            normaliser(h)
-        scatter(0)
-        scatter(1)
+            if h == 0:
+                scatter_scalar(0)
+        scatter_vector(1)
         nc.sync.dma_start(out, window[:])

@@ -35,6 +35,9 @@ def tile_attend_x_router_ks_kernel(tc, xq, kT, vT, ks, vs, offs, qoffs, out):
         make_identity(nc, ident[:])
         ksw = keep.tile([P, T], F32, name="ksw", tag="ksw")
         vsw = keep.tile([P, T], F32, name="vsw", tag="vsw")
+        warm = keep.tile([P, 1], F32, name="warm")
+        nc.vector.memset(warm[:], 0.0)
+        nc.scalar.activation(warm[:], warm[:], EXP)
         nc.vector.memset(vsw[0:LAST, :], 0.0)
         nc.vector.memset(ksw[0:LAST, :], 0.0)
 

@@ -35,9 +35,6 @@ def tile_attend_x_router_ks_kernel(tc, xq, kT, vT, ks, vs, offs, qoffs, out):
         make_identity(nc, ident[:])
         ksw = keep.tile([P, T], F32, name="ksw", tag="ksw")
         vsw = keep.tile([P, T], F32, name="vsw", tag="vsw")
-        warm = keep.tile([P, 1], F32, name="warm")
-        nc.vector.memset(warm[:], 0.0)
-        nc.scalar.activation(warm[:], warm[:], EXP)
         nc.vector.memset(vsw[0:LAST, :], 0.0)
         nc.vector.memset(ksw[0:LAST, :], 0.0)
 
@@ -48,7 +45,7 @@ def tile_attend_x_router_ks_kernel(tc, xq, kT, vT, ks, vs, offs, qoffs, out):
         nc.sync.dma_start(ksw[LAST:P, :], ks[0:1, :])
         kpl = [keep.tile([P, T], F32, name="kplane%d" % t, tag="kplane%d" % t) for t in range(4)]
         qpl = [keep.tile([P, T], F32, name="qplane%d" % t, tag="qplane%d" % t) for t in range(4)]
-        vraw = keep.tile([P, T], F32, name="vraw")
+        vraw = keep.tile([P, T], F32, name="vraw", tag="vraw")
         nc.sync.dma_start(kpl[0][:], kview[:, 0, :])
         nc.sync.dma_start(kpl[1][:], kview[:, 1, :])
         nc.sync.dma_start(qlist[:], qoffs)
@@ -95,10 +92,8 @@ def tile_attend_x_router_ks_kernel(tc, xq, kT, vT, ks, vs, offs, qoffs, out):
             cols = slice(g * 512, (g + 1) * 512)
             nc.vector.quantize_mx(out=kc[:, cols].bitcast(FP8X4), scales=ksc[:, cols], in_=kx[:, g * 2048 : (g + 1) * 2048])
 
-        ks_col = keep.tile([P, 8], F32, name="ks_col", tag="kplane1")
-        vs_col = keep.tile([P, 8], F32, name="vs_col", tag="kplane0")
-        ks_row = keep.tile([P, N], F32, name="ks_row", tag="kplane2")
-        vs_row = keep.tile([P, N], F32, name="vs_row", tag="kplane3")
+        ks_col = keep.tile([P, 8], F32, name="ks_col", tag="kplane3")
+        vs_col = keep.tile([P, 8], F32, name="vs_col", tag="kplane2")
         for g in range(2):
             for i in range(4):
                 c = 4 * g + i
@@ -108,40 +103,33 @@ def tile_attend_x_router_ks_kernel(tc, xq, kT, vT, ks, vs, offs, qoffs, out):
             for t in range(4):
                 nc.tensor.transpose(bank(2 + g)[:, t * P : (t + 1) * P], vsg[:, g * 512 + t : (g + 1) * 512 : 4], ident[:])
             nc.vector.tensor_copy(vs_col[:, 4 * g : 4 * g + 4], bank(2 + g)[:, LAST:BANK:P])
+        qg = keep.tile([P, 3, NQ], BF16, name="qg")
+        qc = keep.tile([P, NQ], U32, name="qc", align_bytes=64)
+        qsc = keep.tile([P, NQ], U8, name="qsc", align_bytes=64)
+        for t in range(2):
+            gather("s", qg[:, t, :], qpl[t][:].indirect(qlist[:]))
+        ks_row = keep.tile([P, N], F32, name="ks_row", tag="qplane1")
+        vs_row = keep.tile([P, N], F32, name="vs_row", tag="qplane0")
         for g in range(2):
             for i in range(4):
                 c = 4 * g + i
                 nc.tensor.transpose(bank(4 + g)[:, i * P : (i + 1) * P], ks_col[:, c : c + 1].to_broadcast([P, P]), ident[:])
-            nc.scalar.copy(ks_row[:, g * BANK : (g + 1) * BANK], bank(4 + g))
+            nc.scalar.copy(ks_row[:, g * BANK : (g + 1) * BANK].rearrange("p (t s) -> p t s", t=4), bank(4 + g).rearrange("p (s t) -> p t s", t=4))
         for g in range(2):
             for t in range(4):
                 c = 4 * g + t
                 nc.tensor.transpose(bank(6 + g)[:, t * P : (t + 1) * P], vs_col[:, c : c + 1].to_broadcast([P, P]), ident[:])
             nc.scalar.copy(vs_row[:, g * BANK : (g + 1) * BANK].rearrange("p (u s e) -> p u s e", u=2, e=2), bank(6 + g).rearrange("p (u e s) -> p u s e", u=2, e=2))
 
-        qg = keep.tile([P, 4, NQ], BF16, name="qg")
-        qc = keep.tile([P, NQ], U32, name="qc", align_bytes=64)
-        qsc = keep.tile([P, NQ], U8, name="qsc", align_bytes=64)
-        for t in range(2):
-            gather("s", qg[:, t, :], qpl[t][:].indirect(qlist[:]))
         qwords = qx[:].rearrange("p (n t) -> p n t", t=4)
         nc.vector.tensor_copy(qwords[:, :, 0:2], qg[:, 0:2, :].rearrange("p t n -> p n t"))
         gather("v", qwords[:, :, 2], qpl[2][:].indirect(qlist[:]))
-        for j in range(4):
-            gather("s", qg[:, 3, j * P : (j + 1) * P], qpl[3][:].indirect(qlist[:, j * 8 : (j + 1) * 8]))
-
-        def weave_q(j):
-            nc.vector.tensor_copy(qwords[:, j * P : (j + 1) * P, 3], qg[:, 3, j * P : (j + 1) * P])
-
-        def quantise_q(j):
-            cols = slice(j * P, (j + 1) * P)
-            nc.vector.quantize_mx(out=qc[:, cols].bitcast(FP8X4), scales=qsc[:, cols], in_=qx[:, j * 512 : (j + 1) * 512])
-
-        weave_q(0)
-        for j in range(4):
-            if j < 3:
-                weave_q(j + 1)
-            quantise_q(j)
+        gather("v", qwords[:, 0:256, 3], qpl[3][:].indirect(qlist[:, 0:16]))
+        gather("s", qg[:, 2, 0:256], qpl[3][:].indirect(qlist[:, 16:32]))
+        nc.vector.tensor_copy(qwords[:, 256:512, 3], qg[:, 2, 0:256])
+        for h in range(2):
+            cols = slice(h * 256, (h + 1) * 256)
+            nc.vector.quantize_mx(out=qc[:, cols].bitcast(FP8X4), scales=qsc[:, cols], in_=qx[:, h * 1024 : (h + 1) * 1024])
 
         nm = keep.tile([P, 4], F32, name="nm")
         total = keep.tile([P, 4], F32, name="total")
@@ -149,17 +137,17 @@ def tile_attend_x_router_ks_kernel(tc, xq, kT, vT, ks, vs, offs, qoffs, out):
         rl_sb = keep.tile([P, NQ], F32, name="rl_sb")
         rl = keep.tile([P, 4], F32, name="rl")
         a_all = keep.tile([P, 4, N], F32, name="a_all")
-        half = keep.tile([P, 4], F32, name="half")
-        at = keep.tile([P, 8, NQ], F32, name="at")
-        p_all = keep.tile([P, 4, N], F32, name="p_all")
+        half = {j: keep.tile([P, 1], F32, name="half%d" % j, tag="half%d" % j) for j in (2, 3)}
+        p_of = [keep.tile([P, N], F32, name="p%d" % j, tag="p%d" % j, align_bytes=64) for j in range(4)]
         wx = keep.tile([P, 4, N], BF16, name="wx", align_bytes=64)
         wc = keep.tile([P, 4, 2 * P], U32, name="wc", align_bytes=64)
         wsc = keep.tile([P, 4, 2 * P], U8, name="wsc", align_bytes=64)
-        wq = keep.tile([P, 4, N], BF16, name="wq")
-        A_BANK = {1: 0, 2: 2, 3: 4}
-        BY_WORDS = (0, 2)
-        P_BANK = {0: 6, 1: 0, 2: 6, 3: 2}
-        Y_BANK = (4, 0)
+        wq = keep.tile([P, 1, N], BF16, name="wq")
+        BY_WORDS = (0,)
+        P_BANK = {0: 3, 1: 6, 2: 0, 3: 4}
+        Y_BANK = (2, 6)
+        L_BANK = (7, 0)
+        V_BANK = 3
 
         def mx(dst, lhs, lhs_scale, rhs, rhs_scale, start=True, stop=True):
             nc.tensor.matmul_mx(out=dst, lhsT=lhs.bitcast(FP8X4), lhsT_scale=lhs_scale, rhs=rhs.bitcast(FP8X4), rhs_scale=rhs_scale, start=start, stop=stop)
@@ -173,12 +161,12 @@ def tile_attend_x_router_ks_kernel(tc, xq, kT, vT, ks, vs, offs, qoffs, out):
             to, frm, sizes = dealt_views(j)
             return a_all[:, j, g * BANK : (g + 1) * BANK].rearrange(to, **sizes), b.rearrange(frm, **sizes)
 
-        def turn_and_scale(j):
-            for g in range(2):
+        def turn_and_scale(j, halves=(0, 1)):
+            for g in halves:
                 b = bank(P_BANK[j] + g)
                 for t in range(4):
                     c = 4 * g + t
-                    nc.tensor.transpose(b[:, t * P : (t + 1) * P], p_all[:, j, c * P : (c + 1) * P], ident[:])
+                    nc.tensor.transpose(b[:, t * P : (t + 1) * P], p_of[j][:, c * P : (c + 1) * P], ident[:])
                 nc.vector.tensor_tensor(
                     wx[:, j, g * BANK : (g + 1) * BANK].rearrange("p (q t) -> p q t", t=4),
                     b.rearrange("p (t q) -> p q t", t=4),
@@ -186,119 +174,114 @@ def tile_attend_x_router_ks_kernel(tc, xq, kT, vT, ks, vs, offs, qoffs, out):
                     MULT,
                 )
 
-        def scale_and_turn(j):
-            nc.gpsimd.tensor_tensor(wq[:, j, :], p_all[:, j, :], vs_row[:], MULT)
+        def scale_and_turn(j, copy):
             b = bank(P_BANK[j])
-            words = wq[:, j, :].bitcast(F32)
-            for c in range(4):
-                nc.tensor.transpose(b[:, c * P : (c + 1) * P], words[:, c * P : (c + 1) * P], ident[:])
-            nc.scalar.copy(wx[:, j, :].bitcast(F32).rearrange("p (g q u) -> p g q u", g=2, u=2), b.rearrange("p (g u q) -> p g q u", g=2, u=2))
+            words = wq[:, j // 2, :].bitcast(F32)
+            for g in range(2):
+                cols = slice(g * BANK, (g + 1) * BANK)
+                nc.gpsimd.tensor_tensor(wq[:, j // 2, cols], p_of[j][:, cols], vs_row[:, cols], MULT)
+                for c in (2 * g, 2 * g + 1):
+                    nc.tensor.transpose(b[:, c * P : (c + 1) * P], words[:, c * P : (c + 1) * P], ident[:])
+            copy(wx[:, j, :].bitcast(F32).rearrange("p (g q u) -> p g q u", g=2, u=2), b.rearrange("p (g u q) -> p g q u", g=2, u=2))
 
-        def scores_by_query(j, b0):
+        def scores_by_query(j):
             q_cols = slice(j * P, (j + 1) * P)
             for g in range(2):
                 k_cols = slice(g * 512, (g + 1) * 512)
-                mx(bank(b0 + g), qc[:, q_cols], qsc[:, q_cols], kc[:, k_cols], ksc[:, k_cols])
+                mx(bank(2 * j + g), qc[:, q_cols], qsc[:, q_cols], kc[:, k_cols], ksc[:, k_cols])
 
-        def scale_by_query(j, b0):
+        def scale_by_query(j):
             to, frm, sizes = dealt_views(j)
             for g in range(2):
-                dst, src = dealt(j, g, bank(b0 + g))
-                nc.vector.tensor_tensor(dst, src, ks_row[:, g * BANK : (g + 1) * BANK].rearrange(frm, **sizes), MULT)
-            nc.vector.tensor_reduce(nm[:, j : j + 1], a_all[:, j, :], X, MAX, negate=True)
+                dst, src = dealt(j, g, bank(2 * j + g))
+                nc.vector.tensor_tensor(dst, src, ks_row[:, g * BANK : (g + 1) * BANK].rearrange("p (u e s) -> p u s e" if j in BY_WORDS else to, **sizes), MULT)
 
-        def scores_by_slot(j0, groups, b0):
-            width = groups * P
-            q_cols = slice(j0 * P, j0 * P + width)
-            per = BANK // width
-            for n in range(8 // per):
-                for i in range(per):
-                    k_cols = slice((per * n + i) * P, (per * n + i + 1) * P)
-                    mx(bank(b0 + n)[:, i * width : (i + 1) * width], kc[:, k_cols], ksc[:, k_cols], qc[:, q_cols], qsc[:, q_cols])
-                for i in range(per):
-                    c = per * n + i
-                    nc.scalar.activation(at[:, c, q_cols], bank(b0 + n)[:, i * width : (i + 1) * width], COPY, scale=ks_col[:, c : c + 1])
+        def scores_by_slot(n):
+            for c in (2 * n, 2 * n + 1):
+                k_cols = slice(c * P, (c + 1) * P)
+                mx(bank(4 + n)[:, c % 2 * 256 : (c % 2 + 1) * 256], kc[:, k_cols], ksc[:, k_cols], qc[:, 256:512], qsc[:, 256:512])
+            for c in (2 * n, 2 * n + 1):
+                nc.scalar.activation(at[:, c, :], bank(4 + n)[:, c % 2 * 256 : (c % 2 + 1) * 256], COPY, scale=ks_col[:, c : c + 1])
 
-        def turn_scores(j):
-            for c in range(8):
-                nc.tensor.transpose(bank(A_BANK[j], 2)[:, c * P : (c + 1) * P], at[:, c, j * P : (j + 1) * P], ident[:])
-
-        def stabiliser(j):
-            for g in range(2):
-                dst, src = dealt(j, g, bank(A_BANK[j] + g))
-                first = None if g == 0 else half[:, j : j + 1]
-                least = half[:, j : j + 1] if g == 0 else nm[:, j : j + 1]
-                nc.vector.tensor_scalar(dst, src, -1.0, first, MULT, MIN, accum_out=least)
+        def stabiliser(j, g):
+            b = bank(2 * g + j - 2)
+            for i in range(4):
+                nc.tensor.transpose(b[:, i * P : (i + 1) * P], at[:, 4 * g + i, (j - 2) * P : (j - 1) * P], ident[:])
+            dst, src = dealt(j, g, b)
+            first = None if g == 0 else half[j][:]
+            least = half[j][:] if g == 0 else nm[:, j : j + 1]
+            nc.vector.tensor_scalar(dst, src, -1.0, first, MULT, MIN, accum_out=least)
 
         def weights(j, sign):
-            nc.scalar.activation(p_all[:, j, :], a_all[:, j, :], EXP, bias=nm[:, j : j + 1], scale=sign, accum_out=total[:, j : j + 1])
+            nc.scalar.activation(p_of[j][:], a_all[:, j, :], EXP, bias=nm[:, j : j + 1], scale=sign, accum_out=total[:, j : j + 1])
 
-        def quantise_weights(j, n):
+        def quantise_weights(h):
             flat = "p j n -> p (j n)"
-            js = slice(j, j + n)
+            js = slice(2 * h, 2 * h + 2)
             nc.vector.quantize_mx(out=wc[:, js, :].rearrange(flat).bitcast(FP8X4), scales=wsc[:, js, :].rearrange(flat), in_=wx[:, js, :].rearrange(flat))
 
-        def values(j):
-            for g in range(2):
-                cols = slice(g * P, (g + 1) * P)
-                mx(bank(Y_BANK[j // 2])[:, j % 2 * P : (j % 2 + 1) * P], vc[:, cols], vsc[:, cols], wc[:, j, cols], wsc[:, j, cols], g == 0, g == 1)
+        def values(h):
+            for i in range(2):
+                for g in range(2):
+                    cols = slice(g * P, (g + 1) * P)
+                    mx(bank(Y_BANK[h])[:, i * P : (i + 1) * P], vc[:, cols], vsc[:, cols], wc[:, 2 * h + i, cols], wsc[:, 2 * h + i, cols], g == 0, g == 1)
 
         def normaliser(h):
             js = slice(2 * h, 2 * h + 2)
             nc.vector.reciprocal(rl[:, js], total[:, js])
-            dst = bank(5 + 2 * h)[:, 0:256]
+            dst = bank(L_BANK[h])[:, 0:256]
             for i in range(2):
                 c = 2 * h + i
                 nc.tensor.transpose(dst[:, i * P : (i + 1) * P], rl[:, c : c + 1].to_broadcast([P, P]), ident[:])
             nc.scalar.copy(rl_sb[:, h * 256 : (h + 1) * 256], dst)
 
-        def scatter_vector(h):
-            cols = slice(h * 256, (h + 1) * 256)
-            nc.scalar.copy(y_sb[:, cols], bank(Y_BANK[h])[:, 0:256])
-            nc.vector.tensor_tensor(window[:].indirect(qlist[:, h * 16 : (h + 1) * 16]), y_sb[:, cols], rl_sb[:, cols], MULT)
-
-        def scatter_scalar(h):
+        def scatter(h, eng):
             cols = slice(h * 256, (h + 1) * 256)
             nc.vector.tensor_tensor(y_sb[:, cols], bank(Y_BANK[h])[:, 0:256], rl_sb[:, cols], MULT)
-            nc.scalar.activation(window[:].indirect(qlist[:, h * 16 : (h + 1) * 16]), y_sb[:, cols], COPY)
+            gather(eng, window[:].indirect(qlist[:, h * 16 : (h + 1) * 16]), y_sb[:, cols])
 
         vg = keep.tile([P, N], BF16, name="vg")
         vx = keep.tile([P, N], BF16, name="vx", align_bytes=64)
         vc = keep.tile([P, 2 * DV], U32, name="vc", align_bytes=64)
         vsc = keep.tile([P, 2 * DV], U8, name="vsc", align_bytes=64)
 
-        def gather_values(g, eng):
-            gather(eng, vg[:, g * 512 : (g + 1) * 512], vraw[:].indirect(slots[:, g * 32 : (g + 1) * 32]))
-
         def turn_values():
             words = vg[:].bitcast(F32)
             for g in range(2):
                 for u in range(2):
                     c = 2 * g + u
-                    nc.tensor.transpose(bank(7)[:, c * P : (c + 1) * P], words[:, g * 256 + u : (g + 1) * 256 : 2], ident[:])
-            nc.vector.tensor_copy(vx[:].bitcast(F32).rearrange("p (g e u) -> p g e u", g=2, u=2), bank(7).rearrange("p (g u e) -> p g e u", g=2, u=2))
+                    nc.tensor.transpose(bank(V_BANK)[:, c * P : (c + 1) * P], words[:, g * 256 + u : (g + 1) * 256 : 2], ident[:])
+            nc.vector.tensor_copy(vx[:].bitcast(F32).rearrange("p (g e u) -> p g e u", g=2, u=2), bank(V_BANK).rearrange("p (g u e) -> p g e u", g=2, u=2))
             nc.vector.quantize_mx(out=vc[:].bitcast(FP8X4), scales=vsc[:], in_=vx[:])
 
-        scores_by_query(0, 0)
-        scores_by_slot(1, 1, 2)
-        scores_by_slot(2, 2, 4)
-        scale_by_query(0, 0)
-        weights(0, 1.0)
-        for j in (1, 2, 3):
-            turn_scores(j)
-            stabiliser(j)
-            weights(j, -1.0)
-        gather_values(0, "v")
-        gather_values(1, "v")
+        gather("s", vg[:], vraw[:].indirect(slots[:]))
+        at = keep.tile([P, 8, 2 * P], F32, name="at", tag="vraw")
+        scores_by_query(0)
+        scores_by_query(1)
+        for n in range(4):
+            scores_by_slot(n)
+        for j in (0, 1):
+            scale_by_query(j)
+        for j in (0, 1):
+            nc.vector.tensor_reduce(nm[:, j : j + 1], a_all[:, j, :], X, MAX, negate=True)
+            weights(j, 1.0)
         turn_values()
-        for h in range(2):
-            scale_and_turn(2 * h)
-            turn_and_scale(2 * h + 1)
-            normaliser(h)
-            quantise_weights(2 * h, 2)
-            values(2 * h)
-            values(2 * h + 1)
-            if h == 0:
-                scatter_scalar(0)
-        scatter_vector(1)
+        for g in range(2):
+            for j in (2, 3):
+                stabiliser(j, g)
+        for j in (2, 3):
+            weights(j, -1.0)
+        turn_and_scale(1)
+        turn_and_scale(2, (0,))
+        scale_and_turn(0, nc.scalar.copy)
+        normaliser(0)
+        quantise_weights(0)
+        turn_and_scale(2, (1,))
+        values(0)
+        scatter(0, "s")
+        normaliser(1)
+        turn_and_scale(3)
+        quantise_weights(1)
+        values(1)
+        scatter(1, "v")
         nc.sync.dma_start(out, window[:])

@@ -22,6 +22,7 @@ MAX = mybir.AluOpType.max
 X = mybir.AxisListType.X
 BANK = 512
 LAST = P - 1
+SPLIT = 640
 
 
 def tile_attend_x_router_ks_kernel(tc, xq, kT, vT, ks, vs, offs, qoffs, out):
@@ -45,7 +46,7 @@ def tile_attend_x_router_ks_kernel(tc, xq, kT, vT, ks, vs, offs, qoffs, out):
         nc.sync.dma_start(ksw[LAST:P, :], ks[0:1, :])
         kpl = [keep.tile([P, T], F32, name="kplane%d" % t, tag="kplane%d" % t) for t in range(4)]
         qpl = [keep.tile([P, T], F32, name="qplane%d" % t, tag="qplane%d" % t) for t in range(4)]
-        vraw = keep.tile([P, T], F32, name="vraw", tag="vraw")
+        vlow = keep.tile([P, T - 512], F32, name="vlow", tag="vlow")
         nc.sync.dma_start(kpl[0][:], kview[:, 0, :])
         nc.sync.dma_start(kpl[1][:], kview[:, 1, :])
         nc.sync.dma_start(qlist[:], qoffs)
@@ -53,7 +54,7 @@ def tile_attend_x_router_ks_kernel(tc, xq, kT, vT, ks, vs, offs, qoffs, out):
             nc.sync.dma_start(kpl[t][:], kview[:, t, :])
         for t in range(4):
             nc.sync.dma_start(qpl[t][:], qview[:, t, :])
-        nc.sync.dma_start(vraw[:], vT)
+        nc.sync.dma_start(vlow[:], vT[:, 0 : T - 512])
 
         def gather(engine, dst, src):
             if engine == "s":
@@ -70,30 +71,24 @@ def tile_attend_x_router_ks_kernel(tc, xq, kT, vT, ks, vs, offs, qoffs, out):
         ksg = keep.tile([P, N], F32, name="ksg")
 
         def gather_keys(t):
-            for g, eng in enumerate("vs"):
-                gather(eng, kg[g][:, t, :], kpl[t][:].indirect(slots[:, g * 32 : (g + 1) * 32]))
+            gather("v", kg[0][:, t, :], kpl[t][:].indirect(slots[:, 0 : SPLIT // 16]))
+            gather("s", kg[1][:, t, :], kpl[t][:].indirect(slots[:, SPLIT // 16 : N // 16]))
 
         vsg = keep.tile([P, N], F32, name="vsg")
         gather("v", ksg[:], ksw[:].indirect(slots[:]))
         gather("s", vsg[:], vsw[:].indirect(slots[:]))
-        kg = [keep.tile([P, 4, 512], BF16, name="kg0", tag="ksw"), keep.tile([P, 4, 512], BF16, name="kg1")]
+        kg = [keep.tile([P, 4, SPLIT], BF16, name="kg0", tag="ksw"), keep.tile([P, 4, N - SPLIT], BF16, name="kg1")]
         window = keep.tile([P, T], F32, name="window", tag="vsw")
         nc.gpsimd.memset(window[:], 0.0)
         for t in range(4):
             gather_keys(t)
+        vhigh = keep.tile([P, T], F32, name="vhigh", tag="kplane0")
+        nc.gpsimd.memset(vhigh[:, 0:512], 0.0)
+        nc.sync.dma_start(vhigh[:, 512:T], vT[:, 512:T])
 
-        kx = keep.tile([P, 4 * N], BF16, name="kx", align_bytes=64)
-        qx = keep.tile([P, 4 * NQ], BF16, name="qx", align_bytes=64)
-        kc = keep.tile([P, N], U32, name="kc", align_bytes=64)
-        ksc = keep.tile([P, N], U8, name="ksc", align_bytes=64)
-        for g in range(2):
-            nc.vector.tensor_copy(kx[:, g * 2048 : (g + 1) * 2048].rearrange("p (n t) -> p n t", t=4), kg[g][:].rearrange("p t n -> p n t"))
-        for g in range(2):
-            cols = slice(g * 512, (g + 1) * 512)
-            nc.vector.quantize_mx(out=kc[:, cols].bitcast(FP8X4), scales=ksc[:, cols], in_=kx[:, g * 2048 : (g + 1) * 2048])
-
-        ks_col = keep.tile([P, 8], F32, name="ks_col", tag="kplane3")
-        vs_col = keep.tile([P, 8], F32, name="vs_col", tag="kplane2")
+        columns = keep.tile([P, 16], F32, name="columns", tag="kplane3")
+        ks_col = columns[:, 0:8]
+        vs_col = columns[:, 8:16]
         for g in range(2):
             for i in range(4):
                 c = 4 * g + i
@@ -103,13 +98,25 @@ def tile_attend_x_router_ks_kernel(tc, xq, kT, vT, ks, vs, offs, qoffs, out):
             for t in range(4):
                 nc.tensor.transpose(bank(2 + g)[:, t * P : (t + 1) * P], vsg[:, g * 512 + t : (g + 1) * 512 : 4], ident[:])
             nc.vector.tensor_copy(vs_col[:, 4 * g : 4 * g + 4], bank(2 + g)[:, LAST:BANK:P])
+        kx = keep.tile([P, 4 * N], BF16, name="kx", align_bytes=64)
+        qx = keep.tile([P, 4 * NQ], BF16, name="qx", align_bytes=64)
+        kc = keep.tile([P, N], U32, name="kc", align_bytes=64)
+        ksc = keep.tile([P, N], U8, name="ksc", align_bytes=64)
+        for g, (lo, hi) in enumerate(((0, SPLIT), (SPLIT, N))):
+            nc.vector.tensor_copy(kx[:, 4 * lo : 4 * hi].rearrange("p (n t) -> p n t", t=4), kg[g][:].rearrange("p t n -> p n t"))
+        for g in range(2):
+            cols = slice(g * 512, (g + 1) * 512)
+            nc.vector.quantize_mx(out=kc[:, cols].bitcast(FP8X4), scales=ksc[:, cols], in_=kx[:, g * 2048 : (g + 1) * 2048])
+
         qg = keep.tile([P, 3, NQ], BF16, name="qg")
         qc = keep.tile([P, NQ], U32, name="qc", align_bytes=64)
         qsc = keep.tile([P, NQ], U8, name="qsc", align_bytes=64)
-        for t in range(2):
-            gather("s", qg[:, t, :], qpl[t][:].indirect(qlist[:]))
-        ks_row = keep.tile([P, N], F32, name="ks_row", tag="qplane1")
-        vs_row = keep.tile([P, N], F32, name="vs_row", tag="qplane0")
+        gather("s", qg[:, 0, :], qpl[0][:].indirect(qlist[:]))
+        for h, eng in enumerate("sv"):
+            gather(eng, qg[:, 1, h * 256 : (h + 1) * 256], qpl[1][:].indirect(qlist[:, h * 16 : (h + 1) * 16]))
+        rows = keep.tile([P, 2 * N], F32, name="rows", tag="qplane1")
+        ks_row = rows[:, 0:N]
+        vs_row = rows[:, N : 2 * N]
         for g in range(2):
             for i in range(4):
                 c = 4 * g + i
@@ -145,9 +152,9 @@ def tile_attend_x_router_ks_kernel(tc, xq, kT, vT, ks, vs, offs, qoffs, out):
         wq = keep.tile([P, 1, N], BF16, name="wq")
         BY_WORDS = (0,)
         P_BANK = {0: 3, 1: 6, 2: 0, 3: 4}
-        Y_BANK = (2, 6)
+        Y_BANK = (6, 2)
         L_BANK = (7, 0)
-        V_BANK = 3
+        V_BANK = 5
 
         def mx(dst, lhs, lhs_scale, rhs, rhs_scale, start=True, stop=True):
             nc.tensor.matmul_mx(out=dst, lhsT=lhs.bitcast(FP8X4), lhsT_scale=lhs_scale, rhs=rhs.bitcast(FP8X4), rhs_scale=rhs_scale, start=start, stop=stop)
@@ -240,22 +247,20 @@ def tile_attend_x_router_ks_kernel(tc, xq, kT, vT, ks, vs, offs, qoffs, out):
             nc.vector.tensor_tensor(y_sb[:, cols], bank(Y_BANK[h])[:, 0:256], rl_sb[:, cols], MULT)
             gather(eng, window[:].indirect(qlist[:, h * 16 : (h + 1) * 16]), y_sb[:, cols])
 
-        vg = keep.tile([P, N], BF16, name="vg")
+        vg = {0: keep.tile([P, 512], BF16, name="vg0")}
         vx = keep.tile([P, N], BF16, name="vx", align_bytes=64)
-        vc = keep.tile([P, 2 * DV], U32, name="vc", align_bytes=64)
         vsc = keep.tile([P, 2 * DV], U8, name="vsc", align_bytes=64)
 
         def turn_values():
-            words = vg[:].bitcast(F32)
             for g in range(2):
+                words = vg[g][:].bitcast(F32)
                 for u in range(2):
                     c = 2 * g + u
-                    nc.tensor.transpose(bank(V_BANK)[:, c * P : (c + 1) * P], words[:, g * 256 + u : (g + 1) * 256 : 2], ident[:])
-            nc.vector.tensor_copy(vx[:].bitcast(F32).rearrange("p (g e u) -> p g e u", g=2, u=2), bank(V_BANK).rearrange("p (g u e) -> p g e u", g=2, u=2))
-            nc.vector.quantize_mx(out=vc[:].bitcast(FP8X4), scales=vsc[:], in_=vx[:])
+                    nc.tensor.transpose(bank(V_BANK)[:, c * P : (c + 1) * P], words[:, u:256:2], ident[:])
+            nc.scalar.copy(vx[:].bitcast(F32).rearrange("p (g e u) -> p g e u", g=2, u=2), bank(V_BANK).rearrange("p (g u e) -> p g e u", g=2, u=2))
 
-        gather("s", vg[:], vraw[:].indirect(slots[:]))
-        at = keep.tile([P, 8, 2 * P], F32, name="at", tag="vraw")
+        gather("s", vg[0][:], vlow[:].indirect(slots[:, 0:32]))
+        at = keep.tile([P, 8, 2 * P], F32, name="at", tag="vlow")
         scores_by_query(0)
         scores_by_query(1)
         for n in range(4):
@@ -265,18 +270,21 @@ def tile_attend_x_router_ks_kernel(tc, xq, kT, vT, ks, vs, offs, qoffs, out):
         for j in (0, 1):
             nc.vector.tensor_reduce(nm[:, j : j + 1], a_all[:, j, :], X, MAX, negate=True)
             weights(j, 1.0)
-        turn_values()
         for g in range(2):
             for j in (2, 3):
                 stabiliser(j, g)
         for j in (2, 3):
             weights(j, -1.0)
+        vg[1] = keep.tile([P, 512], BF16, name="vg1", tag="half3")
+        gather("v", vg[1][:], vhigh[:].indirect(slots[:, 32:64]))
         turn_and_scale(1)
-        turn_and_scale(2, (0,))
+        turn_values()
         scale_and_turn(0, nc.scalar.copy)
+        turn_and_scale(2)
         normaliser(0)
+        vc = keep.tile([P, 2 * DV], U32, name="vc", tag="p2", align_bytes=64)
+        nc.vector.quantize_mx(out=vc[:].bitcast(FP8X4), scales=vsc[:], in_=vx[:])
         quantise_weights(0)
-        turn_and_scale(2, (1,))
         values(0)
         scatter(0, "s")
         normaliser(1)

@@ -22,7 +22,8 @@ MAX = mybir.AluOpType.max
 X = mybir.AxisListType.X
 BANK = 512
 LAST = P - 1
-SPLIT = 640
+SPLIT = 576
+HEAD = 512
 
 
 def tile_attend_x_router_ks_kernel(tc, xq, kT, vT, ks, vs, offs, qoffs, out):
@@ -41,13 +42,14 @@ def tile_attend_x_router_ks_kernel(tc, xq, kT, vT, ks, vs, offs, qoffs, out):
 
         kview = kT.rearrange("(p t) w -> p t w", t=4)
         qview = xq.rearrange("(p t) w -> p t w", t=4)
-        nc.sync.dma_start(slots[:], offs)
-        nc.sync.dma_start(vsw[LAST:P, :], vs[0:1, :])
-        nc.sync.dma_start(ksw[LAST:P, :], ks[0:1, :])
         kpl = [keep.tile([P, T], F32, name="kplane%d" % t, tag="kplane%d" % t) for t in range(4)]
         qpl = [keep.tile([P, T], F32, name="qplane%d" % t, tag="qplane%d" % t) for t in range(4)]
         vlow = keep.tile([P, T - 512], F32, name="vlow", tag="vlow")
-        nc.sync.dma_start(kpl[0][:], kview[:, 0, :])
+        nc.sync.dma_start(kpl[0][:, 0:HEAD], kview[:, 0, 0:HEAD])
+        nc.sync.dma_start(slots[:], offs)
+        nc.sync.dma_start(vsw[LAST:P, :], vs[0:1, :])
+        nc.sync.dma_start(ksw[LAST:P, :], ks[0:1, :])
+        nc.sync.dma_start(kpl[0][:, HEAD:T], kview[:, 0, HEAD:T])
         nc.sync.dma_start(kpl[1][:], kview[:, 1, :])
         nc.sync.dma_start(qlist[:], qoffs)
         for t in (2, 3):
@@ -114,19 +116,18 @@ def tile_attend_x_router_ks_kernel(tc, xq, kT, vT, ks, vs, offs, qoffs, out):
         gather("s", qg[:, 0, :], qpl[0][:].indirect(qlist[:]))
         for h, eng in enumerate("sv"):
             gather(eng, qg[:, 1, h * 256 : (h + 1) * 256], qpl[1][:].indirect(qlist[:, h * 16 : (h + 1) * 16]))
-        rows = keep.tile([P, 2 * N], F32, name="rows", tag="qplane1")
-        ks_row = rows[:, 0:N]
-        vs_row = rows[:, N : 2 * N]
+        ks_row = keep.tile([P, 2, N], F32, name="ks_row", tag="qplane1")
         for g in range(2):
             for i in range(4):
                 c = 4 * g + i
                 nc.tensor.transpose(bank(4 + g)[:, i * P : (i + 1) * P], ks_col[:, c : c + 1].to_broadcast([P, P]), ident[:])
-            nc.scalar.copy(ks_row[:, g * BANK : (g + 1) * BANK].rearrange("p (t s) -> p t s", t=4), bank(4 + g).rearrange("p (s t) -> p t s", t=4))
+            cols = slice(g * BANK, (g + 1) * BANK)
+            nc.scalar.copy(ks_row[:, 0, cols].rearrange("p (u s e) -> p u s e", u=2, e=2), bank(4 + g).rearrange("p (s u e) -> p u s e", u=2, e=2))
+            nc.scalar.copy(ks_row[:, 1, cols].rearrange("p (t s) -> p t s", t=4), bank(4 + g).rearrange("p (s t) -> p t s", t=4))
         for g in range(2):
             for t in range(4):
                 c = 4 * g + t
                 nc.tensor.transpose(bank(6 + g)[:, t * P : (t + 1) * P], vs_col[:, c : c + 1].to_broadcast([P, P]), ident[:])
-            nc.scalar.copy(vs_row[:, g * BANK : (g + 1) * BANK].rearrange("p (u s e) -> p u s e", u=2, e=2), bank(6 + g).rearrange("p (u e s) -> p u s e", u=2, e=2))
 
         qwords = qx[:].rearrange("p (n t) -> p n t", t=4)
         nc.vector.tensor_copy(qwords[:, :, 0:2], qg[:, 0:2, :].rearrange("p t n -> p n t"))
@@ -134,6 +135,9 @@ def tile_attend_x_router_ks_kernel(tc, xq, kT, vT, ks, vs, offs, qoffs, out):
         gather("v", qwords[:, 0:256, 3], qpl[3][:].indirect(qlist[:, 0:16]))
         gather("s", qg[:, 2, 0:256], qpl[3][:].indirect(qlist[:, 16:32]))
         nc.vector.tensor_copy(qwords[:, 256:512, 3], qg[:, 2, 0:256])
+        vs_row = keep.tile([P, N], F32, name="vs_row", tag="qplane3")
+        for g in range(2):
+            nc.scalar.copy(vs_row[:, g * BANK : (g + 1) * BANK].rearrange("p (u s e) -> p u s e", u=2, e=2), bank(6 + g).rearrange("p (u e s) -> p u s e", u=2, e=2))
         for h in range(2):
             cols = slice(h * 256, (h + 1) * 256)
             nc.vector.quantize_mx(out=qc[:, cols].bitcast(FP8X4), scales=qsc[:, cols], in_=qx[:, h * 1024 : (h + 1) * 1024])
@@ -201,7 +205,7 @@ def tile_attend_x_router_ks_kernel(tc, xq, kT, vT, ks, vs, offs, qoffs, out):
             to, frm, sizes = dealt_views(j)
             for g in range(2):
                 dst, src = dealt(j, g, bank(2 * j + g))
-                nc.vector.tensor_tensor(dst, src, ks_row[:, g * BANK : (g + 1) * BANK].rearrange("p (u e s) -> p u s e" if j in BY_WORDS else to, **sizes), MULT)
+                nc.vector.tensor_tensor(dst, src, ks_row[:, j, g * BANK : (g + 1) * BANK].rearrange(to, **sizes), MULT)
 
         def scores_by_slot(n):
             for c in (2 * n, 2 * n + 1):

@@ -145,19 +145,21 @@ def tile_attend_x_router_ks_kernel(tc, xq, kT, vT, ks, vs, offs, qoffs, out):
         nm = keep.tile([P, 4], F32, name="nm")
         total = keep.tile([P, 4], F32, name="total")
         y_sb = keep.tile([P, NQ], F32, name="y_sb")
-        rl_sb = keep.tile([P, NQ], F32, name="rl_sb")
+        rl_sb = [keep.tile([P, 256], F32, name="rl_sb%d" % h, tag="rl_sb%d" % h, align_bytes=64) for h in range(2)]
         rl = keep.tile([P, 4], F32, name="rl")
         a_all = keep.tile([P, 4, N], F32, name="a_all")
         half = {j: keep.tile([P, 1], F32, name="half%d" % j, tag="half%d" % j) for j in (2, 3)}
         p_of = [keep.tile([P, N], F32, name="p%d" % j, tag="p%d" % j, align_bytes=64) for j in range(4)]
-        wx = keep.tile([P, 4, N], BF16, name="wx", align_bytes=64)
-        wc = keep.tile([P, 4, 2 * P], U32, name="wc", align_bytes=64)
+        first_w = keep.tile([P, 2, N], BF16, name="first_w", tag="first_w", align_bytes=64)
+        wx = {0: first_w[:, 0, :], 1: first_w[:, 1, :], 2: keep.tile([P, N], BF16, name="wx2", align_bytes=64)[:]}
+        first_c = keep.tile([P, 2, 2 * P], U32, name="first_c", align_bytes=64)
+        wc = {0: first_c[:, 0, :], 1: first_c[:, 1, :], 2: keep.tile([P, 2 * P], U32, name="wc2", align_bytes=64)[:]}
         wsc = keep.tile([P, 4, 2 * P], U8, name="wsc", align_bytes=64)
-        wq = keep.tile([P, 1, N], BF16, name="wq")
-        BY_WORDS = (0,)
-        P_BANK = {0: 3, 1: 6, 2: 0, 3: 4}
+        wq = keep.tile([P, 2, N], BF16, name="wq")
+        BY_WORDS = (0, 2)
+        P_BANK = {0: 3, 1: 6, 2: 5, 3: 0}
         Y_BANK = (6, 2)
-        L_BANK = (7, 0)
+        L_BANK = (7, 4)
         V_BANK = 5
 
         def mx(dst, lhs, lhs_scale, rhs, rhs_scale, start=True, stop=True):
@@ -179,21 +181,19 @@ def tile_attend_x_router_ks_kernel(tc, xq, kT, vT, ks, vs, offs, qoffs, out):
                     c = 4 * g + t
                     nc.tensor.transpose(b[:, t * P : (t + 1) * P], p_of[j][:, c * P : (c + 1) * P], ident[:])
                 nc.vector.tensor_tensor(
-                    wx[:, j, g * BANK : (g + 1) * BANK].rearrange("p (q t) -> p q t", t=4),
+                    wx[j][:, g * BANK : (g + 1) * BANK].rearrange("p (q t) -> p q t", t=4),
                     b.rearrange("p (t q) -> p q t", t=4),
                     vs_col[:, 4 * g : 4 * g + 4].unsqueeze(1).to_broadcast([P, P, 4]),
                     MULT,
                 )
 
-        def scale_and_turn(j, copy):
+        def scale_and_turn(j, engine):
+            engine.tensor_tensor(wq[:, j // 2, :], p_of[j][:], vs_row[:], MULT)
             b = bank(P_BANK[j])
             words = wq[:, j // 2, :].bitcast(F32)
-            for g in range(2):
-                cols = slice(g * BANK, (g + 1) * BANK)
-                nc.gpsimd.tensor_tensor(wq[:, j // 2, cols], p_of[j][:, cols], vs_row[:, cols], MULT)
-                for c in (2 * g, 2 * g + 1):
-                    nc.tensor.transpose(b[:, c * P : (c + 1) * P], words[:, c * P : (c + 1) * P], ident[:])
-            copy(wx[:, j, :].bitcast(F32).rearrange("p (g q u) -> p g q u", g=2, u=2), b.rearrange("p (g u q) -> p g q u", g=2, u=2))
+            for c in range(4):
+                nc.tensor.transpose(b[:, c * P : (c + 1) * P], words[:, c * P : (c + 1) * P], ident[:])
+            nc.scalar.copy(wx[j].bitcast(F32).rearrange("p (g q u) -> p g q u", g=2, u=2), b.rearrange("p (g u q) -> p g q u", g=2, u=2))
 
         def scores_by_query(j):
             q_cols = slice(j * P, (j + 1) * P)
@@ -226,16 +226,14 @@ def tile_attend_x_router_ks_kernel(tc, xq, kT, vT, ks, vs, offs, qoffs, out):
         def weights(j, sign):
             nc.scalar.activation(p_of[j][:], a_all[:, j, :], EXP, bias=nm[:, j : j + 1], scale=sign, accum_out=total[:, j : j + 1])
 
-        def quantise_weights(h):
-            flat = "p j n -> p (j n)"
-            js = slice(2 * h, 2 * h + 2)
-            nc.vector.quantize_mx(out=wc[:, js, :].rearrange(flat).bitcast(FP8X4), scales=wsc[:, js, :].rearrange(flat), in_=wx[:, js, :].rearrange(flat))
+        def quantise_weights(j):
+            nc.vector.quantize_mx(out=wc[j].bitcast(FP8X4), scales=wsc[:, j, :], in_=wx[j])
 
         def values(h):
             for i in range(2):
                 for g in range(2):
                     cols = slice(g * P, (g + 1) * P)
-                    mx(bank(Y_BANK[h])[:, i * P : (i + 1) * P], vc[:, cols], vsc[:, cols], wc[:, 2 * h + i, cols], wsc[:, 2 * h + i, cols], g == 0, g == 1)
+                    mx(bank(Y_BANK[h])[:, i * P : (i + 1) * P], vc[:, cols], vsc[:, cols], wc[2 * h + i][:, cols], wsc[:, 2 * h + i, cols], g == 0, g == 1)
 
         def normaliser(h):
             js = slice(2 * h, 2 * h + 2)
@@ -244,11 +242,11 @@ def tile_attend_x_router_ks_kernel(tc, xq, kT, vT, ks, vs, offs, qoffs, out):
             for i in range(2):
                 c = 2 * h + i
                 nc.tensor.transpose(dst[:, i * P : (i + 1) * P], rl[:, c : c + 1].to_broadcast([P, P]), ident[:])
-            nc.scalar.copy(rl_sb[:, h * 256 : (h + 1) * 256], dst)
+            nc.scalar.copy(rl_sb[h][:], dst)
 
         def scatter(h, eng):
             cols = slice(h * 256, (h + 1) * 256)
-            nc.vector.tensor_tensor(y_sb[:, cols], bank(Y_BANK[h])[:, 0:256], rl_sb[:, cols], MULT)
+            nc.vector.tensor_tensor(y_sb[:, cols], bank(Y_BANK[h])[:, 0:256], rl_sb[h][:], MULT)
             gather(eng, window[:].indirect(qlist[:, h * 16 : (h + 1) * 16]), y_sb[:, cols])
 
         vg = {0: keep.tile([P, 512], BF16, name="vg0")}
@@ -283,17 +281,21 @@ def tile_attend_x_router_ks_kernel(tc, xq, kT, vT, ks, vs, offs, qoffs, out):
         gather("v", vg[1][:], vhigh[:].indirect(slots[:, 32:64]))
         turn_and_scale(1)
         turn_values()
-        scale_and_turn(0, nc.scalar.copy)
-        turn_and_scale(2)
+        scale_and_turn(0, nc.gpsimd)
         normaliser(0)
+        scale_and_turn(2, nc.vector)
         vc = keep.tile([P, 2 * DV], U32, name="vc", tag="p2", align_bytes=64)
         nc.vector.quantize_mx(out=vc[:].bitcast(FP8X4), scales=vsc[:], in_=vx[:])
-        quantise_weights(0)
+        flat = "p j n -> p (j n)"
+        nc.vector.quantize_mx(out=first_c[:].rearrange(flat).bitcast(FP8X4), scales=wsc[:, 0:2, :].rearrange(flat), in_=first_w[:].rearrange(flat))
         values(0)
-        scatter(0, "s")
         normaliser(1)
+        wx[3] = keep.tile([P, N], BF16, name="wx3", tag="first_w", align_bytes=64)[:]
         turn_and_scale(3)
-        quantise_weights(1)
+        scatter(0, "s")
+        quantise_weights(2)
+        wc[3] = keep.tile([P, 2 * P], U32, name="wc3", tag="rl_sb0", align_bytes=64)[:]
+        quantise_weights(3)
         values(1)
         scatter(1, "v")
         nc.sync.dma_start(out, window[:])

@@ -159,7 +159,7 @@ def tile_attend_x_router_ks_kernel(tc, xq, kT, vT, ks, vs, offs, qoffs, out):
         BY_WORDS = (0, 2)
         P_BANK = {0: 3, 1: 6, 2: 5, 3: 0}
         Y_BANK = (6, 2)
-        L_BANK = (7, 4)
+        L_BANK = (7, 0)
         V_BANK = 5
 
         def mx(dst, lhs, lhs_scale, rhs, rhs_scale, start=True, stop=True):
@@ -174,15 +174,15 @@ def tile_attend_x_router_ks_kernel(tc, xq, kT, vT, ks, vs, offs, qoffs, out):
             to, frm, sizes = dealt_views(j)
             return a_all[:, j, g * BANK : (g + 1) * BANK].rearrange(to, **sizes), b.rearrange(frm, **sizes)
 
-        def turn_and_scale(j, halves=(0, 1)):
-            for g in halves:
-                b = bank(P_BANK[j] + g)
-                for t in range(4):
-                    c = 4 * g + t
-                    nc.tensor.transpose(b[:, t * P : (t + 1) * P], p_of[j][:, c * P : (c + 1) * P], ident[:])
+        def turn(j):
+            for c in range(8):
+                nc.tensor.transpose(bank(P_BANK[j], 2)[:, c * P : (c + 1) * P], p_of[j][:, c * P : (c + 1) * P], ident[:])
+
+        def scale(j):
+            for g in range(2):
                 nc.vector.tensor_tensor(
                     wx[j][:, g * BANK : (g + 1) * BANK].rearrange("p (q t) -> p q t", t=4),
-                    b.rearrange("p (t q) -> p q t", t=4),
+                    bank(P_BANK[j] + g).rearrange("p (t q) -> p q t", t=4),
                     vs_col[:, 4 * g : 4 * g + 4].unsqueeze(1).to_broadcast([P, P, 4]),
                     MULT,
                 )
@@ -279,19 +279,21 @@ def tile_attend_x_router_ks_kernel(tc, xq, kT, vT, ks, vs, offs, qoffs, out):
             weights(j, -1.0)
         vg[1] = keep.tile([P, 512], BF16, name="vg1", tag="half3")
         gather("v", vg[1][:], vhigh[:].indirect(slots[:, 32:64]))
-        turn_and_scale(1)
+        turn(1)
+        scale(1)
         turn_values()
         scale_and_turn(0, nc.gpsimd)
         normaliser(0)
+        turn(3)
         scale_and_turn(2, nc.vector)
         vc = keep.tile([P, 2 * DV], U32, name="vc", tag="p2", align_bytes=64)
         nc.vector.quantize_mx(out=vc[:].bitcast(FP8X4), scales=vsc[:], in_=vx[:])
         flat = "p j n -> p (j n)"
         nc.vector.quantize_mx(out=first_c[:].rearrange(flat).bitcast(FP8X4), scales=wsc[:, 0:2, :].rearrange(flat), in_=first_w[:].rearrange(flat))
         values(0)
-        normaliser(1)
         wx[3] = keep.tile([P, N], BF16, name="wx3", tag="first_w", align_bytes=64)[:]
-        turn_and_scale(3)
+        scale(3)
+        normaliser(1)
         scatter(0, "s")
         quantise_weights(2)
         wc[3] = keep.tile([P, 2 * P], U32, name="wc3", tag="rl_sb0", align_bytes=64)[:]

@@ -235,14 +235,14 @@ def tile_attend_x_router_ks_kernel(tc, xq, kT, vT, ks, vs, offs, qoffs, out):
                     cols = slice(g * P, (g + 1) * P)
                     mx(bank(Y_BANK[h])[:, i * P : (i + 1) * P], vc[:, cols], vsc[:, cols], wc[2 * h + i][:, cols], wsc[:, 2 * h + i, cols], g == 0, g == 1)
 
-        def normaliser(h):
+        def normaliser(h, copy):
             js = slice(2 * h, 2 * h + 2)
             nc.vector.reciprocal(rl[:, js], total[:, js])
             dst = bank(L_BANK[h])[:, 0:256]
             for i in range(2):
                 c = 2 * h + i
                 nc.tensor.transpose(dst[:, i * P : (i + 1) * P], rl[:, c : c + 1].to_broadcast([P, P]), ident[:])
-            nc.scalar.copy(rl_sb[h][:], dst)
+            copy(rl_sb[h][:], dst)
 
         def scatter(h, eng):
             cols = slice(h * 256, (h + 1) * 256)
@@ -283,7 +283,7 @@ def tile_attend_x_router_ks_kernel(tc, xq, kT, vT, ks, vs, offs, qoffs, out):
         scale(1)
         turn_values()
         scale_and_turn(0, nc.gpsimd)
-        normaliser(0)
+        normaliser(0, nc.scalar.copy)
         turn(3)
         scale_and_turn(2, nc.vector)
         vc = keep.tile([P, 2 * DV], U32, name="vc", tag="p2", align_bytes=64)
@@ -293,11 +293,12 @@ def tile_attend_x_router_ks_kernel(tc, xq, kT, vT, ks, vs, offs, qoffs, out):
         values(0)
         wx[3] = keep.tile([P, N], BF16, name="wx3", tag="first_w", align_bytes=64)[:]
         scale(3)
-        normaliser(1)
         scatter(0, "s")
         quantise_weights(2)
         wc[3] = keep.tile([P, 2 * P], U32, name="wc3", tag="rl_sb0", align_bytes=64)[:]
         quantise_weights(3)
         values(1)
+        normaliser(1, nc.vector.tensor_copy)
         scatter(1, "v")
-        nc.sync.dma_start(out, window[:])
+        nc.sync.dma_start(out[:, 0 : T // 2], window[:, 0 : T // 2])
+        nc.scalar.dma_start(out[:, T // 2 : T], window[:, T // 2 : T])

@@ -285,7 +285,7 @@ def tile_attend_x_router_ks_kernel(tc, xq, kT, vT, ks, vs, offs, qoffs, out):
         scale_and_turn(0, nc.gpsimd)
         normaliser(0, nc.scalar.copy)
         turn(3)
-        scale_and_turn(2, nc.vector)
+        scale_and_turn(2, nc.gpsimd)
         vc = keep.tile([P, 2 * DV], U32, name="vc", tag="p2", align_bytes=64)
         nc.vector.quantize_mx(out=vc[:].bitcast(FP8X4), scales=vsc[:], in_=vx[:])
         flat = "p j n -> p (j n)"
@@ -300,5 +300,4 @@ def tile_attend_x_router_ks_kernel(tc, xq, kT, vT, ks, vs, offs, qoffs, out):
         values(1)
         normaliser(1, nc.vector.tensor_copy)
         scatter(1, "v")
-        nc.sync.dma_start(out[:, 0 : T // 2], window[:, 0 : T // 2])
-        nc.scalar.dma_start(out[:, T // 2 : T], window[:, T // 2 : T])
+        nc.sync.dma_start(out, window[:])

@@ -187,8 +187,9 @@ def tile_attend_x_router_ks_kernel(tc, xq, kT, vT, ks, vs, offs, qoffs, out):
                     MULT,
                 )
 
-        def scale_and_turn(j, engine):
-            engine.tensor_tensor(wq[:, j // 2, :], p_of[j][:], vs_row[:], MULT)
+        def scale_and_turn(j, shares):
+            for engine, lo, hi in shares:
+                engine.tensor_tensor(wq[:, j // 2, lo:hi], p_of[j][:, lo:hi], vs_row[:, lo:hi], MULT)
             b = bank(P_BANK[j])
             words = wq[:, j // 2, :].bitcast(F32)
             for c in range(4):
@@ -282,10 +283,10 @@ def tile_attend_x_router_ks_kernel(tc, xq, kT, vT, ks, vs, offs, qoffs, out):
         turn(1)
         scale(1)
         turn_values()
-        scale_and_turn(0, nc.gpsimd)
+        scale_and_turn(0, ((nc.gpsimd, 0, N),))
         normaliser(0, nc.scalar.copy)
         turn(3)
-        scale_and_turn(2, nc.gpsimd)
+        scale_and_turn(2, ((nc.gpsimd, 0, N // 2), (nc.vector, N // 2, N)))
         vc = keep.tile([P, 2 * DV], U32, name="vc", tag="p2", align_bytes=64)
         nc.vector.quantize_mx(out=vc[:].bitcast(FP8X4), scales=vsc[:], in_=vx[:])
         flat = "p j n -> p (j n)"

@@ -22,8 +22,11 @@ MAX = mybir.AluOpType.max
 X = mybir.AxisListType.X
 BANK = 512
 LAST = P - 1
-SPLIT = 576
+SPLIT = 640
 HEAD = 512
+MID = P // 2 - 1
+HALF = NQ // 2
+PLANE = 4 * T
 
 
 def tile_attend_x_router_ks_kernel(tc, xq, kT, vT, ks, vs, offs, qoffs, out):
@@ -31,24 +34,50 @@ def tile_attend_x_router_ks_kernel(tc, xq, kT, vT, ks, vs, offs, qoffs, out):
     with ExitStack() as ctx:
         lists = ctx.enter_context(tc.tile_pool(name="lists", bufs=1))
         keep = ctx.enter_context(tc.tile_pool(name="keep", bufs=1))
+        planes = ctx.enter_context(tc.tile_pool(name="planes", bufs=1))
+        banks = ctx.enter_context(tc.psum_pool(name="banks", bufs=1))
+        ps = banks.tile([P, 8 * BANK], F32, name="ps")
+
+        def bank(b, n=1):
+            return ps[:, b * BANK : (b + n) * BANK]
+
+        def placed(name, shape, dtype, place, within=0):
+            return planes.tile(shape, dtype, name=name, offset=place * PLANE + within, align_bytes=64)
+
+        def s_move(dst, src):
+            nc.scalar.activation(dst, src, COPY)
+
+        v_move = nc.vector.tensor_copy
+
         slots = lists.tile([P, N // 16], U16, name="slots")
         qlist = lists.tile([P, NQ // 16], U16, name="qlist")
         ident = keep.tile([P, P], F32, name="ident")
         make_identity(nc, ident[:])
+
+        def turn(dst, src):
+            nc.tensor.transpose(dst, src, ident[:])
+
+        def mx(dst, lhs, lhs_scale, rhs, rhs_scale, start=True, stop=True):
+            nc.tensor.matmul_mx(out=dst, lhsT=lhs.bitcast(FP8X4), lhsT_scale=lhs_scale, rhs=rhs.bitcast(FP8X4), rhs_scale=rhs_scale, start=start, stop=stop)
+
+        def quantise(codes, scales, src):
+            nc.vector.quantize_mx(out=codes.bitcast(FP8X4), scales=scales, in_=src)
+
         ksw = keep.tile([P, T], F32, name="ksw", tag="ksw")
         vsw = keep.tile([P, T], F32, name="vsw", tag="vsw")
-        nc.vector.memset(vsw[0:LAST, :], 0.0)
         nc.vector.memset(ksw[0:LAST, :], 0.0)
+        nc.vector.memset(vsw[0:MID, :], 0.0)
+        nc.vector.memset(vsw[MID + 1 : P, :], 0.0)
 
         kview = kT.rearrange("(p t) w -> p t w", t=4)
         qview = xq.rearrange("(p t) w -> p t w", t=4)
-        kpl = [keep.tile([P, T], F32, name="kplane%d" % t, tag="kplane%d" % t) for t in range(4)]
-        qpl = [keep.tile([P, T], F32, name="qplane%d" % t, tag="qplane%d" % t) for t in range(4)]
+        kpl = [placed("kplane%d" % t, [P, T], F32, t) for t in range(4)]
+        qpl = [placed("qplane%d" % t, [P, T], F32, 4 + t) for t in range(4)]
         vlow = keep.tile([P, T - 512], F32, name="vlow", tag="vlow")
         nc.sync.dma_start(kpl[0][:, 0:HEAD], kview[:, 0, 0:HEAD])
         nc.sync.dma_start(slots[:], offs)
-        nc.sync.dma_start(vsw[LAST:P, :], vs[0:1, :])
         nc.sync.dma_start(ksw[LAST:P, :], ks[0:1, :])
+        nc.sync.dma_start(vsw[MID : MID + 1, :], vs[0:1, :])
         nc.sync.dma_start(kpl[0][:, HEAD:T], kview[:, 0, HEAD:T])
         nc.sync.dma_start(kpl[1][:], kview[:, 1, :])
         nc.sync.dma_start(qlist[:], qoffs)
@@ -57,90 +86,84 @@ def tile_attend_x_router_ks_kernel(tc, xq, kT, vT, ks, vs, offs, qoffs, out):
         for t in range(4):
             nc.sync.dma_start(qpl[t][:], qview[:, t, :])
         nc.sync.dma_start(vlow[:], vT[:, 0 : T - 512])
-
-        def gather(engine, dst, src):
-            if engine == "s":
-                nc.scalar.activation(dst, src, COPY)
-            else:
-                nc.vector.tensor_copy(dst, src)
-
-        banks = ctx.enter_context(tc.psum_pool(name="banks", bufs=1))
-        ps = banks.tile([P, 8 * BANK], F32, name="ps")
-
-        def bank(b, n=1):
-            return ps[:, b * BANK : (b + n) * BANK]
-
-        ksg = keep.tile([P, N], F32, name="ksg")
-
-        def gather_keys(t):
-            gather("v", kg[0][:, t, :], kpl[t][:].indirect(slots[:, 0 : SPLIT // 16]))
-            gather("s", kg[1][:, t, :], kpl[t][:].indirect(slots[:, SPLIT // 16 : N // 16]))
-
-        vsg = keep.tile([P, N], F32, name="vsg")
-        gather("v", ksg[:], ksw[:].indirect(slots[:]))
-        gather("s", vsg[:], vsw[:].indirect(slots[:]))
-        kg = [keep.tile([P, 4, SPLIT], BF16, name="kg0", tag="ksw"), keep.tile([P, 4, N - SPLIT], BF16, name="kg1")]
-        window = keep.tile([P, T], F32, name="window", tag="vsw")
-        nc.gpsimd.memset(window[:], 0.0)
-        for t in range(4):
-            gather_keys(t)
-        vhigh = keep.tile([P, T], F32, name="vhigh", tag="kplane0")
+        vhigh = placed("vhigh", [P, T], F32, 8)
         nc.gpsimd.memset(vhigh[:, 0:512], 0.0)
         nc.sync.dma_start(vhigh[:, 512:T], vT[:, 512:T])
 
-        columns = keep.tile([P, 16], F32, name="columns", tag="kplane3")
-        ks_col = columns[:, 0:8]
-        vs_col = columns[:, 8:16]
+        ksg = keep.tile([P, N], F32, name="ksg")
+        vsg = keep.tile([P, N], F32, name="vsg")
+        v_move(ksg[:], ksw[:].indirect(slots[:]))
+        s_move(vsg[:], vsw[:].indirect(slots[:]))
+        window = keep.tile([P, T], F32, name="window")
+        nc.gpsimd.memset(window[:], 0.0)
+        ks_col = keep.tile([P, 8], F32, name="ks_col")
         for g in range(2):
             for i in range(4):
                 c = 4 * g + i
-                nc.tensor.transpose(bank(g)[:, i * P : (i + 1) * P], ksg[:, c * P : (c + 1) * P], ident[:])
-            nc.vector.tensor_copy(ks_col[:, 4 * g : 4 * g + 4], bank(g)[:, LAST:BANK:P])
+                turn(bank(g)[:, i * P : (i + 1) * P], ksg[:, c * P : (c + 1) * P])
+            nc.scalar.copy(ks_col[:, 4 * g : 4 * g + 4], bank(g)[:, LAST:BANK:P])
         for g in range(2):
             for t in range(4):
-                nc.tensor.transpose(bank(2 + g)[:, t * P : (t + 1) * P], vsg[:, g * 512 + t : (g + 1) * 512 : 4], ident[:])
-            nc.vector.tensor_copy(vs_col[:, 4 * g : 4 * g + 4], bank(2 + g)[:, LAST:BANK:P])
-        kx = keep.tile([P, 4 * N], BF16, name="kx", align_bytes=64)
-        qx = keep.tile([P, 4 * NQ], BF16, name="qx", align_bytes=64)
-        kc = keep.tile([P, N], U32, name="kc", align_bytes=64)
-        ksc = keep.tile([P, N], U8, name="ksc", align_bytes=64)
-        for g, (lo, hi) in enumerate(((0, SPLIT), (SPLIT, N))):
-            nc.vector.tensor_copy(kx[:, 4 * lo : 4 * hi].rearrange("p (n t) -> p n t", t=4), kg[g][:].rearrange("p t n -> p n t"))
-        for g in range(2):
-            cols = slice(g * 512, (g + 1) * 512)
-            nc.vector.quantize_mx(out=kc[:, cols].bitcast(FP8X4), scales=ksc[:, cols], in_=kx[:, g * 2048 : (g + 1) * 2048])
-
-        qg = keep.tile([P, 3, NQ], BF16, name="qg")
-        qc = keep.tile([P, NQ], U32, name="qc", align_bytes=64)
-        qsc = keep.tile([P, NQ], U8, name="qsc", align_bytes=64)
-        gather("s", qg[:, 0, :], qpl[0][:].indirect(qlist[:]))
-        for h, eng in enumerate("sv"):
-            gather(eng, qg[:, 1, h * 256 : (h + 1) * 256], qpl[1][:].indirect(qlist[:, h * 16 : (h + 1) * 16]))
-        ks_row = keep.tile([P, 2, N], F32, name="ks_row", tag="qplane1")
+                turn(bank(2 + g)[:, t * P : (t + 1) * P], vsg[:, g * 512 + t : (g + 1) * 512 : 4])
         for g in range(2):
             for i in range(4):
                 c = 4 * g + i
-                nc.tensor.transpose(bank(4 + g)[:, i * P : (i + 1) * P], ks_col[:, c : c + 1].to_broadcast([P, P]), ident[:])
-            cols = slice(g * BANK, (g + 1) * BANK)
-            nc.scalar.copy(ks_row[:, 0, cols].rearrange("p (u s e) -> p u s e", u=2, e=2), bank(4 + g).rearrange("p (s u e) -> p u s e", u=2, e=2))
-            nc.scalar.copy(ks_row[:, 1, cols].rearrange("p (t s) -> p t s", t=4), bank(4 + g).rearrange("p (s t) -> p t s", t=4))
+                turn(bank(4 + g)[:, i * P : (i + 1) * P], ks_col[:, c : c + 1].to_broadcast([P, P]))
+
+        kg = keep.tile([P, 4, N], BF16, name="kg", tag="ksw")
+        kc = keep.tile([P, N], U32, name="kc", align_bytes=64)
+        ksc = keep.tile([P, N], U8, name="ksc", align_bytes=64)
+        kx = {}
+
+        def gather_keys(t):
+            v_move(kg[:, t, 0:SPLIT], kpl[t][:].indirect(slots[:, 0 : SPLIT // 16]))
+            s_move(kg[:, t, SPLIT:N], kpl[t][:].indirect(slots[:, SPLIT // 16 : N // 16]))
+
+        def weave_keys(g):
+            v_move(kx[g][:].rearrange("p (n t) -> p n t", t=4), kg[:, :, g * 512 : (g + 1) * 512].rearrange("p t n -> p n t"))
+
+        gather_keys(0)
+        gather_keys(1)
+        kx[0] = keep.tile([P, 4 * 512], BF16, name="kx0", align_bytes=64)
+        gather_keys(2)
+        kx[1] = placed("kx1", [P, 4 * 512], BF16, 2)
+        vs_col = placed("vs_col", [P, 8], F32, 2, 4096)
+        for g in range(2):
+            nc.scalar.copy(vs_col[:, 4 * g : 4 * g + 4], bank(2 + g)[:, MID:BANK:P])
         for g in range(2):
             for t in range(4):
                 c = 4 * g + t
-                nc.tensor.transpose(bank(6 + g)[:, t * P : (t + 1) * P], vs_col[:, c : c + 1].to_broadcast([P, P]), ident[:])
+                turn(bank(6 + g)[:, t * P : (t + 1) * P], vs_col[:, c : c + 1].to_broadcast([P, P]))
+        gather_keys(3)
+        for g in range(2):
+            weave_keys(g)
+        for g in range(2):
+            cols = slice(g * 512, (g + 1) * 512)
+            quantise(kc[:, cols], ksc[:, cols], kx[g][:])
+        ks_row = placed("ks_row", [P, N], F32, 3)
+        for g in range(2):
+            nc.scalar.copy(ks_row[:, g * BANK : (g + 1) * BANK].rearrange("p (t s) -> p t s", t=4), bank(4 + g).rearrange("p (s t) -> p t s", t=4))
 
+        qx = keep.tile([P, 4 * NQ], BF16, name="qx", align_bytes=64)
+        qg = keep.tile([P, 2, NQ], BF16, name="qg")
+        qlate = keep.tile([P, 2, HALF], BF16, name="qlate")
+        qc = keep.tile([P, NQ], U32, name="qc", align_bytes=64)
+        qsc = keep.tile([P, NQ], U8, name="qsc", align_bytes=64)
         qwords = qx[:].rearrange("p (n t) -> p n t", t=4)
-        nc.vector.tensor_copy(qwords[:, :, 0:2], qg[:, 0:2, :].rearrange("p t n -> p n t"))
-        gather("v", qwords[:, :, 2], qpl[2][:].indirect(qlist[:]))
-        gather("v", qwords[:, 0:256, 3], qpl[3][:].indirect(qlist[:, 0:16]))
-        gather("s", qg[:, 2, 0:256], qpl[3][:].indirect(qlist[:, 16:32]))
-        nc.vector.tensor_copy(qwords[:, 256:512, 3], qg[:, 2, 0:256])
-        vs_row = keep.tile([P, N], F32, name="vs_row", tag="qplane3")
+        first, second = qlist[:, 0 : HALF // 16], qlist[:, HALF // 16 : NQ // 16]
+        s_move(qg[:, 0, :], qpl[0][:].indirect(qlist[:]))
+        s_move(qg[:, 1, 0:HALF], qpl[1][:].indirect(first))
+        v_move(qg[:, 1, HALF:NQ], qpl[1][:].indirect(second))
+        vs_row = placed("vs_row", [P, N], F32, 5)
         for g in range(2):
             nc.scalar.copy(vs_row[:, g * BANK : (g + 1) * BANK].rearrange("p (u s e) -> p u s e", u=2, e=2), bank(6 + g).rearrange("p (u e s) -> p u s e", u=2, e=2))
-        for h in range(2):
-            cols = slice(h * 256, (h + 1) * 256)
-            nc.vector.quantize_mx(out=qc[:, cols].bitcast(FP8X4), scales=qsc[:, cols], in_=qx[:, h * 1024 : (h + 1) * 1024])
+        v_move(qwords[:, :, 0:2], qg[:].rearrange("p t n -> p n t"))
+        for t in (2, 3):
+            v_move(qwords[:, 0:HALF, t], qpl[t][:].indirect(first))
+            s_move(qlate[:, t - 2, :], qpl[t][:].indirect(second))
+        quantise(qc[:, 0:HALF], qsc[:, 0:HALF], qx[:, 0 : 4 * HALF])
+        v_move(qwords[:, HALF:NQ, 2:4], qlate[:].rearrange("p t n -> p n t"))
+        quantise(qc[:, HALF:NQ], qsc[:, HALF:NQ], qx[:, 4 * HALF : 4 * NQ])
 
         nm = keep.tile([P, 4], F32, name="nm")
         total = keep.tile([P, 4], F32, name="total")
@@ -162,12 +185,7 @@ def tile_attend_x_router_ks_kernel(tc, xq, kT, vT, ks, vs, offs, qoffs, out):
         L_BANK = (7, 0)
         V_BANK = 5
 
-        def mx(dst, lhs, lhs_scale, rhs, rhs_scale, start=True, stop=True):
-            nc.tensor.matmul_mx(out=dst, lhsT=lhs.bitcast(FP8X4), lhsT_scale=lhs_scale, rhs=rhs.bitcast(FP8X4), rhs_scale=rhs_scale, start=start, stop=stop)
-
         def dealt_views(j):
-            if j in BY_WORDS:
-                return "p (u s e) -> p u s e", "p (s u e) -> p u s e", dict(u=2, e=2)
             return "p (t s) -> p t s", "p (s t) -> p t s", dict(t=4)
 
         def dealt(j, g, b):
@@ -206,7 +224,7 @@ def tile_attend_x_router_ks_kernel(tc, xq, kT, vT, ks, vs, offs, qoffs, out):
             to, frm, sizes = dealt_views(j)
             for g in range(2):
                 dst, src = dealt(j, g, bank(2 * j + g))
-                nc.vector.tensor_tensor(dst, src, ks_row[:, j, g * BANK : (g + 1) * BANK].rearrange(to, **sizes), MULT)
+                nc.vector.tensor_tensor(dst, src, ks_row[:, g * BANK : (g + 1) * BANK].rearrange(to, **sizes), MULT)
 
         def scores_by_slot(n):
             for c in (2 * n, 2 * n + 1):
@@ -225,7 +243,10 @@ def tile_attend_x_router_ks_kernel(tc, xq, kT, vT, ks, vs, offs, qoffs, out):
             nc.vector.tensor_scalar(dst, src, -1.0, first, MULT, MIN, accum_out=least)
 
         def weights(j, sign):
-            nc.scalar.activation(p_of[j][:], a_all[:, j, :], EXP, bias=nm[:, j : j + 1], scale=sign, accum_out=total[:, j : j + 1])
+            dst, src = p_of[j][:], a_all[:, j, :]
+            if j in BY_WORDS:
+                dst, src = dst.rearrange("p (u s e) -> p u s e", u=4, e=2), src.rearrange("p (u e s) -> p u s e", u=4, e=2)
+            nc.scalar.activation(dst, src, EXP, bias=nm[:, j : j + 1], scale=sign, accum_out=total[:, j : j + 1])
 
         def quantise_weights(j):
             nc.vector.quantize_mx(out=wc[j].bitcast(FP8X4), scales=wsc[:, j, :], in_=wx[j])
@@ -248,7 +269,7 @@ def tile_attend_x_router_ks_kernel(tc, xq, kT, vT, ks, vs, offs, qoffs, out):
         def scatter(h, eng):
             cols = slice(h * 256, (h + 1) * 256)
             nc.vector.tensor_tensor(y_sb[:, cols], bank(Y_BANK[h])[:, 0:256], rl_sb[h][:], MULT)
-            gather(eng, window[:].indirect(qlist[:, h * 16 : (h + 1) * 16]), y_sb[:, cols])
+            eng(window[:].indirect(qlist[:, h * 16 : (h + 1) * 16]), y_sb[:, cols])
 
         vg = {0: keep.tile([P, 512], BF16, name="vg0")}
         vx = keep.tile([P, N], BF16, name="vx", align_bytes=64)
@@ -262,7 +283,7 @@ def tile_attend_x_router_ks_kernel(tc, xq, kT, vT, ks, vs, offs, qoffs, out):
                     nc.tensor.transpose(bank(V_BANK)[:, c * P : (c + 1) * P], words[:, u:256:2], ident[:])
             nc.scalar.copy(vx[:].bitcast(F32).rearrange("p (g e u) -> p g e u", g=2, u=2), bank(V_BANK).rearrange("p (g u e) -> p g e u", g=2, u=2))
 
-        gather("s", vg[0][:], vlow[:].indirect(slots[:, 0:32]))
+        s_move(vg[0][:], vlow[:].indirect(slots[:, 0:32]))
         at = keep.tile([P, 8, 2 * P], F32, name="at", tag="vlow")
         scores_by_query(0)
         scores_by_query(1)
@@ -279,7 +300,7 @@ def tile_attend_x_router_ks_kernel(tc, xq, kT, vT, ks, vs, offs, qoffs, out):
         for j in (2, 3):
             weights(j, -1.0)
         vg[1] = keep.tile([P, 512], BF16, name="vg1", tag="half3")
-        gather("v", vg[1][:], vhigh[:].indirect(slots[:, 32:64]))
+        v_move(vg[1][:], vhigh[:].indirect(slots[:, 32:64]))
         turn(1)
         scale(1)
         turn_values()
@@ -294,11 +315,11 @@ def tile_attend_x_router_ks_kernel(tc, xq, kT, vT, ks, vs, offs, qoffs, out):
         values(0)
         wx[3] = keep.tile([P, N], BF16, name="wx3", tag="first_w", align_bytes=64)[:]
         scale(3)
-        scatter(0, "s")
+        scatter(0, s_move)
         quantise_weights(2)
         wc[3] = keep.tile([P, 2 * P], U32, name="wc3", tag="rl_sb0", align_bytes=64)[:]
         quantise_weights(3)
         values(1)
         normaliser(1, nc.vector.tensor_copy)
-        scatter(1, "v")
+        scatter(1, v_move)
         nc.sync.dma_start(out, window[:])

@@ -161,9 +161,9 @@ def tile_attend_x_router_ks_kernel(tc, xq, kT, vT, ks, vs, offs, qoffs, out):
         for t in (2, 3):
             v_move(qwords[:, 0:HALF, t], qpl[t][:].indirect(first))
             s_move(qlate[:, t - 2, :], qpl[t][:].indirect(second))
-        quantise(qc[:, 0:HALF], qsc[:, 0:HALF], qx[:, 0 : 4 * HALF])
+        quantise(qc[:, 0:P], qsc[:, 0:P], qx[:, 0 : 4 * P])
         v_move(qwords[:, HALF:NQ, 2:4], qlate[:].rearrange("p t n -> p n t"))
-        quantise(qc[:, HALF:NQ], qsc[:, HALF:NQ], qx[:, 4 * HALF : 4 * NQ])
+        quantise(qc[:, P:NQ], qsc[:, P:NQ], qx[:, 4 * P : 4 * NQ])
 
         nm = keep.tile([P, 4], F32, name="nm")
         total = keep.tile([P, 4], F32, name="total")

@@ -24,6 +24,7 @@ BANK = 512
 LAST = P - 1
 SPLIT = 640
 HEAD = 512
+SHARE = 384
 MID = P // 2 - 1
 HALF = NQ // 2
 PLANE = 4 * T
@@ -54,7 +55,7 @@ def tile_attend_x_router_ks_kernel(tc, xq, kT, vT, ks, vs, offs, qoffs, out):
         ident = keep.tile([P, P], F32, name="ident")
         make_identity(nc, ident[:])
 
-        def turn(dst, src):
+        def turn_one(dst, src):
             nc.tensor.transpose(dst, src, ident[:])
 
         def mx(dst, lhs, lhs_scale, rhs, rhs_scale, start=True, stop=True):
@@ -100,15 +101,15 @@ def tile_attend_x_router_ks_kernel(tc, xq, kT, vT, ks, vs, offs, qoffs, out):
         for g in range(2):
             for i in range(4):
                 c = 4 * g + i
-                turn(bank(g)[:, i * P : (i + 1) * P], ksg[:, c * P : (c + 1) * P])
+                turn_one(bank(g)[:, i * P : (i + 1) * P], ksg[:, c * P : (c + 1) * P])
             nc.scalar.copy(ks_col[:, 4 * g : 4 * g + 4], bank(g)[:, LAST:BANK:P])
         for g in range(2):
             for t in range(4):
-                turn(bank(2 + g)[:, t * P : (t + 1) * P], vsg[:, g * 512 + t : (g + 1) * 512 : 4])
+                turn_one(bank(2 + g)[:, t * P : (t + 1) * P], vsg[:, g * 512 + t : (g + 1) * 512 : 4])
         for g in range(2):
             for i in range(4):
                 c = 4 * g + i
-                turn(bank(4 + g)[:, i * P : (i + 1) * P], ks_col[:, c : c + 1].to_broadcast([P, P]))
+                turn_one(bank(4 + g)[:, i * P : (i + 1) * P], ks_col[:, c : c + 1].to_broadcast([P, P]))
 
         kg = keep.tile([P, 4, N], BF16, name="kg", tag="ksw")
         kc = keep.tile([P, N], U32, name="kc", align_bytes=64)
@@ -133,7 +134,7 @@ def tile_attend_x_router_ks_kernel(tc, xq, kT, vT, ks, vs, offs, qoffs, out):
         for g in range(2):
             for t in range(4):
                 c = 4 * g + t
-                turn(bank(6 + g)[:, t * P : (t + 1) * P], vs_col[:, c : c + 1].to_broadcast([P, P]))
+                turn_one(bank(6 + g)[:, t * P : (t + 1) * P], vs_col[:, c : c + 1].to_broadcast([P, P]))
         gather_keys(3)
         for g in range(2):
             weave_keys(g)
@@ -182,7 +183,7 @@ def tile_attend_x_router_ks_kernel(tc, xq, kT, vT, ks, vs, offs, qoffs, out):
         BY_WORDS = (0, 2)
         P_BANK = {0: 3, 1: 6, 2: 5, 3: 0}
         Y_BANK = (6, 2)
-        L_BANK = (7, 0)
+        L_BANK = (4, 0)
         V_BANK = 5
 
         def dealt_views(j):
@@ -257,14 +258,12 @@ def tile_attend_x_router_ks_kernel(tc, xq, kT, vT, ks, vs, offs, qoffs, out):
                     cols = slice(g * P, (g + 1) * P)
                     mx(bank(Y_BANK[h])[:, i * P : (i + 1) * P], vc[:, cols], vsc[:, cols], wc[2 * h + i][:, cols], wsc[:, 2 * h + i, cols], g == 0, g == 1)
 
-        def normaliser(h, copy):
+        def normaliser(h):
             js = slice(2 * h, 2 * h + 2)
             nc.vector.reciprocal(rl[:, js], total[:, js])
-            dst = bank(L_BANK[h])[:, 0:256]
             for i in range(2):
                 c = 2 * h + i
-                nc.tensor.transpose(dst[:, i * P : (i + 1) * P], rl[:, c : c + 1].to_broadcast([P, P]), ident[:])
-            copy(rl_sb[h][:], dst)
+                turn_one(bank(L_BANK[h])[:, i * P : (i + 1) * P], rl[:, c : c + 1].to_broadcast([P, P]))
 
         def scatter(h, eng):
             cols = slice(h * 256, (h + 1) * 256)
@@ -302,12 +301,13 @@ def tile_attend_x_router_ks_kernel(tc, xq, kT, vT, ks, vs, offs, qoffs, out):
         vg[1] = keep.tile([P, 512], BF16, name="vg1", tag="half3")
         v_move(vg[1][:], vhigh[:].indirect(slots[:, 32:64]))
         turn(1)
+        normaliser(0)
         scale(1)
         turn_values()
         scale_and_turn(0, ((nc.gpsimd, 0, N),))
-        normaliser(0, nc.scalar.copy)
+        nc.scalar.copy(rl_sb[0][:], bank(L_BANK[0])[:, 0:HALF])
         turn(3)
-        scale_and_turn(2, ((nc.gpsimd, 0, N // 2), (nc.vector, N // 2, N)))
+        scale_and_turn(2, ((nc.gpsimd, 0, SHARE), (nc.vector, SHARE, N)))
         vc = keep.tile([P, 2 * DV], U32, name="vc", tag="p2", align_bytes=64)
         nc.vector.quantize_mx(out=vc[:].bitcast(FP8X4), scales=vsc[:], in_=vx[:])
         flat = "p j n -> p (j n)"
@@ -320,6 +320,7 @@ def tile_attend_x_router_ks_kernel(tc, xq, kT, vT, ks, vs, offs, qoffs, out):
         wc[3] = keep.tile([P, 2 * P], U32, name="wc3", tag="rl_sb0", align_bytes=64)[:]
         quantise_weights(3)
         values(1)
-        normaliser(1, nc.vector.tensor_copy)
+        normaliser(1)
+        v_move(rl_sb[1][:], bank(L_BANK[1])[:, 0:HALF])
         scatter(1, v_move)
         nc.sync.dma_start(out, window[:])

@@ -253,7 +253,7 @@ def tile_attend_x_router_ks_kernel(tc, xq, kT, vT, ks, vs, offs, qoffs, out):
             nc.vector.quantize_mx(out=wc[j].bitcast(FP8X4), scales=wsc[:, j, :], in_=wx[j])
 
         def values(h):
-            for i in range(2):
+            for i in ((1, 0), (0, 1))[h]:
                 for g in range(2):
                     cols = slice(g * P, (g + 1) * P)
                     mx(bank(Y_BANK[h])[:, i * P : (i + 1) * P], vc[:, cols], vsc[:, cols], wc[2 * h + i][:, cols], wsc[:, 2 * h + i, cols], g == 0, g == 1)
@@ -310,8 +310,8 @@ def tile_attend_x_router_ks_kernel(tc, xq, kT, vT, ks, vs, offs, qoffs, out):
         scale_and_turn(2, ((nc.gpsimd, 0, SHARE), (nc.vector, SHARE, N)))
         vc = keep.tile([P, 2 * DV], U32, name="vc", tag="p2", align_bytes=64)
         nc.vector.quantize_mx(out=vc[:].bitcast(FP8X4), scales=vsc[:], in_=vx[:])
-        flat = "p j n -> p (j n)"
-        nc.vector.quantize_mx(out=first_c[:].rearrange(flat).bitcast(FP8X4), scales=wsc[:, 0:2, :].rearrange(flat), in_=first_w[:].rearrange(flat))
+        for j in (1, 0):
+            quantise_weights(j)
         values(0)
         wx[3] = keep.tile([P, N], BF16, name="wx3", tag="first_w", align_bytes=64)[:]
         scale(3)

@@ -88,15 +88,12 @@ def tile_attend_x_router_ks_kernel(tc, xq, kT, vT, ks, vs, offs, qoffs, out):
             nc.sync.dma_start(qpl[t][:], qview[:, t, :])
         nc.sync.dma_start(vlow[:], vT[:, 0 : T - 512])
         vhigh = placed("vhigh", [P, T], F32, 8)
-        nc.gpsimd.memset(vhigh[:, 0:512], 0.0)
-        nc.sync.dma_start(vhigh[:, 512:T], vT[:, 512:T])
+        nc.sync.dma_start(vhigh[:], vT)
 
         ksg = keep.tile([P, N], F32, name="ksg")
         vsg = keep.tile([P, N], F32, name="vsg")
         v_move(ksg[:], ksw[:].indirect(slots[:]))
         s_move(vsg[:], vsw[:].indirect(slots[:]))
-        window = keep.tile([P, T], F32, name="window")
-        nc.gpsimd.memset(window[:], 0.0)
         ks_col = keep.tile([P, 8], F32, name="ks_col")
         for g in range(2):
             for i in range(4):
@@ -145,7 +142,7 @@ def tile_attend_x_router_ks_kernel(tc, xq, kT, vT, ks, vs, offs, qoffs, out):
         for g in range(2):
             nc.scalar.copy(ks_row[:, g * BANK : (g + 1) * BANK].rearrange("p (t s) -> p t s", t=4), bank(4 + g).rearrange("p (s t) -> p t s", t=4))
 
-        qx = keep.tile([P, 4 * NQ], BF16, name="qx", align_bytes=64)
+        qx = keep.tile([P, 4 * NQ], BF16, name="qx", tag="qx", align_bytes=64)
         qg = keep.tile([P, 2, NQ], BF16, name="qg")
         qlate = keep.tile([P, 2, HALF], BF16, name="qlate")
         qc = keep.tile([P, NQ], U32, name="qc", align_bytes=64)
@@ -165,6 +162,8 @@ def tile_attend_x_router_ks_kernel(tc, xq, kT, vT, ks, vs, offs, qoffs, out):
         quantise(qc[:, 0:P], qsc[:, 0:P], qx[:, 0 : 4 * P])
         v_move(qwords[:, HALF:NQ, 2:4], qlate[:].rearrange("p t n -> p n t"))
         quantise(qc[:, P:NQ], qsc[:, P:NQ], qx[:, 4 * P : 4 * NQ])
+        window = keep.tile([P, T], F32, name="window", tag="qx", align_bytes=64)
+        nc.gpsimd.memset(window[:], 0.0)
 
         nm = keep.tile([P, 4], F32, name="nm")
         total = keep.tile([P, 4], F32, name="total")

@@ -25,7 +25,7 @@ LAST = P - 1
 SPLIT = 640
 HEAD = 512
 SHARE = 384
-MID = P // 2 - 1
+MID = P - 1
 HALF = NQ // 2
 PLANE = 4 * T
 
@@ -67,8 +67,7 @@ def tile_attend_x_router_ks_kernel(tc, xq, kT, vT, ks, vs, offs, qoffs, out):
         ksw = keep.tile([P, T], F32, name="ksw", tag="ksw")
         vsw = keep.tile([P, T], F32, name="vsw", tag="vsw")
         nc.vector.memset(ksw[0:LAST, :], 0.0)
-        nc.vector.memset(vsw[0:MID, :], 0.0)
-        nc.vector.memset(vsw[MID + 1 : P, :], 0.0)
+        nc.gpsimd.memset(vsw[0:LAST, :], 0.0)
 
         kview = kT.rearrange("(p t) w -> p t w", t=4)
         qview = xq.rearrange("(p t) w -> p t w", t=4)
@@ -168,21 +167,22 @@ def tile_attend_x_router_ks_kernel(tc, xq, kT, vT, ks, vs, offs, qoffs, out):
         nm = keep.tile([P, 4], F32, name="nm")
         total = keep.tile([P, 4], F32, name="total")
         y_sb = keep.tile([P, NQ], F32, name="y_sb")
-        rl_sb = [keep.tile([P, 256], F32, name="rl_sb%d" % h, tag="rl_sb%d" % h, align_bytes=64) for h in range(2)]
+        rl_sb = [keep.tile([P, HALF], F32, name="rl_sb%d" % h) for h in range(2)]
         rl = keep.tile([P, 4], F32, name="rl")
         a_all = keep.tile([P, 4, N], F32, name="a_all")
         half = {j: keep.tile([P, 1], F32, name="half%d" % j, tag="half%d" % j) for j in (2, 3)}
         p_of = [keep.tile([P, N], F32, name="p%d" % j, tag="p%d" % j, align_bytes=64) for j in range(4)]
         first_w = keep.tile([P, 2, N], BF16, name="first_w", tag="first_w", align_bytes=64)
         wx = {0: first_w[:, 0, :], 1: first_w[:, 1, :], 2: keep.tile([P, N], BF16, name="wx2", align_bytes=64)[:]}
-        first_c = keep.tile([P, 2, 2 * P], U32, name="first_c", align_bytes=64)
-        wc = {0: first_c[:, 0, :], 1: first_c[:, 1, :], 2: keep.tile([P, 2 * P], U32, name="wc2", align_bytes=64)[:]}
-        wsc = keep.tile([P, 4, 2 * P], U8, name="wsc", align_bytes=64)
+        first_c = placed("first_c", [P, 2, 2 * P], U32, 0)
+        wc = {0: first_c[:, 0, :], 1: first_c[:, 1, :]}
+        first_s = placed("first_s", [P, 2, 2 * P], U8, 0, 2048)
+        wsc = {0: first_s[:, 0, :], 1: first_s[:, 1, :], 2: keep.tile([P, 2 * P], U8, name="wsc2", align_bytes=64)[:]}
         wq = keep.tile([P, 2, N], BF16, name="wq")
         BY_WORDS = (0, 2)
         P_BANK = {0: 3, 1: 6, 2: 5, 3: 0}
-        Y_BANK = (6, 2)
-        L_BANK = (4, 0)
+        Y_BANK = (6, 6, 2, 3)
+        L_BANK = (4, 4)
         V_BANK = 5
 
         def dealt_views(j):
@@ -196,14 +196,17 @@ def tile_attend_x_router_ks_kernel(tc, xq, kT, vT, ks, vs, offs, qoffs, out):
             for c in range(8):
                 nc.tensor.transpose(bank(P_BANK[j], 2)[:, c * P : (c + 1) * P], p_of[j][:, c * P : (c + 1) * P], ident[:])
 
+        def scale_pass(j, g, dst):
+            nc.vector.tensor_tensor(
+                dst.rearrange("p (q t) -> p q t", t=4),
+                bank(P_BANK[j] + g).rearrange("p (t q) -> p q t", t=4),
+                vs_col[:, 4 * g : 4 * g + 4].unsqueeze(1).to_broadcast([P, P, 4]),
+                MULT,
+            )
+
         def scale(j):
             for g in range(2):
-                nc.vector.tensor_tensor(
-                    wx[j][:, g * BANK : (g + 1) * BANK].rearrange("p (q t) -> p q t", t=4),
-                    bank(P_BANK[j] + g).rearrange("p (t q) -> p q t", t=4),
-                    vs_col[:, 4 * g : 4 * g + 4].unsqueeze(1).to_broadcast([P, P, 4]),
-                    MULT,
-                )
+                scale_pass(j, g, wx[j][:, g * BANK : (g + 1) * BANK])
 
         def scale_and_turn(j, shares):
             for engine, lo, hi in shares:
@@ -249,13 +252,13 @@ def tile_attend_x_router_ks_kernel(tc, xq, kT, vT, ks, vs, offs, qoffs, out):
             nc.scalar.activation(dst, src, EXP, bias=nm[:, j : j + 1], scale=sign, accum_out=total[:, j : j + 1])
 
         def quantise_weights(j):
-            nc.vector.quantize_mx(out=wc[j].bitcast(FP8X4), scales=wsc[:, j, :], in_=wx[j])
+            nc.vector.quantize_mx(out=wc[j].bitcast(FP8X4), scales=wsc[j], in_=wx[j])
 
-        def values(h):
-            for i in ((1, 0), (0, 1))[h]:
+        def values(groups):
+            for j in groups:
                 for g in range(2):
                     cols = slice(g * P, (g + 1) * P)
-                    mx(bank(Y_BANK[h])[:, i * P : (i + 1) * P], vc[:, cols], vsc[:, cols], wc[2 * h + i][:, cols], wsc[:, 2 * h + i, cols], g == 0, g == 1)
+                    mx(bank(Y_BANK[j])[:, j % 2 * P : (j % 2 + 1) * P], vc[:, cols], vsc[:, cols], wc[j][:, cols], wsc[j][:, cols], g == 0, g == 1)
 
         def normaliser(h):
             js = slice(2 * h, 2 * h + 2)
@@ -264,10 +267,10 @@ def tile_attend_x_router_ks_kernel(tc, xq, kT, vT, ks, vs, offs, qoffs, out):
                 c = 2 * h + i
                 turn_one(bank(L_BANK[h])[:, i * P : (i + 1) * P], rl[:, c : c + 1].to_broadcast([P, P]))
 
-        def scatter(h, eng):
-            cols = slice(h * 256, (h + 1) * 256)
-            nc.vector.tensor_tensor(y_sb[:, cols], bank(Y_BANK[h])[:, 0:256], rl_sb[h][:], MULT)
-            eng(window[:].indirect(qlist[:, h * 16 : (h + 1) * 16]), y_sb[:, cols])
+        def scatter_pair():
+            nc.vector.tensor_tensor(y_sb[:, 0:HALF], bank(Y_BANK[0])[:, 0:HALF], rl_sb[0][:], MULT)
+            s_move(window[:].indirect(first), y_sb[:, 0:HALF])
+
 
         vg = {0: keep.tile([P, 512], BF16, name="vg0")}
         vx = keep.tile([P, N], BF16, name="vx", align_bytes=64)
@@ -297,7 +300,7 @@ def tile_attend_x_router_ks_kernel(tc, xq, kT, vT, ks, vs, offs, qoffs, out):
                 stabiliser(j, g)
         for j in (2, 3):
             weights(j, -1.0)
-        vg[1] = keep.tile([P, 512], BF16, name="vg1", tag="half3")
+        vg[1] = keep.tile([P, 512], BF16, name="vg1", tag="vlow")
         v_move(vg[1][:], vhigh[:].indirect(slots[:, 32:64]))
         turn(1)
         normaliser(0)
@@ -311,15 +314,24 @@ def tile_attend_x_router_ks_kernel(tc, xq, kT, vT, ks, vs, offs, qoffs, out):
         nc.vector.quantize_mx(out=vc[:].bitcast(FP8X4), scales=vsc[:], in_=vx[:])
         for j in (1, 0):
             quantise_weights(j)
-        values(0)
-        wx[3] = keep.tile([P, N], BF16, name="wx3", tag="first_w", align_bytes=64)[:]
-        scale(3)
-        scatter(0, s_move)
-        quantise_weights(2)
-        wc[3] = keep.tile([P, 2 * P], U32, name="wc3", tag="rl_sb0", align_bytes=64)[:]
-        quantise_weights(3)
-        values(1)
+        values((1, 0))
+        last_w = {0: keep.tile([P, BANK], BF16, name="last_w0", tag="first_w", align_bytes=64)[:]}
+        wc[3] = keep.tile([P, 2 * P], U32, name="wc3", align_bytes=64)[:]
         normaliser(1)
-        v_move(rl_sb[1][:], bank(L_BANK[1])[:, 0:HALF])
-        scatter(1, v_move)
+        nc.scalar.copy(rl_sb[1][:], bank(L_BANK[1])[:, 0:HALF])
+        scale_pass(3, 0, last_w[0])
+        scatter_pair()
+        wc[2] = placed("wc2", [P, 2 * P], U32, 0)[:]
+        wsc[3] = placed("wsc3", [P, 2 * P], U8, 0, 2048)[:]
+        last_w[1] = placed("last_w1", [P, BANK], BF16, 0, 1024)[:]
+        quantise_weights(2)
+        values((2,))
+        scale_pass(3, 1, last_w[1])
+        quantise(wc[3][:, 0:P], wsc[3][:, 0:P], last_w[0])
+        quantise(wc[3][:, P : 2 * P], wsc[3][:, P : 2 * P], last_w[1])
+        values((3,))
+        for j in (2, 3):
+            within = slice(j % 2 * P, (j % 2 + 1) * P)
+            nc.vector.tensor_tensor(y_sb[:, j * P : (j + 1) * P], bank(Y_BANK[j])[:, within], rl_sb[1][:, within], MULT)
+        v_move(window[:].indirect(second), y_sb[:, HALF:NQ])
         nc.sync.dma_start(out, window[:])

@@ -96,8 +96,7 @@ def tile_attend_x_router_ks_kernel(tc, xq, kT, vT, ks, vs, offs, qoffs, out):
         ks_col = keep.tile([P, 8], F32, name="ks_col")
         for g in range(2):
             for i in range(4):
-                c = 4 * g + i
-                turn_one(bank(g)[:, i * P : (i + 1) * P], ksg[:, c * P : (c + 1) * P])
+                turn_one(bank(g)[:, i * P : (i + 1) * P], ksg[:, g * 512 + i : (g + 1) * 512 : 4])
             nc.scalar.copy(ks_col[:, 4 * g : 4 * g + 4], bank(g)[:, LAST:BANK:P])
         for g in range(2):
             for t in range(4):
@@ -117,7 +116,7 @@ def tile_attend_x_router_ks_kernel(tc, xq, kT, vT, ks, vs, offs, qoffs, out):
             s_move(kg[:, t, SPLIT:N], kpl[t][:].indirect(slots[:, SPLIT // 16 : N // 16]))
 
         def weave_keys(g):
-            v_move(kx[g][:].rearrange("p (n t) -> p n t", t=4), kg[:, :, g * 512 : (g + 1) * 512].rearrange("p t n -> p n t"))
+            v_move(kx[g][:].rearrange("p (r s t) -> p r s t", r=4, t=4), kg[:, :, g * 512 : (g + 1) * 512].rearrange("p t (s r) -> p r s t", r=4))
 
         gather_keys(0)
         gather_keys(1)
@@ -139,7 +138,7 @@ def tile_attend_x_router_ks_kernel(tc, xq, kT, vT, ks, vs, offs, qoffs, out):
             quantise(kc[:, cols], ksc[:, cols], kx[g][:])
         ks_row = placed("ks_row", [P, N], F32, 3)
         for g in range(2):
-            nc.scalar.copy(ks_row[:, g * BANK : (g + 1) * BANK].rearrange("p (t s) -> p t s", t=4), bank(4 + g).rearrange("p (s t) -> p t s", t=4))
+            nc.scalar.copy(ks_row[:, g * BANK : (g + 1) * BANK], bank(4 + g))
 
         qx = keep.tile([P, 4 * NQ], BF16, name="qx", tag="qx", align_bytes=64)
         qg = keep.tile([P, 2, NQ], BF16, name="qg")
@@ -185,22 +184,15 @@ def tile_attend_x_router_ks_kernel(tc, xq, kT, vT, ks, vs, offs, qoffs, out):
         L_BANK = (4, 4)
         V_BANK = 5
 
-        def dealt_views(j):
-            return "p (t s) -> p t s", "p (s t) -> p t s", dict(t=4)
-
-        def dealt(j, g, b):
-            to, frm, sizes = dealt_views(j)
-            return a_all[:, j, g * BANK : (g + 1) * BANK].rearrange(to, **sizes), b.rearrange(frm, **sizes)
-
         def turn(j):
             for c in range(8):
                 nc.tensor.transpose(bank(P_BANK[j], 2)[:, c * P : (c + 1) * P], p_of[j][:, c * P : (c + 1) * P], ident[:])
 
         def scale_pass(j, g, dst):
             nc.vector.tensor_tensor(
-                dst.rearrange("p (q t) -> p q t", t=4),
-                bank(P_BANK[j] + g).rearrange("p (t q) -> p q t", t=4),
-                vs_col[:, 4 * g : 4 * g + 4].unsqueeze(1).to_broadcast([P, P, 4]),
+                dst.rearrange("p (c i t) -> p c t i", i=2, t=4),
+                bank(P_BANK[j] + g).rearrange("p (t c i) -> p c t i", t=4, i=2),
+                vs_col[:, 4 * g : 4 * g + 4].unsqueeze(1).unsqueeze(3).to_broadcast([P, P // 2, 4, 2]),
                 MULT,
             )
 
@@ -224,10 +216,9 @@ def tile_attend_x_router_ks_kernel(tc, xq, kT, vT, ks, vs, offs, qoffs, out):
                 mx(bank(2 * j + g), qc[:, q_cols], qsc[:, q_cols], kc[:, k_cols], ksc[:, k_cols])
 
         def scale_by_query(j):
-            to, frm, sizes = dealt_views(j)
             for g in range(2):
-                dst, src = dealt(j, g, bank(2 * j + g))
-                nc.vector.tensor_tensor(dst, src, ks_row[:, g * BANK : (g + 1) * BANK].rearrange(to, **sizes), MULT)
+                cols = slice(g * BANK, (g + 1) * BANK)
+                nc.vector.tensor_tensor(a_all[:, j, cols], bank(2 * j + g), ks_row[:, cols], MULT)
 
         def scores_by_slot(n):
             for c in (2 * n, 2 * n + 1):
@@ -240,10 +231,9 @@ def tile_attend_x_router_ks_kernel(tc, xq, kT, vT, ks, vs, offs, qoffs, out):
             b = bank(2 * g + j - 2)
             for i in range(4):
                 nc.tensor.transpose(b[:, i * P : (i + 1) * P], at[:, 4 * g + i, (j - 2) * P : (j - 1) * P], ident[:])
-            dst, src = dealt(j, g, b)
             first = None if g == 0 else half[j][:]
             least = half[j][:] if g == 0 else nm[:, j : j + 1]
-            nc.vector.tensor_scalar(dst, src, -1.0, first, MULT, MIN, accum_out=least)
+            nc.vector.tensor_scalar(a_all[:, j, g * BANK : (g + 1) * BANK], b, -1.0, first, MULT, MIN, accum_out=least)
 
         def weights(j, sign):
             dst, src = p_of[j][:], a_all[:, j, :]

from contextlib import ExitStack

import concourse.mybir as mybir
from concourse.masks import make_identity

P = 128
D, T, N, NQ, DV = 512, 2048, 1024, 512, 128
FLOPS = 2 * NQ * N * (D + DV)

F32 = mybir.dt.float32
BF16 = mybir.dt.bfloat16
U32 = mybir.dt.uint32
U16 = mybir.dt.uint16
U8 = mybir.dt.uint8
FP8X4 = mybir.dt.float8_e4m3fn_x4
COPY = mybir.ActivationFunctionType.Copy
EXP = mybir.ActivationFunctionType.Exp
MULT = mybir.AluOpType.mult
ADD = mybir.AluOpType.add
MIN = mybir.AluOpType.min
MAX = mybir.AluOpType.max
X = mybir.AxisListType.X
BANK = 512
LAST = P - 1
SPLIT = 640
HEAD = 512
SHARE = 384
MID = P - 1
HALF = NQ // 2
PLANE = 4 * T


def tile_attend_x_router_ks_kernel(tc, xq, kT, vT, ks, vs, offs, qoffs, out):
    nc = tc.nc
    with ExitStack() as ctx:
        lists = ctx.enter_context(tc.tile_pool(name="lists", bufs=1))
        keep = ctx.enter_context(tc.tile_pool(name="keep", bufs=1))
        planes = ctx.enter_context(tc.tile_pool(name="planes", bufs=1))
        banks = ctx.enter_context(tc.psum_pool(name="banks", bufs=1))
        ps = banks.tile([P, 8 * BANK], F32, name="ps")

        def bank(b, n=1):
            return ps[:, b * BANK : (b + n) * BANK]

        def placed(name, shape, dtype, place, within=0):
            return planes.tile(shape, dtype, name=name, offset=place * PLANE + within, align_bytes=64)

        def s_move(dst, src):
            nc.scalar.activation(dst, src, COPY)

        v_move = nc.vector.tensor_copy

        slots = lists.tile([P, N // 16], U16, name="slots")
        qlist = lists.tile([P, NQ // 16], U16, name="qlist")
        ident = keep.tile([P, P], F32, name="ident")
        make_identity(nc, ident[:])

        def turn_one(dst, src):
            nc.tensor.transpose(dst, src, ident[:])

        def mx(dst, lhs, lhs_scale, rhs, rhs_scale, start=True, stop=True):
            nc.tensor.matmul_mx(out=dst, lhsT=lhs.bitcast(FP8X4), lhsT_scale=lhs_scale, rhs=rhs.bitcast(FP8X4), rhs_scale=rhs_scale, start=start, stop=stop)

        def quantise(codes, scales, src):
            nc.vector.quantize_mx(out=codes.bitcast(FP8X4), scales=scales, in_=src)

        ksw = keep.tile([P, T], F32, name="ksw", tag="ksw")
        vsw = keep.tile([P, T], F32, name="vsw", tag="vsw")
        nc.vector.memset(ksw[0:LAST, :], 0.0)
        nc.gpsimd.memset(vsw[0:LAST, :], 0.0)

        kview = kT.rearrange("(p t) w -> p t w", t=4)
        qview = xq.rearrange("(p t) w -> p t w", t=4)
        kpl = [placed("kplane%d" % t, [P, T], F32, t) for t in range(4)]
        qpl = [placed("qplane%d" % t, [P, T], F32, 4 + t) for t in range(4)]
        vlow = keep.tile([P, T - 512], F32, name="vlow", tag="vlow")
        nc.sync.dma_start(kpl[0][:, 0:HEAD], kview[:, 0, 0:HEAD])
        nc.sync.dma_start(slots[:], offs)
        nc.sync.dma_start(ksw[LAST:P, :], ks[0:1, :])
        nc.sync.dma_start(vsw[MID : MID + 1, :], vs[0:1, :])
        nc.sync.dma_start(kpl[0][:, HEAD:T], kview[:, 0, HEAD:T])
        nc.sync.dma_start(kpl[1][:], kview[:, 1, :])
        nc.sync.dma_start(qlist[:], qoffs)
        for t in (2, 3):
            nc.sync.dma_start(kpl[t][:], kview[:, t, :])
        for t in range(4):
            nc.sync.dma_start(qpl[t][:], qview[:, t, :])
        nc.sync.dma_start(vlow[:], vT[:, 0 : T - 512])
        vhigh = placed("vhigh", [P, T], F32, 8)
        nc.sync.dma_start(vhigh[:], vT)

        ksg = keep.tile([P, N], F32, name="ksg")
        vsg = keep.tile([P, N], F32, name="vsg")
        v_move(ksg[:], ksw[:].indirect(slots[:]))
        s_move(vsg[:], vsw[:].indirect(slots[:]))
        ks_col = keep.tile([P, 8], F32, name="ks_col")
        for g in range(2):
            for i in range(4):
                turn_one(bank(g)[:, i * P : (i + 1) * P], ksg[:, g * 512 + i : (g + 1) * 512 : 4])
            nc.scalar.copy(ks_col[:, 4 * g : 4 * g + 4], bank(g)[:, LAST:BANK:P])
        for g in range(2):
            for t in range(4):
                turn_one(bank(2 + g)[:, t * P : (t + 1) * P], vsg[:, g * 512 + t : (g + 1) * 512 : 4])
        for g in range(2):
            for i in range(4):
                c = 4 * g + i
                turn_one(bank(4 + g)[:, i * P : (i + 1) * P], ks_col[:, c : c + 1].to_broadcast([P, P]))

        kg = keep.tile([P, 4, N], BF16, name="kg", tag="ksw")
        kc = keep.tile([P, N], U32, name="kc", align_bytes=64)
        ksc = keep.tile([P, N], U8, name="ksc", align_bytes=64)
        kx = {}

        def gather_keys(t):
            v_move(kg[:, t, 0:SPLIT], kpl[t][:].indirect(slots[:, 0 : SPLIT // 16]))
            s_move(kg[:, t, SPLIT:N], kpl[t][:].indirect(slots[:, SPLIT // 16 : N // 16]))

        def weave_keys(g):
            v_move(kx[g][:].rearrange("p (r s t) -> p r s t", r=4, t=4), kg[:, :, g * 512 : (g + 1) * 512].rearrange("p t (s r) -> p r s t", r=4))

        gather_keys(0)
        gather_keys(1)
        kx[0] = keep.tile([P, 4 * 512], BF16, name="kx0", align_bytes=64)
        gather_keys(2)
        kx[1] = placed("kx1", [P, 4 * 512], BF16, 2)
        vs_col = placed("vs_col", [P, 8], F32, 2, 4096)
        for g in range(2):
            nc.scalar.copy(vs_col[:, 4 * g : 4 * g + 4], bank(2 + g)[:, MID:BANK:P])
        for g in range(2):
            for t in range(4):
                c = 4 * g + t
                turn_one(bank(6 + g)[:, t * P : (t + 1) * P], vs_col[:, c : c + 1].to_broadcast([P, P]))
        gather_keys(3)
        for g in range(2):
            weave_keys(g)
        for g in range(2):
            cols = slice(g * 512, (g + 1) * 512)
            quantise(kc[:, cols], ksc[:, cols], kx[g][:])
        ks_row = placed("ks_row", [P, N], F32, 3)
        for g in range(2):
            nc.scalar.copy(ks_row[:, g * BANK : (g + 1) * BANK], bank(4 + g))

        qx = keep.tile([P, 4 * NQ], BF16, name="qx", tag="qx", align_bytes=64)
        qg = keep.tile([P, 2, NQ], BF16, name="qg")
        qlate = keep.tile([P, 2, HALF], BF16, name="qlate")
        qc = keep.tile([P, NQ], U32, name="qc", align_bytes=64)
        qsc = keep.tile([P, NQ], U8, name="qsc", align_bytes=64)
        qwords = qx[:].rearrange("p (n t) -> p n t", t=4)
        first, second = qlist[:, 0 : HALF // 16], qlist[:, HALF // 16 : NQ // 16]
        s_move(qg[:, 0, :], qpl[0][:].indirect(qlist[:]))
        s_move(qg[:, 1, 0:HALF], qpl[1][:].indirect(first))
        v_move(qg[:, 1, HALF:NQ], qpl[1][:].indirect(second))
        vs_row = placed("vs_row", [P, N], F32, 5)
        for g in range(2):
            nc.scalar.copy(vs_row[:, g * BANK : (g + 1) * BANK].rearrange("p (u s e) -> p u s e", u=2, e=2), bank(6 + g).rearrange("p (u e s) -> p u s e", u=2, e=2))
        v_move(qwords[:, :, 0:2], qg[:].rearrange("p t n -> p n t"))
        for t in (2, 3):
            v_move(qwords[:, 0:HALF, t], qpl[t][:].indirect(first))
            s_move(qlate[:, t - 2, :], qpl[t][:].indirect(second))
        quantise(qc[:, 0:P], qsc[:, 0:P], qx[:, 0 : 4 * P])
        v_move(qwords[:, HALF:NQ, 2:4], qlate[:].rearrange("p t n -> p n t"))
        quantise(qc[:, P:NQ], qsc[:, P:NQ], qx[:, 4 * P : 4 * NQ])
        window = keep.tile([P, T], F32, name="window", tag="qx", align_bytes=64)
        nc.gpsimd.memset(window[:], 0.0)

        nm = keep.tile([P, 4], F32, name="nm")
        total = keep.tile([P, 4], F32, name="total")
        y_sb = keep.tile([P, NQ], F32, name="y_sb")
        rl_sb = [keep.tile([P, HALF], F32, name="rl_sb%d" % h) for h in range(2)]
        rl = keep.tile([P, 4], F32, name="rl")
        a_all = keep.tile([P, 4, N], F32, name="a_all")
        half = {j: keep.tile([P, 1], F32, name="half%d" % j, tag="half%d" % j) for j in (2, 3)}
        p_of = [keep.tile([P, N], F32, name="p%d" % j, tag="p%d" % j, align_bytes=64) for j in range(4)]
        first_w = keep.tile([P, 2, N], BF16, name="first_w", tag="first_w", align_bytes=64)
        wx = {0: first_w[:, 0, :], 1: first_w[:, 1, :], 2: keep.tile([P, N], BF16, name="wx2", align_bytes=64)[:]}
        first_c = placed("first_c", [P, 2, 2 * P], U32, 0)
        wc = {0: first_c[:, 0, :], 1: first_c[:, 1, :]}
        first_s = placed("first_s", [P, 2, 2 * P], U8, 0, 2048)
        wsc = {0: first_s[:, 0, :], 1: first_s[:, 1, :], 2: keep.tile([P, 2 * P], U8, name="wsc2", align_bytes=64)[:]}
        wq = keep.tile([P, 2, N], BF16, name="wq")
        BY_WORDS = (0, 2)
        P_BANK = {0: 3, 1: 6, 2: 5, 3: 0}
        Y_BANK = (6, 6, 2, 3)
        L_BANK = (4, 4)
        V_BANK = 5

        def turn(j):
            for c in range(8):
                nc.tensor.transpose(bank(P_BANK[j], 2)[:, c * P : (c + 1) * P], p_of[j][:, c * P : (c + 1) * P], ident[:])

        def scale_pass(j, g, dst):
            nc.vector.tensor_tensor(
                dst.rearrange("p (c i t) -> p c t i", i=2, t=4),
                bank(P_BANK[j] + g).rearrange("p (t c i) -> p c t i", t=4, i=2),
                vs_col[:, 4 * g : 4 * g + 4].unsqueeze(1).unsqueeze(3).to_broadcast([P, P // 2, 4, 2]),
                MULT,
            )

        def scale(j):
            for g in range(2):
                scale_pass(j, g, wx[j][:, g * BANK : (g + 1) * BANK])

        def scale_and_turn(j, shares):
            for engine, lo, hi in shares:
                engine.tensor_tensor(wq[:, j // 2, lo:hi], p_of[j][:, lo:hi], vs_row[:, lo:hi], MULT)
            b = bank(P_BANK[j])
            words = wq[:, j // 2, :].bitcast(F32)
            for c in range(4):
                nc.tensor.transpose(b[:, c * P : (c + 1) * P], words[:, c * P : (c + 1) * P], ident[:])
            nc.scalar.copy(wx[j].bitcast(F32).rearrange("p (g q u) -> p g q u", g=2, u=2), b.rearrange("p (g u q) -> p g q u", g=2, u=2))

        def scores_by_query(j):
            q_cols = slice(j * P, (j + 1) * P)
            for g in range(2):
                k_cols = slice(g * 512, (g + 1) * 512)
                mx(bank(2 * j + g), qc[:, q_cols], qsc[:, q_cols], kc[:, k_cols], ksc[:, k_cols])

        def scale_by_query(j):
            for g in range(2):
                cols = slice(g * BANK, (g + 1) * BANK)
                nc.vector.tensor_tensor(a_all[:, j, cols], bank(2 * j + g), ks_row[:, cols], MULT)

        def scores_by_slot(n):
            for c in (2 * n, 2 * n + 1):
                k_cols = slice(c * P, (c + 1) * P)
                mx(bank(4 + n)[:, c % 2 * 256 : (c % 2 + 1) * 256], kc[:, k_cols], ksc[:, k_cols], qc[:, 256:512], qsc[:, 256:512])
            for c in (2 * n, 2 * n + 1):
                nc.scalar.activation(at[:, c, :], bank(4 + n)[:, c % 2 * 256 : (c % 2 + 1) * 256], COPY, scale=ks_col[:, c : c + 1])

        def stabiliser(j, g):
            b = bank(2 * g + j - 2)
            for i in range(4):
                nc.tensor.transpose(b[:, i * P : (i + 1) * P], at[:, 4 * g + i, (j - 2) * P : (j - 1) * P], ident[:])
            first = None if g == 0 else half[j][:]
            least = half[j][:] if g == 0 else nm[:, j : j + 1]
            nc.vector.tensor_scalar(a_all[:, j, g * BANK : (g + 1) * BANK], b, -1.0, first, MULT, MIN, accum_out=least)

        def weights(j, sign):
            dst, src = p_of[j][:], a_all[:, j, :]
            if j in BY_WORDS:
                dst, src = dst.rearrange("p (u s e) -> p u s e", u=4, e=2), src.rearrange("p (u e s) -> p u s e", u=4, e=2)
            nc.scalar.activation(dst, src, EXP, bias=nm[:, j : j + 1], scale=sign, accum_out=total[:, j : j + 1])

        def quantise_weights(j):
            nc.vector.quantize_mx(out=wc[j].bitcast(FP8X4), scales=wsc[j], in_=wx[j])

        def values(groups):
            for j in groups:
                for g in range(2):
                    cols = slice(g * P, (g + 1) * P)
                    mx(bank(Y_BANK[j])[:, j % 2 * P : (j % 2 + 1) * P], vc[:, cols], vsc[:, cols], wc[j][:, cols], wsc[j][:, cols], g == 0, g == 1)

        def normaliser(h):
            js = slice(2 * h, 2 * h + 2)
            nc.vector.reciprocal(rl[:, js], total[:, js])
            for i in range(2):
                c = 2 * h + i
                turn_one(bank(L_BANK[h])[:, i * P : (i + 1) * P], rl[:, c : c + 1].to_broadcast([P, P]))

        def scatter_pair():
            nc.vector.tensor_tensor(y_sb[:, 0:HALF], bank(Y_BANK[0])[:, 0:HALF], rl_sb[0][:], MULT)
            s_move(window[:].indirect(first), y_sb[:, 0:HALF])


        vg = {0: keep.tile([P, 512], BF16, name="vg0")}
        vx = keep.tile([P, N], BF16, name="vx", align_bytes=64)
        vsc = keep.tile([P, 2 * DV], U8, name="vsc", align_bytes=64)

        def turn_values():
            for g in range(2):
                words = vg[g][:].bitcast(F32)
                for u in range(2):
                    c = 2 * g + u
                    nc.tensor.transpose(bank(V_BANK)[:, c * P : (c + 1) * P], words[:, u:256:2], ident[:])
            nc.scalar.copy(vx[:].bitcast(F32).rearrange("p (g e u) -> p g e u", g=2, u=2), bank(V_BANK).rearrange("p (g u e) -> p g e u", g=2, u=2))

        s_move(vg[0][:], vlow[:].indirect(slots[:, 0:32]))
        at = keep.tile([P, 8, 2 * P], F32, name="at", tag="vlow")
        scores_by_query(0)
        scores_by_query(1)
        for n in range(4):
            scores_by_slot(n)
        for j in (0, 1):
            scale_by_query(j)
        for j in (0, 1):
            nc.vector.tensor_reduce(nm[:, j : j + 1], a_all[:, j, :], X, MAX, negate=True)
            weights(j, 1.0)
        for g in range(2):
            for j in (2, 3):
                stabiliser(j, g)
        for j in (2, 3):
            weights(j, -1.0)
        vg[1] = keep.tile([P, 512], BF16, name="vg1", tag="vlow")
        v_move(vg[1][:], vhigh[:].indirect(slots[:, 32:64]))
        turn(1)
        normaliser(0)
        scale(1)
        turn_values()
        scale_and_turn(0, ((nc.gpsimd, 0, N),))
        nc.scalar.copy(rl_sb[0][:], bank(L_BANK[0])[:, 0:HALF])
        turn(3)
        scale_and_turn(2, ((nc.gpsimd, 0, SHARE), (nc.vector, SHARE, N)))
        vc = keep.tile([P, 2 * DV], U32, name="vc", tag="p2", align_bytes=64)
        nc.vector.quantize_mx(out=vc[:].bitcast(FP8X4), scales=vsc[:], in_=vx[:])
        for j in (1, 0):
            quantise_weights(j)
        values((1, 0))
        last_w = {0: keep.tile([P, BANK], BF16, name="last_w0", tag="first_w", align_bytes=64)[:]}
        wc[3] = keep.tile([P, 2 * P], U32, name="wc3", align_bytes=64)[:]
        normaliser(1)
        nc.scalar.copy(rl_sb[1][:], bank(L_BANK[1])[:, 0:HALF])
        scale_pass(3, 0, last_w[0])
        scatter_pair()
        wc[2] = placed("wc2", [P, 2 * P], U32, 0)[:]
        wsc[3] = placed("wsc3", [P, 2 * P], U8, 0, 2048)[:]
        last_w[1] = placed("last_w1", [P, BANK], BF16, 0, 1024)[:]
        quantise_weights(2)
        values((2,))
        scale_pass(3, 1, last_w[1])
        quantise(wc[3][:, 0:P], wsc[3][:, 0:P], last_w[0])
        quantise(wc[3][:, P : 2 * P], wsc[3][:, P : 2 * P], last_w[1])
        values((3,))
        for j in (2, 3):
            within = slice(j % 2 * P, (j % 2 + 1) * P)
            nc.vector.tensor_tensor(y_sb[:, j * P : (j + 1) * P], bank(Y_BANK[j])[:, within], rl_sb[1][:, within], MULT)
        v_move(window[:].indirect(second), y_sb[:, HALF:NQ])
        nc.sync.dma_start(out, window[:])
